import numpy as np, ml_dtypes
CORES = [48,51,52,55]
N = 4
BF = ml_dtypes.bfloat16
H, W, V, K, F, S, R, CAP = 3904, 4096, 1024, 256, 4, 3, 3, 64
def start(q, ans):
    s = np.add.reduce(np.arange(1, 17)[:, None] * q, axis=-2) + ans
    return F * np.arange(K) + (s & (F - 1))
def parts(rng):
    return (rng.integers(0, 256, (N, 8, 16, H)), rng.integers(0, 256, (N, 8, 16, K)), rng.integers(0, H, (N, 8, 16, V)),
            np.ascontiguousarray(np.argsort(rng.random((N, 8, V)), axis=-1)), rng.integers(800, 961, (N, 8)))
def pack(x, q, p, mo, th):
    return {"x": np.ascontiguousarray(x).reshape(N, 128, H).astype(np.float32).astype(BF), "qs": np.ascontiguousarray(q).reshape(N, 128, K).astype(np.float32).astype(BF),
            "towns": np.ascontiguousarray(p).reshape(N, 128, V).astype(np.int32), "mo": np.ascontiguousarray(mo).astype(np.int32),
            "th": np.repeat(th, 16, axis=1).reshape(N, 128, 1).astype(np.int32)}
def mothers(rng, src, dst):
    m = np.zeros(V, np.int64); i = np.arange(V)
    m[src] = dst; m[np.setdiff1d(i, src)] = rng.permutation(np.setdiff1d(i, dst))
    return m
def setup_inputs(rng):
    return pack(*parts(rng))
def setup_inputs_room(rng):
    x, q, p, mo, th = parts(rng)
    x = rng.integers(0, 112, x.shape); th = rng.integers(1, 17, (N, 8))
    for a in range(N):
        for g in range(8):
            n = int(rng.choice(np.array([0, 1, CAP - 1, CAP, CAP + 1, K])))
            if a == 0: n = (CAP, CAP + 1, CAP - 1, 0, 1, K, CAP, K - 1)[g]
            hard = np.zeros(K, bool); hard[rng.permutation(K)[:n]] = True
            rec = rng.integers(0, H - K, K)
            w = np.where(hard, rng.integers(128, 256, (16, K)), x[a, g][:, rec]); w[0, hard] = 128 + 16 * a
            q[a, g] = w; u = start(w, 0)
            e = np.flatnonzero(~hard); p[a, g][rng.integers(0, 8, len(e)), u[e]] = rec[e]
            v = u
            for s in range(S): v = mo[a, g][v]
            b = np.flatnonzero(hard); b = b[rng.random(len(b)) < 0.5]; o = (a + 1) % N
            x[o, g][:, H - K + b] = w[:, b]; p[o, g][rng.integers(8, 16, len(b)), v[b]] = H - K + b
    return pack(x, q, p, mo, th)
def setup_inputs_ties(rng):
    x, q, p, mo, th = parts(rng); o = rng.permutation(8); i, e = o[:4], o[4:]
    x[:, i] = 64 * rng.integers(0, 4, (N, 4, 16, H)); q[:, i] = 64 * rng.integers(0, 4, (N, 4, 16, K))
    y = p[:, i]; y[:, :, 8:, 1::3] = y[:, :, :8, 1::3]; p[:, i] = y
    th[:, i] = rng.choice(np.array([768, 769, 832, 833, 896]), (N, 4))
    k = rng.integers(0, 3, (N, 4, 1, H)); y = np.where(k == 0, 0, np.where(k == 1, 255, x[:, e])); y[..., 0] = 255; x[:, e] = y
    k = rng.integers(0, 3, (N, 4, 1, K)); q[:, e] = np.where(k == 0, 0, np.where(k == 1, 255, q[:, e]))
    y = p[:, e]; y[..., ::5] = 0; p[:, e] = y
    th[:, e] = np.concatenate([rng.permutation(np.array([0, 1, 800, 900, 2000, 4080, 4081, 4096])) for a in range((N + 1) // 2)])[:4 * N].reshape(N, 4)
    return pack(x, q, p, mo, th)
def setup_inputs_alike(rng):
    x, q, p, mo, th = parts(rng)
    pool = rng.integers(0, H, (N, 8, 40)); pool[..., 0] = 0; pool[..., 1] = H - 1
    p = np.take_along_axis(pool, rng.integers(0, 40, (N, 8, 16 * V)), 2).reshape(N, 8, 16, V)
    q[:, :, :, 1::2] = q[:, :, :, 0::2]
    o = rng.permutation(8); i = np.arange(V)
    mo[:, o[0]] = i; mo[:, o[1]] = (i + 1) % V; mo[:, o[2]] = V - 1 - i
    return pack(x, q, p, mo, rng.integers(850, 1001, (N, 8)))
def setup_inputs_crowd(rng):
    x, q, p, mo, th = parts(rng)
    x = rng.integers(0, 96, x.shape); p = rng.integers(0, H - 2 * K, p.shape); th = rng.integers(400, 513, (N, 8))
    for a in range(0, N, 2):
        o = a + 1
        for g in range(8):
            hard = np.zeros(K, bool); hard[rng.permutation(K)[:CAP]] = True
            rec = rng.integers(0, H - 2 * K, K)
            w = x[a, g][:, rec] + rng.integers(0, 8, (16, K)); w[:, hard] = rng.integers(240, 256, (16, CAP))
            q[a, g] = w; u = start(w, 0)
            e = np.flatnonzero(~hard); p[a, g][rng.integers(0, 16, len(e)), u[e]] = rec[e]
            b = np.flatnonzero(hard); c = K * int(rng.integers(0, F))
            free = rng.permutation(np.setdiff1d(np.arange(c, c + K), u[b]))
            way = np.concatenate([u[b], free[:S * CAP]]).reshape(S + 1, CAP)
            mo[a, g] = mothers(rng, way[:-1].reshape(-1), way[1:].reshape(-1))
            x[o, g][:, H - K:H - K + CAP] = 8 * rng.integers(30, 32, (16, CAP))
            p[o, g][rng.integers(8, 16, CAP), way[S]] = H - K + np.arange(CAP)
            x[o, g][:, H - 2 * K:H - K] = rng.integers(136, 200, (16, K))
            if g % 2 == 0: rec = np.full(K, H - 2 * K)
            else:
                rec = H - 2 * K + rng.permutation(K); rec[K - 1] = rec[0]
            w = x[o, g][:, rec] + rng.integers(-8, 9, (16, K))
            q[o, g] = w; u = start(w, 0)
            free = rng.permutation(np.setdiff1d(np.arange(V), u))
            if g // 2 % 2 == 0: free = free[np.argsort(free // K != int(rng.integers(0, F)), kind="stable")]
            v = rng.permutation(free[:K]); mo[o, g] = mothers(rng, u, v)
            p[o, g][rng.integers(0, 8, K), v] = rec
    z = rng.integers(0, H, (N, 8, 1, 1))
    return pack(np.take_along_axis(x, (np.arange(H) - z) % H, 3), q, (p + z) % H, mo, th)
def setup_inputs_spread(rng):
    x, q, p, mo, th = parts(rng)
    x = np.minimum((np.exp2(8.2 * rng.random((N, 8, 1, H))) * rng.random((N, 8, 16, H))).astype(np.int64), 255)
    q = np.minimum((np.exp2(8.2 * rng.random((N, 8, 1, K))) * rng.random((N, 8, 16, K))).astype(np.int64), 255)
    return pack(x, q, p, mo, np.exp2(5 + 6 * rng.random((N, 8))).astype(np.int64))
def check_inputs(d):
    bad = []
    for k in ("x", "qs"):
        v = np.asarray(d[k]).astype(np.float64)
        if not np.all((v >= 0) & (v <= 255) & (v == np.floor(v))): bad.append("whole numbers from 0 to 255 in " + k)
    if np.min(d["towns"]) < 0 or np.max(d["towns"]) > H - 1: bad.append("range of towns")
    m = np.sort(np.asarray(d["mo"]), axis=-1)
    if not np.array_equal(m, np.broadcast_to(np.arange(V), m.shape)): bad.append("the mothers of a group are all different")
    t = np.asarray(d["th"]).reshape(-1, 16)
    if np.min(t) < 0 or np.max(t) > 4096: bad.append("range of th")
    if not np.all(t == t[:, :1]): bad.append("one threshold a group")
    return bad
def tries(rec, lists, u, q, th):
    li = np.take_along_axis(lists, u[:, None, :], 2)
    col = np.take_along_axis(rec, li.reshape(8, 1, 16 * K), 2).reshape(8, 16, 16, K)
    dist = np.add.reduce(np.abs(col - q[:, :, None, :]), axis=1)
    best = np.argmin(dist, axis=1); worst = np.argmax(dist, axis=1)
    num = np.take_along_axis(li, best[:, None, :], 1)[:, 0]
    return np.min(dist, axis=1) < th[:, None], num, worst, li
def reference(x, qs, towns, mo, th):
    X = np.zeros((N, 8, 16, W), np.int32); X[..., :H] = x.astype(np.float32).astype(np.int32).reshape(N, 8, 16, H)
    q = qs.astype(np.float32).astype(np.int32).reshape(N, 8, 16, K)
    P = towns.astype(np.int64).reshape(N, 8, 16, V); M = mo.astype(np.int64); T = th.reshape(N, 8, 16)[:, :, 0].astype(np.int64)
    ans = np.zeros((N, K), np.int64)
    for t in range(R):
        X1, P1, M1, q1, ans1 = X.copy(), P.copy(), M.copy(), q.copy(), ans.copy()
        for a in range(N):
            u = start(q[a].astype(np.int64), ans[a][None, :]); home = np.zeros((8, K), bool); num = np.zeros((8, K), np.int64); path = []
            for s in range(S):
                ok, nm, worst, li = tries(X[a], P[a], u, q[a], T[a])
                hit = ok & ~home; fail = ~ok & ~home
                num = np.where(hit, nm, num); path.append((u, fail, worst, li)); home = home | hit
                u = np.where(fail, np.take_along_axis(M[a], u, 1), u)
            slot = np.add.accumulate((~home).astype(np.int64), axis=1) - 1; place = H + CAP * t + slot
            o = (a + 1 + t) % N
            ok, nm, worst, li = tries(X[o], P[o], u, q[a], T[o])
            came = ok & ~home & (slot < CAP); got = home | came
            old = np.where(home[:, None, :], np.take_along_axis(X[a], num[:, None, :], 2), np.take_along_axis(X[o], nm[:, None, :], 2))
            num = np.where(came, place, num)
            for g in range(8):
                for u_, fail, worst, li in path[::-1]:
                    j = np.flatnonzero(fail[g] & got[g]); new = li[g][:, j]; new[worst[g, j], np.arange(len(j))] = num[g, j]
                    P1[a, g][:, u_[g, j]] = new
                u0, f0 = path[0][0][g], path[0][1][g]
                k = np.flatnonzero(f0[0::2] & f0[1::2]); v, w = u0[2 * k], u0[2 * k + 1]
                M1[a, g, v] = M[a, g, w]; M1[a, g, w] = M[a, g, v]
                j = np.flatnonzero(home[g]); r, i = np.unique(num[g, j], return_index=True); j = j[i]
                X1[a, g][:, r] = (X[a, g][:, r] + q[a, g][:, j]) >> 1
                j = np.flatnonzero(came[g]); X1[a, g][:, place[g, j]] = old[g][:, j]
            q1[a] = np.where(got[:, None, :], (q[a] + old) & 255, q[a])
            ans1[a] = np.add.reduce(got.astype(np.int64), axis=0)
        X, P, M, q, ans = X1, P1, M1, q1, ans1
    return {"yx": X.reshape(N, 128, W).astype(np.float32).astype(BF), "yp": P.reshape(N, 128, V).astype(np.float32), "ym": M.astype(np.float32)}

@@ -1,0 +1,601 @@
+from concourse.mybir import AluOpType as OP, ActivationFunctionType as AF
+
+R, N = 3, 4
+BIG = 1000000.0
+FAR = 2097152.0
+LANES = [(0, 64), (64, 112), (176, 48), (224, 32)]
+VL = 176
+SPLIT0, SPLIT, PART = 4, 11, 64
+POOL, VEC = (1, 5, 9, 13), (3, 11)
+LEAST, MOST = [0, 256, 512, 1536], [1024, 1280, 768]
+
+SCRATCH = {}
+PLACE = {}
+PS = ["K0", "K1", "SM", "WB0", "WB1", "KN", "SUB0", "SUB1"]
+
+
+def _declare():
+    f, b, i, u = "float32", "bfloat16", "int32", "uint16"
+    sb = {}
+
+    def add(d, text):
+        for w in text.split():
+            k, n = w.split(":")
+            sb[k] = (int(n), d)
+
+    add(b, "xw:4352 dd:16640 qr:4096 qf0:256 qf1:256 q2:256 mmb:16 f0h:16 f2h:16 f2b:16 te:48 junk:256 cum:24 wb16:48 got:16 gv:256 cs:16 cc:16")
+    add(b, "bo:128 bw:144 bwf:144 pb:2048 rr:128 tri:128 sw:128 swi:128 idm:128 nid:128 dlt:16 lub:16 gcs:48 ep:256 zz:256 lanep:256")
+    add(f, "pw:1288 mw:1024 th32:1 tb32:1 km:1792 bm:256 bs:256 b1:256 li32:768 lim:768 wm:768 mn:768 uu:48 fc:64 nft:32 hit:48 tu:48 us:16")
+    add(f, "be:48 hb:48 hm:16 m1:256 pm:256 kb:256 na:16 nb:16 nd:16 aa:16 ab:16 okd:16 fin:16 ud:48 fud:48 g48:48 so:48")
+    add(f, "ex:16 exd:16 xo:16 c3:16 came:16 t3:16 i3:16 oh:16 og:16 cg:16")
+    add(f, "colr:1 colp:1 colg:1 colg15:1 colr1:1 cole:1 colb:1 par:1 colsw:1 cold:1 colp16:1 mr:256 mf:256 mg:256 mask:256 bo32:128 bo256:128 idm32:128")
+    add(f, "mn0:256 mx0:256 sd0:256 one:16 lu:16 dp:48 dx:16 dn:16 bp:64")
+    add(i, "twi:1024 thi:1 u0i:16 mmi:16 ki:64 em:64 wi:48 wj:48 k3:16 e3:16 vi:256 vq:256 hv:256 ip:1 il:16 pr:1 pp:1 b4:16")
+    add(u, "us16:16 so16:48 xo16:16 i316:16 oh16:16 og16:16 li0:256 li1:256 li2:256 li3:256 uo0:16 uo1:16 uo2:16 uo3:16")
+    for t in range(R):
+        add(b, "xb%d:4096" % t)
+        add(f, "pb%d:1032" % t)
+    size = {}
+    for k, (n, d) in sb.items():
+        if n > 256 or k in ("qf0", "thi"):
+            SCRATCH[k] = ("sbuf", [128, n], d)
+            PLACE[k] = (k, 0, n)
+        else:
+            PLACE[k] = ("all_" + d, size.get(d, 0), n)
+            size[d] = size.get(d, 0) + (n + 15) // 16 * 16
+    for d in size:
+        SCRATCH["all_" + d] = ("sbuf", [128, size[d]], d)
+    for k in range(3):
+        SCRATCH["ring%d" % k] = ("sbuf", [128, (LANES[k][1] if k < 2 else 256 - VL) // 16, 16, 16], b)
+    SCRATCH["mo8"] = ("sbuf", [8, 1024], i)
+    SCRATCH["mo8f"] = ("sbuf", [8, 1024], f)
+    SCRATCH["sel8"] = ("sbuf", [8, 128], f)
+    for k in PS:
+        SCRATCH[k] = ("psum", [128, 512], f)
+        PLACE[k] = (k, 0, 512)
+
+
+_declare()
+SEMAPHORES = ["sv", "sa", "st", "sg", "dq", "dx", "dt", "dh", "dm", "oy", "op", "om"] + ["%s%d" % (k, t) for k in ("ax", "ap", "lx", "lp") for t in range(R)]
+
+
+def rank_program(g, core, T, topo):
+    rank = T.rank_of(core)
+    if rank is None:
+        return
+    ENG = {"V": g.vector, "S": g.scalar, "P": g.tensor, "G": g, "Y": g.sync}
+    SEM = {"V": "sv", "S": "sa", "P": "st", "G": "sg"}
+    count, known, hist = {}, {q: {} for q in ENG}, {}
+
+    def wait_toks(q, toks):
+        need = {}
+        for (s, v, vc) in toks:
+            if known[q].get(s, 0) < v and need.get(s, (0, None))[0] < v:
+                need[s] = (v, vc)
+        for s in list(need):
+            if any(o != s and need[o][1].get(s, 0) >= need[s][0] for o in need):
+                del need[s]
+        for s in need:
+            ENG[q].wait_ge(T.sem[s], need[s][0])
+        for (s, v, vc) in toks:
+            for k in vc:
+                if known[q].get(k, 0) < vc[k]:
+                    known[q][k] = vc[k]
+
+    def deps(q, reads, writes):
+        out = []
+        for wr, regs in ((False, reads), (True, writes)):
+            for (b, lo, hi) in regs:
+                for (l, h, w, eq, tok) in hist.get(b, []):
+                    same = eq == q
+                    if b in PS and not same:
+                        out.append(tok)
+                    elif l < hi and lo < h and (w or wr):
+                        if same and (q == "P" or not w):
+                            continue
+                        out.append(tok)
+        return out
+
+    def note(eq, reads, writes, tok):
+        for (b, lo, hi) in writes:
+            hist[b] = [e for e in hist.get(b, []) if not (lo <= e[0] and e[1] <= hi)] + [(lo, hi, True, eq, tok)]
+        for (b, lo, hi) in reads:
+            hist[b] = [e for e in hist.get(b, []) if not (not e[2] and e[3] == eq and eq in SEM and lo <= e[0] and e[1] <= hi)] + [(lo, hi, False, eq, tok)]
+
+    def finish(q, sem, n, ins, reads, writes, eq):
+        count[sem] = count.get(sem, 0) + n
+        ins.then_inc(T.sem[sem], n)
+        vc = dict(known[q])
+        vc[sem] = count[sem]
+        note(eq, reads, writes, (sem, count[sem], vc))
+
+    def op(q, reads, writes, fn):
+        wait_toks(q, deps(q, reads, writes))
+        finish(q, SEM[q], 1, fn(), reads, writes, q)
+
+    def dma(sem, out, in_, reads, writes):
+        wait_toks("Y", deps("Y", reads, writes))
+        finish("Y", sem, 16, g.sync.dma_start(out, in_), reads, writes, "dma")
+
+    def C(name, a=0, b=None, st=1):
+        buf, at, n = PLACE[name]
+        b = n if b is None else b
+        if name == "qr":
+            return (T[buf][:, a:b:st], [("qr", a, a + 1)], []) if st == 16 else (T[buf][:, a:b], [("qr", 0, 16)], [])
+        return (T[buf][:, at + a:at + b:st] if st != 1 else T[buf][:, at + a:at + b], [(name, a, b)], [])
+
+    def U(name, s, n=1):
+        return C(name, 16 * s, 16 * s + 16 * n)
+
+    def PB(r):
+        return C("pb", 128 * r, 128 * r + 128)
+
+    def IND(w, o):
+        return (w[0].indirect(o[0]), w[1], o[1])
+
+    def rg(*xs):
+        return [r for x in xs if isinstance(x, tuple) for r in x[1] + x[2]]
+
+    def ap(x):
+        return x[0] if isinstance(x, tuple) else x
+
+    def tt(out, a, b, o):
+        op("V", rg(a, b) + out[2], out[1], lambda: g.vector.tensor_tensor(out[0], a[0], b[0], o))
+
+    def ts(out, a, s1, o1, s2=None, o2=None):
+        if o2 is None:
+            op("V", rg(a, s1), out[1], lambda: g.vector.tensor_scalar(out[0], a[0], ap(s1), None, o1))
+        else:
+            op("V", rg(a, s1, s2), out[1], lambda: g.vector.tensor_scalar(out[0], a[0], ap(s1), ap(s2), o1, o2))
+
+    def cp(out, a):
+        op("V", rg(a) + out[2], out[1], lambda: g.vector.tensor_copy(out[0], a[0]))
+
+    def fill(out, k):
+        op("V", [], out[1], lambda: g.vector.memset(out[0], k))
+
+    def scan(out, d0, d1, o0, o1):
+        op("V", rg(d0, d1), out[1], lambda: g.vector.tensor_tensor_scan(out[0], d0[0], d1[0], 0.0, o0, o1))
+
+    def act(out, a, func=AF.Copy, bias=None, scale=None, acc=None):
+        kw = {}
+        if bias is not None:
+            kw["bias"] = ap(bias)
+        if scale is not None:
+            kw["scale"] = ap(scale)
+        if acc is not None:
+            kw["accum_out"] = acc[0]
+        op("S", rg(a, bias, scale), out[1] + (acc[1] if acc is not None else []), lambda: g.scalar.activation(out[0], a[0], func, **kw))
+
+    def iota(x, pattern, start, by):
+        op("G", [], x[1], lambda: g.iota(x[0], pattern, start, by, allow_small_or_imprecise_dtypes=True))
+
+    def mms(lst):
+        def go():
+            for (o, l, r, a, b) in lst:
+                ins = g.tensor.matmul(o[0], l[0], r[0], a, b)
+            return ins
+        op("P", [x for m in lst for x in m[1][1] + m[2][1]], [x for m in lst for x in m[0][1]], go)
+
+    dma("dq", T["qf0"][:], T.qs[:], [], [("qf0", 0, 256)])
+    dma("dt", T["twi"][:], T.towns[:], [], [("twi", 0, 1024)])
+    dma("dx", T["xw"][:, 0:3904], T.x[:], [], [("xw", 0, 3904)])
+    dma("dh", T["thi"][:], T.th[:], [], [("thi", 0, 1)])
+    dma("dm", T["mo8"][:], T.mo[:], [], [("mo8", 0, 1024)])
+
+    iota(C("ip"), [[0, 1]], 0, 1)
+    iota(C("il"), [[16, 16]], 0, 1)
+    iota(C("mf"), [[1, 256]], 0, 0)
+    iota(C("mr"), [[0, 16], [1, 16]], 0, 0)
+    iota(C("mg"), [[16, 16], [0, 16]], 0, 0)
+    iota(C("ep"), [[0, 16], [1, 16]], 1, 0)
+    iota(C("lanep"), [[1, 256]], 0, 0)
+    ts(C("pr"), C("ip"), 15, OP.bitwise_and)
+    cp(C("colp"), C("ip"))
+    cp(C("colr"), C("pr"))
+    tt(C("colg"), C("colp"), C("colr"), OP.subtract)
+    ts(C("colr1"), C("colr"), 1.0, OP.add)
+    ts(C("colg15"), C("colg"), 15.0, OP.add)
+    ts(C("bwf"), C("mf", 0, 144), C("colg15"), OP.is_equal, C("colr1"), OP.mult)
+    ts(C("lu"), C("il"), C("colg"), OP.subtract)
+    ts(C("b4"), C("lu"), 4.0, OP.mult)
+    ts(C("bo"), C("mg", 0, 128), C("colg"), OP.is_equal)
+    ts(C("mask"), C("mr"), C("colr"), OP.is_equal)
+    ts(C("bw"), C("mf", 0, 144), C("colg15"), OP.is_equal, 32.0, OP.mult)
+    ts(C("idm"), C("mf", 0, 128), C("colp"), OP.is_equal)
+
+    def spread(qn, where):
+        for e in range(16):
+            o = C("qr", e, 4096, 16)
+            if e in POOL:
+                if where == "G":
+                    op("G", [(qn, 0, 256)], o[1], lambda: g.affine_select(o[0], C(qn)[0], [[0, 256]], OP.is_ge, 0.0, 0, 0))
+            elif e in VEC:
+                if where == "V":
+                    cp(o, C(qn))
+            elif where == "S":
+                act(o, C(qn))
+
+    def starts(t, qn):
+        lst = [(C("SM", 0, 16), C("bwf", 15 - r, 143 - r), C(qn, r, 256, 16), r == 0, t == 0 and r == 15) for r in range(16)]
+        if t:
+            lst.append((C("SM", 0, 16), C("rr"), C("got"), False, True))
+        mms(lst)
+
+    def start_towns():
+        cp(C("u0i"), C("SM", 0, 16))
+        ts(C("mmi"), C("u0i"), 3, OP.bitwise_and)
+        tt(U("uu", 0), C("mmi"), C("b4"), OP.add)
+        cp(C("uo0"), U("uu", 0))
+
+    def entries(s, P):
+        cp(C("li%d" % s), IND(C(P, 0, 1024), C("uo%d" % s)))
+
+    starts(0, "qf0")
+    for e in range(16):
+        act(C("qr", e, 4096, 16), C("qf0"))
+    act(C("nid"), C("idm"), AF.Copy, None, -1.0)
+    cp(C("pw", 0, 1024), C("twi"))
+    start_towns()
+    entries(0, "pw")
+    fill(C("xw", 3904, 4096), 0.0)
+    fill(C("pw", 1024, 1032), 0.0)
+    cp(C("pw", 1024, 1025), C("thi"))
+
+    def constants():
+        for r in range(16):
+            if r % 2:
+                act(PB(r), C("bo"), AF.Identity, None, C("mask", r, r + 1))
+            else:
+                ts(PB(r), C("bo"), C("mask", r, r + 1), OP.mult)
+        ts(C("th32"), C("thi"), 32.0, OP.mult)
+        ts(C("mn0"), C("mr"), 0.0, OP.is_equal, 2.0 * BIG, OP.mult)
+        ts(C("mn0"), C("mn0"), -BIG, OP.add)
+        ts(C("sd0"), C("mr"), 0.0, OP.not_equal)
+        ts(C("mx0"), C("mr"), 0.0, OP.is_equal, -BIG, OP.mult)
+        ts(C("mx0"), C("mx0"), 2.0, OP.add)
+        fill(C("dd", 16384 + VL, 16640), 0.0)
+
+    def late_constants():
+        ts(C("pp"), C("ip"), 1, OP.bitwise_and)
+        cp(C("par"), C("pp"))
+        ts(C("cole"), C("colr"), -1.0, OP.mult, 31.0, OP.add)
+        ts(C("colb"), C("colr"), 64.0, OP.mult, -1984.0, OP.add)
+        ts(C("colsw"), C("par"), -2.0, OP.mult, 1.0, OP.add)
+        ts(C("cold"), C("par"), -8.0, OP.mult, 4.0, OP.add)
+        tt(C("colsw"), C("colsw"), C("colp"), OP.add)
+        ts(C("tri"), C("mr", 0, 128), C("colr"), OP.is_gt)
+        tt(C("tri"), C("tri"), C("bo"), OP.mult)
+        ts(C("sw"), C("mf", 0, 128), C("colsw"), OP.is_equal)
+        tt(C("swi"), C("sw"), C("idm"), OP.subtract)
+        ts(C("dlt"), C("mr", 0, 16), 0.0, OP.mult, C("cold"), OP.add)
+        act(C("rr"), C("mask", 0, 128))
+        ts(C("bo32"), C("mg", 0, 128), C("colg"), OP.is_equal)
+        act(C("idm32"), C("idm"))
+        act(C("lub"), C("lu"))
+        for s in range(R):
+            act(U("gcs", s), C("lu"), AF.Copy, 64.0 * s - 192.0, 0.0)
+        act(C("bo256"), C("bo32"), AF.Copy, None, 256.0)
+        fill(C("one"), 1.0)
+        fill(C("fc", 0, 16), 1.0)
+        fill(C("cum"), 0.0)
+        fill(C("zz"), 0.0)
+        for s in range(3):
+            act(U("dp", s), C("lu"), AF.Copy, 1032.0)
+        act(C("dx"), C("lu"), AF.Copy, 4096.0)
+        act(C("dn"), C("lu"), AF.Copy, 16384.0)
+        for s in range(4):
+            act(U("bp", s), C("lu"), AF.Copy, 4096.0 * s - 16385.0, 15.0)
+
+    def load_mothers():
+        cp((T["mo8f"][:, :], [("mo8f", 0, 1024)], []), (T["mo8"][:, :], [("mo8", 0, 1024)], []))
+        ts(C("colp16"), C("colp"), 16.0, OP.mult)
+        bm, am, _ = PLACE["mg"]
+        bc, ac, _ = PLACE["colp16"]
+        op("V", [("mg", 0, 128), ("colp16", 0, 1)], [("sel8", 0, 128)], lambda: g.vector.tensor_scalar(T["sel8"][:, :], T[bm][0:8, am:am + 128], T[bc][0:8, ac:ac + 1], None, OP.is_equal))
+        for h, b in ((0, "WB0"), (1, "WB1")):
+            mms([(C(b), (T["sel8"][:, :], [("sel8", 0, 128)], []), (T["mo8f"][:, 512 * h:512 * h + 512], [("mo8f", 0, 1024)], []), True, True)])
+
+    def keep_mothers():
+        for h, b in ((0, "WB0"), (1, "WB1")):
+            act(C("mw", 512 * h, 512 * h + 512), C(b))
+
+    def send(t):
+        dst, frm = T.cores[(rank - 1 - t) % N], T.cores[(rank + 1 + t) % N]
+        rid, pid, _ = topo.addr(dst)
+        for kind, src, dest, n in (("p", "pw", "pb%d" % t, 1032), ("x", "xw", "xb%d" % t, 4096)):
+            wait_toks("G", deps("G", [(src, 0, n)], []))
+            asem, lsem = "a%s%d" % (kind, t), "l%s%d" % (kind, t)
+            g.remote_dma(T[dest][:, 0:n], T[src][:, 0:n], T.sem[asem], T.sem[lsem], pid, rid, topo.mask(core, dst))
+            count[lsem] = len(topo.engines(core, dst))
+            vc = dict(known["G"])
+            vc[lsem] = count[lsem]
+            note("dma", [(src, 0, n)], [], (lsem, count[lsem], vc))
+            count[asem] = len(topo.engines(frm, core))
+            note("dma", [], [(dest, 0, n)], (asem, count[asem], {asem: count[asem]}))
+
+    def mother(s):
+        tt(C("bm"), IND(C("mw"), C("uo%d" % s)), C("mask"), OP.mult)
+        scan(C("bs"), C("sd0"), C("bm"), OP.mult, OP.add)
+        cp(C("uo%d" % (s + 1)), C("bs", 15, 256, 16))
+        if s < 2:
+            act(U("uu", s + 1), C("bs", 15, 256, 16))
+
+    def dcols(s, k):
+        a, n = LANES[k]
+        return C("dd", 4096 * s + 16 * a, 4096 * s + 16 * (a + n))
+
+    def half(k, h):
+        c = LANES[k][1] // 16
+        lo, hi = (0, (c + 1) // 2) if h == 0 else ((c + 1) // 2, c)
+        o = LANES[2][1] // 16 if k == 3 else 0
+        return (T["ring2"][:, o + lo:o + hi, :, :], [("ring2", 256 * (o + lo), 256 * (o + hi))], []), 256 * lo, 256 * hi
+
+    def vpart(s, a, n, X):
+        tt(C("dd", 4096 * s + 16 * a, 4096 * s + 16 * (a + n)), IND(C(X, 0, 4096), C("li%d" % s, a, a + n)), C("qr", 16 * a, 16 * (a + n)), OP.subtract)
+
+    def vget(s, k, X):
+        vpart(s, LANES[k][0], LANES[k][1], X)
+
+    def sget(s, k, X):
+        a, n = LANES[k]
+        act(dcols(s, k), IND(C(X, 0, 4096), C("li%d" % s, a, a + n)))
+
+    def ssub(s, k):
+        for h in range(2):
+            _, lo, hi = half(k, h)
+            a = 16 * LANES[k][0]
+            o = C("SUB%d" % h, 0, hi - lo)
+            mms([(o, C("nid"), C("qr", a + lo, a + hi), True, False), (o, C("idm"), C("dd", 4096 * s + a + lo, 4096 * s + a + hi), False, True)])
+
+    def vabs(s, k, c0=0, c1=None):
+        c1 = LANES[k][1] // 16 if c1 is None else c1
+        n, a = "ring%d" % k, 4096 * s + 16 * LANES[k][0]
+        act((T[n][:, c0:c1, :, :], [(n, 256 * c0, 256 * c1)], []), C("dd", a + 256 * c0, a + 256 * c1), AF.Abs)
+
+    def sabs(s, k):
+        for h in range(2):
+            r, lo, hi = half(k, h)
+            act(r, C("SUB%d" % h, 0, hi - lo), AF.Abs)
+
+    def dist(s, k, c0=0, c1=None):
+        c1 = LANES[k][1] // 16 if c1 is None else c1
+        a, n = LANES[k][0] + 16 * c0, 16 * (c1 - c0)
+        o = C("K%d" % (s % 2), a, a + n)
+        rn = "ring%d" % k
+        mms([(o, PB(0), C("ep", 0, n), True, False)] + [(o, C("bw", 15 - r, 143 - r), (T[rn][:, c0:c1, r, :], [(rn, 256 * c0, 256 * c1)], []), False, r == 15) for r in range(16)])
+
+    def sdist(s):
+        dist(s, 2, 0, (256 - VL) // 16)
+
+    def sA(s, X):
+        if s:
+            sget(s, 2, X)
+            ssub(s, 2)
+        vabs(s, 0)
+        dist(s, 0)
+        sget(s, 3, X)
+        sabs(s, 2)
+        ssub(s, 3)
+
+    def sB(s):
+        vabs(s, 1)
+        dist(s, 1)
+        sabs(s, 3)
+        sdist(s)
+
+    def minscan(s):
+        scan(C("km", LEAST[s], LEAST[s] + 256), C("mn0"), C("K%d" % (s % 2), 0, 256), OP.max, OP.min)
+
+    def maxscan(s):
+        scan(C("km", MOST[s], MOST[s] + 256), C("mx0"), C("K%d" % (s % 2), 0, 256), OP.add, OP.max)
+
+    def bcast(bank, at, srcs, whole):
+        return [(C(bank, at + r, at + 256, 16), PB(r), src, whole and i == 0, whole and i == len(srcs) - 1) for r in range(16) for i, src in enumerate(srcs)]
+
+    for t in range(R):
+        last = t == R - 1
+        split = 16 if last else SPLIT
+        q, qn = "qf%d" % (t % 2), "qf%d" % ((t + 1) % 2)
+        X3, P3 = "xb%d" % t, "pb%d" % t
+        if t:
+            entries(0, "pw")
+        vget(0, 0, "xw")
+        sget(0, 2, "xw")
+        ssub(0, 2)
+        if t == 0:
+            constants()
+            load_mothers()
+        vget(0, 1, "xw")
+        if t == 0:
+            send(0)
+        sA(0, "xw")
+        if t == 0:
+            keep_mothers()
+            late_constants()
+        mother(0)
+        entries(1, "pw")
+        vget(1, 0, "xw")
+        sB(0)
+        mother(1)
+        entries(2, "pw")
+        vget(1, 1, "xw")
+        act(C("b1"), IND(C("mw"), C("uo0")))
+        cp(C("mmb"), C("mmi"))
+        mother(2)
+        minscan(0)
+        maxscan(0)
+        sA(1, "xw")
+        ts(U("fc", 1), C("km", 15, 256, 16), C("th32"), OP.is_ge)
+        cp(C("f0h"), U("fc", 1))
+        act(C("li32", 0, 256), IND(C("pw", 0, 1024), C("uo0")))
+        sB(1)
+        mms([(C("SM", 16, 32), C("sw"), C("f0h"), True, True), (C("SM", 32, 48), C("swi"), C("mmb"), True, False), (C("SM", 32, 48), C("idm"), C("dlt"), False, True)])
+        vget(2, 0, "xw")
+        vget(2, 1, "xw")
+        act(C("li32", 256, 512), IND(C("pw", 0, 1024), C("uo1")))
+        minscan(1)
+        maxscan(1)
+        sA(2, "xw")
+        tt(C("ex"), U("fc", 1), C("SM", 16, 32), OP.mult)
+        tt(C("exd"), C("ex"), C("SM", 32, 48), OP.mult)
+        tt(C("xo"), C("exd"), U("uu", 0), OP.add)
+        cp(C("xo16"), C("xo"))
+        cp(IND(C("mw"), C("xo16")), C("b1"))
+        if last:
+            dma("om", T.ym[:], T["mw"][0:128:16, :], [("mw", 0, 1024)], [])
+        act(C("li32", 512, 768), IND(C("pw", 0, 1024), C("uo2")))
+        cp(U("wi", 0, 2), C("km", 1039, 1536, 16))
+        ts(U("wj", 0, 2), U("wi", 0, 2), 31, OP.bitwise_and)
+        cp(U("wb16", 0, 2), U("wj", 0, 2))
+        mms(bcast("WB0", 0, [U("wb16", 0)], True) + bcast("WB0", 256, [U("wb16", 1)], True))
+        sB(2)
+        entries(3, P3)
+        vget(3, 0, X3)
+        tt(C("ud"), C("uu"), C("dp"), OP.subtract)
+        ts(C("wm", 0, 512), C("WB0"), C("cole"), OP.is_equal)
+        act(C("WB0"), C("WB0"), AF.Square, C("colb"), 64.0)
+        tt(C("lim", 0, 512), C("li32", 0, 512), C("WB0"), OP.min)
+        act(C("tb32"), C(P3, 1024, 1025), AF.Copy, None, 32.0)
+        sget(3, 2, X3)
+        ssub(3, 2)
+        minscan(2)
+        maxscan(2)
+        ts(C("nft"), C("km", 271, 768, 16), C("th32"), OP.is_ge)
+        cp(C("ki"), C("km", 15, 1024, 16))
+        tt(U("fc", 2), U("fc", 1), U("nft", 0), OP.mult)
+        ts(C("em"), C("ki"), 31, OP.bitwise_and)
+        tt(U("fc", 3), U("fc", 2), U("nft", 1), OP.mult)
+        tt(C("hit"), U("fc", 0, 3), U("fc", 1, 3), OP.subtract)
+        scan(C("cum", 1, 17), C("one"), U("fc", 3), OP.mult, OP.add)
+        tt(C("te"), C("hit"), U("em", 0, 3), OP.mult)
+        tt(C("tu"), C("hit"), C("uu"), OP.mult)
+        tt(U("te", 0), U("te", 0), U("te", 1), OP.add)
+        tt(C("us"), U("tu", 0), U("tu", 1), OP.add)
+        tt(U("te", 0), U("te", 0), U("te", 2), OP.add)
+        tt(C("us"), C("us"), U("tu", 2), OP.add)
+        mms(bcast("SM", 256, [U("te", 0)], True))
+        cp(C("us16"), C("us"))
+        cp(C("f2h"), U("fc", 3))
+        mms([(C("SM", 48, 64), C("bo"), C("cum", 0, 16), True, False), (C("SM", 48, 64), C("tri"), C("f2h"), False, True)])
+        mms([(C("SM", 80, 96), l, x, i == 0, i == 3) for i, (l, x) in enumerate([(C("bo"), C("cum", 0, 16)), (C("tri"), C("f2h")), (C("nid"), C("lub")), (C("idm"), U("gcs", t))])])
+        sget(3, 3, X3)
+        act(C("f2b"), U("fc", 3), AF.Copy, None, FAR)
+        act(C("hm"), U("fc", 3), AF.Copy, 1.0, -1.0)
+        mms([(C("KN", 0, 256), PB(0), C("lanep"), True, False)] + bcast("KN", 0, [C("f2b")], False))
+        sabs(3, 2)
+        ssub(3, 3)
+        ts(C("m1"), C("SM", 256, 512), C("colr1"), OP.is_equal)
+        tt(C("pm"), IND(C("pw", 0, 1024), C("us16")), C("m1"), OP.mult)
+        mms([(C("KN", 0, 256), C("bo256"), C("pm"), False, True)])
+        cp(U("wb16", 2), U("em", 3))
+        vabs(3, 0)
+        dist(3, 0)
+        sabs(3, 3)
+        a3, n3 = LANES[1]
+        vpart(3, a3, PART, X3)
+        mms(bcast("WB1", 0, [U("wb16", 2)], True))
+        sdist(3)
+        vabs(3, 1, 0, PART // 16)
+        dist(3, 1, 0, PART // 16)
+        tt(C("be"), U("em", 0, 3), U("bp", 0, 3), OP.add)
+        ts(C("fin"), C("SM", 48, 64), 64.0, OP.is_lt)
+        tt(C("hb"), C("hit"), C("be"), OP.mult)
+        tt(C("fin"), C("fin"), U("fc", 3), OP.mult)
+        tt(C("fud"), U("fc", 1, 3), C("ud"), OP.mult)
+        tt(C("bm"), C("KN", 0, 256), C("mask"), OP.mult)
+        act(C("kb"), C("KN", 0, 256))
+        act(C("WB1", 256, 512), C("WB1", 0, 256), AF.Square, C("colb"), 64.0)
+        mms([(C("KN", 256, 512), C("bo32"), C("pm"), True, False)])
+        scan(C("bs"), C("sd0"), C("bm"), OP.mult, OP.add)
+        ts(C("na"), C("bs", 15, 256, 16), -1.0, OP.mult, 0.5, OP.add)
+        tt(C("nb"), C("na"), C("lu"), OP.add)
+        act(C("nd"), C("nb"), AF.Copy, 1.0 / 512, -1.0 / 256)
+        vpart(3, a3 + PART, n3 - PART, X3)
+
+        def lowest(c0, c1):
+            for c in range(c0, c1):
+                for k, o in (("na", "aa"), ("nb", "ab")):
+                    act(C("junk", 0, 16 * c + 16), C("kb", 0, 16 * c + 16), AF.Sign, C(k, c, c + 1), None, C(o, c, c + 1))
+
+        lowest(0, SPLIT0)
+        vabs(3, 1, PART // 16)
+        dist(3, 1, PART // 16)
+        ts(C("wm", 512, 768), C("WB1", 0, 256), C("cole"), OP.is_equal)
+        tt(C("lim", 512, 768), C("li32", 512, 768), C("WB1", 256, 512), OP.min)
+        mms([(C("SM", 64, 80), C("idm32"), x, i == 0, i == 3) for i, x in enumerate([U("hb", 0), U("hb", 1), U("hb", 2), C("dn")])])
+        act(C("dd", 16384, 16384 + VL), C(q, 0, VL), AF.Copy, None, -1.0)
+        act(C("q2", 0, VL), C(q, 0, VL), AF.Copy, None, 2.0)
+        act(C("q2", VL, 256), C(q, VL, 256))
+        mms([(C("WB0", 0, 256), C("idm"), C(q), True, True)])
+        tt(C("nd"), C("nd"), C("dx"), OP.subtract)
+        tt(C("nd"), C("nd"), C("hm"), OP.mult)
+        lowest(SPLIT0, split)
+        minscan(3)
+        ts(C("c3"), C("km", 1551, 1792, 16), C("tb32"), OP.is_lt)
+        cp(C("k3"), C("km", 1551, 1792, 16))
+        tt(C("came"), C("c3"), C("fin"), OP.mult)
+        ts(C("e3"), C("k3"), 31, OP.bitwise_and)
+        tt(C("got"), C("came"), C("hm"), OP.add)
+        tt(C("t3"), C("e3"), U("bp", 3), OP.add)
+        tt(C("cs"), C("came"), C("SM", 48, 64), OP.mult)
+        tt(C("i3"), C("t3"), C("came"), OP.mult)
+        act(C("cc"), C("came"), AF.Copy, None, 3904.0 + 64 * t)
+        for s in range(3):
+            act(U("g48", s), C("got"))
+        mms(bcast("KN", 256, [C("cs"), C("cc")], False) + [(C("KN", 256, 512), PB(0), C("zz"), False, True)])
+        tt(C("i3"), C("i3"), C("SM", 64, 80), OP.add)
+        cp(C("i316"), C("i3"))
+        tt(C("cg"), C("came"), C("SM", 80, 96), OP.mult)
+        tt(C("vi"), IND(C("dd"), C("i316")), C("q2"), OP.add)
+        tt(C("og"), C("cg"), C("dx"), OP.add)
+        if not last:
+            ts(C("vq"), C("vi"), 255, OP.bitwise_and)
+        cp(C("og16"), C("og"))
+        if not last:
+            cp(C(qn), C("vq"))
+            starts(t + 1, qn)
+            spread(qn, "G")
+            spread(qn, "S")
+        lowest(split, 16)
+        tt(C("gv"), C("vi"), C("WB0", 0, 256), OP.subtract)
+        ts(C("hv"), C("vi"), 1, OP.arith_shift_right)
+        cp(IND(C("xw"), C("og16")), C("gv"))
+
+        def lists():
+            tt(C("so"), C("fud"), C("g48"), OP.mult)
+            for s in (2, 1, 0):
+                tt(C("mn", 256 * s, 256 * s + 256), C("KN", 256, 512), C("wm", 256 * s, 256 * s + 256), OP.mult)
+                if s == 2:
+                    tt(C("so"), C("so"), C("dp"), OP.add)
+                if s == 1:
+                    cp(C("so16"), C("so"))
+
+        def lists_in():
+            for s in (2, 1, 0):
+                a, b = 256 * s, 256 * s + 256
+                tt(IND(C("pw"), U("so16", s)), C("lim", a, b), C("mn", a, b), OP.add)
+
+        def records():
+            tt(C("okd"), C("ab"), C("aa"), OP.is_equal)
+            tt(C("oh"), C("okd"), C("nd"), OP.mult)
+            tt(C("oh"), C("oh"), C("dx"), OP.add)
+            cp(C("oh16"), C("oh"))
+            cp(IND(C("xw"), C("oh16")), C("hv"))
+
+        lists()
+        if last:
+            records()
+            dma("oy", T.yx[:], T["xw"][:, 0:4096], [("xw", 0, 4096)], [])
+            lists_in()
+            dma("op", T.yp[:], T["pw"][:, 0:1024], [("pw", 0, 1024)], [])
+        else:
+            lists_in()
+            start_towns()
+            spread(qn, "V")
+            records()
+            send(t + 1)
+
+    for s in count:
+        if known["G"].get(s, 0) < count[s]:
+            g.wait_ge(T.sem[s], count[s])

@@ -2,16 +2,20 @@ from concourse.mybir import AluOpType as OP, ActivationFunctionType as AF
 
 R, N = 3, 4
 BIG = 1000000.0
-FAR = 2097152.0
-LANES = [(0, 64), (64, 112), (176, 48), (224, 32)]
-VL = 176
-SPLIT0, SPLIT, PART = 4, 11, 64
-POOL, VEC = (1, 5, 9, 13), (3, 11)
-LEAST, MOST = [0, 256, 512, 1536], [1024, 1280, 768]
+H, ZERO, DUMP = 3904, 4096, 4288
+NUM, PDUMP = 1040, 1424
+REPEAT = [("S", 0, 4), ("S", 4, 11), ("G", 11, 16)]
+QV = 11
+VEC = [[(0, 4), (4, 11)], [(0, 4), (4, 11)], [(0, 7), (7, 11)]]
+SCA = [[(11, 13), (13, 16)]] * 3
+LEAST, MOST = [0, 256, 1024, 1536], [512, 768, 1280]
+FLOOR, HOP, GATHER, SCATTER, PE = 64, 180, 1.5, 3.5, 0.5
+PASSES = 4
+ORDER = []
 
 SCRATCH = {}
 PLACE = {}
-PS = ["K0", "K1", "SM", "WB0", "WB1", "KN", "SUB0", "SUB1"]
+PS = ["K0", "K1", "SM", "WB", "KN", "ZA", "SUB0", "SUB1"]
 
 
 def _declare():
@@ -23,21 +27,21 @@ def _declare():
             k, n = w.split(":")
             sb[k] = (int(n), d)
 
-    add(b, "xw:4352 dd:16640 qr:4096 qf0:256 qf1:256 q2:256 mmb:16 f0h:16 f2h:16 f2b:16 te:48 junk:256 cum:24 wb16:48 got:16 gv:256 cs:16 cc:16")
-    add(b, "bo:128 bw:144 bwf:144 pb:2048 rr:128 tri:128 sw:128 swi:128 idm:128 nid:128 dlt:16 lub:16 gcs:48 ep:256 zz:256 lanep:256")
-    add(f, "pw:1288 mw:1024 th32:1 tb32:1 km:1792 bm:256 bs:256 b1:256 li32:768 lim:768 wm:768 mn:768 uu:48 fc:64 nft:32 hit:48 tu:48 us:16")
-    add(f, "be:48 hb:48 hm:16 m1:256 pm:256 kb:256 na:16 nb:16 nd:16 aa:16 ab:16 okd:16 fin:16 ud:48 fud:48 g48:48 so:48")
-    add(f, "ex:16 exd:16 xo:16 c3:16 came:16 t3:16 i3:16 oh:16 og:16 cg:16")
-    add(f, "colr:1 colp:1 colg:1 colg15:1 colr1:1 cole:1 colb:1 par:1 colsw:1 cold:1 colp16:1 mr:256 mf:256 mg:256 mask:256 bo32:128 bo256:128 idm32:128")
-    add(f, "mn0:256 mx0:256 sd0:256 one:16 lu:16 dp:48 dx:16 dn:16 bp:64")
-    add(i, "twi:1024 thi:1 u0i:16 mmi:16 ki:64 em:64 wi:48 wj:48 k3:16 e3:16 vi:256 vq:256 hv:256 ip:1 il:16 pr:1 pp:1 b4:16")
-    add(u, "us16:16 so16:48 xo16:16 i316:16 oh16:16 og16:16 li0:256 li1:256 li2:256 li3:256 uo0:16 uo1:16 uo2:16 uo3:16")
+    add(b, "xw:4544 dd:12288 dd3:1040 qf0:608 qf1:608 cf:608 yy:768 fc:64 te:64 cum:24 fl:16 wb16:48 got:16 hit:32 m1:256 cntb:256 av:256 sg:256")
+    add(b, "sq:64 nb:64 fl64:64 ftab:16 bo:128 bw:144 bwf:144 bwn:144 pb:2048 dg:2048 rr:128 tri:128 trim:128 sw:128 idm:128 nid:128 i4k:128")
+    add(b, "n128:128 zm:128 lub:16 ep:256 nib:256 nib2:256")
+    add(f, "pw:1680 mw:1024 th32:1 tb32:1 km:1600 bm:1024 bs:1024 b1:256 lim:768 rl:768 uu:48 nft:32 tu:64 us:16 ud2:16 qp:256 pack:256 pm:256")
+    add(f, "ud:48 fud:48 so:48 ex:16 xo:16 oh:16 f3:4 t3:4")
+    add(f, "colr:1 colp:1 colg:1 colg15:1 colr1:1 colb:1 par:1 colsw:1 colp16:1 coln:1 cola:1 colc:1 cold:1 mr:256 mf:144 mg:256 mask:256 bo32:128 idm32:128 swi:128")
+    add(f, "mn0:256 mx0:256 sd0:256 one:16 lu:16 dp:48 dx:16 bp:4")
+    add(i, "twi:1024 pk:768 thi:1 u0i:16 mmi:16 ki:64 em:64 k2:32 e2:32 k3:4 e3:4 hv:256 a3:64 q3:64 n3:64 vs:64 vt:64 fillk:64 ip:1 il:16 pr:1 pp:1 b4:16")
+    add(u, "us16:16 so16:48 sl16:16 xo16:16 i316:4 c16:4 ls16:4 oh16:16 an16:16 kb16:256 li0:256 li1:256 li2:256 li3:64 uo0:16 uo1:16 uo2:16 uo3:16")
     for t in range(R):
-        add(b, "xb%d:4096" % t)
+        add(b, "xb%d:%d" % (t, H + 64 * t))
         add(f, "pb%d:1032" % t)
     size = {}
     for k, (n, d) in sb.items():
-        if n > 256 or k in ("qf0", "thi"):
+        if n > 256 or k == "thi":
             SCRATCH[k] = ("sbuf", [128, n], d)
             PLACE[k] = (k, 0, n)
         else:
@@ -46,7 +50,11 @@ def _declare():
     for d in size:
         SCRATCH["all_" + d] = ("sbuf", [128, size[d]], d)
     for k in range(3):
-        SCRATCH["ring%d" % k] = ("sbuf", [128, (LANES[k][1] if k < 2 else 256 - VL) // 16, 16, 16], b)
+        SCRATCH["ring%d" % k] = ("sbuf", [128, 16, 16, 16], b)
+    SCRATCH["ring3"] = ("sbuf", [128, 4, 16, 16], b)
+    SCRATCH["qr"] = ("sbuf", [128, 256 * QV], b)
+    SCRATCH["qr3"] = ("sbuf", [128, 256 - 16 * QV, 16], b)
+    SCRATCH["eq"] = ("sbuf", [128, 16, 256], b)
     SCRATCH["mo8"] = ("sbuf", [8, 1024], i)
     SCRATCH["mo8f"] = ("sbuf", [8, 1024], f)
     SCRATCH["sel8"] = ("sbuf", [8, 128], f)
@@ -109,29 +117,94 @@ def rank_program(g, core, T, topo):
         vc[sem] = count[sem]
         note(eq, reads, writes, (sem, count[sem], vc))
 
-    def op(q, reads, writes, fn):
-        wait_toks(q, deps(q, reads, writes))
-        finish(q, SEM[q], 1, fn(), reads, writes, q)
+    calls = []
 
-    def dma(sem, out, in_, reads, writes):
-        wait_toks("Y", deps("Y", reads, writes))
-        finish("Y", sem, 16, g.sync.dma_start(out, in_), reads, writes, "dma")
+    def op(q, reads, writes, n, fn):
+        def go():
+            wait_toks(q, deps(q, reads, writes))
+            finish(q, SEM[q], 1, fn(), reads, writes, q)
+        calls.append((q, reads, writes, max(n, FLOOR), max(n, FLOOR), go))
+
+    def dma(sem, out, in_, reads, writes, n):
+        def go():
+            wait_toks("Y", deps("Y", reads, writes))
+            finish("Y", sem, 16, g.sync.dma_start(out, in_), reads, writes, "dma")
+        calls.append(("Y", reads, writes, FLOOR, n, go))
+
+    def plan():
+        before, seen = [], {}
+        for i, (q, reads, writes, _, _, _) in enumerate(calls):
+            pre = {i - 1: FLOOR} if i and q == calls[i - 1][0] == "Y" else {}
+            for wr, regs in ((False, reads), (True, writes)):
+                for (b, lo, hi) in regs:
+                    for (l, h, w, j) in seen.get(b, []):
+                        p = calls[j][0]
+                        if (b in PS and p == q == "P") or (l < hi and lo < h and (w or wr)):
+                            pre[j] = max(pre.get(j, 0), calls[j][4] + (0 if p == q and (q == "P" or not w) else HOP))
+            for wr, regs in ((False, reads), (True, writes)):
+                for (b, lo, hi) in regs:
+                    seen[b] = [e for e in seen.get(b, []) if not (wr and lo <= e[0] and e[1] <= hi)] + [(lo, hi, wr, i)]
+            pre.pop(i, None)
+            before.append(pre)
+        after = [{} for _ in calls]
+        for i, pre in enumerate(before):
+            for j in pre:
+                after[j][i] = pre[j] + calls[i][3] - calls[j][3]
+        banks = [{b for (b, _, _) in c[1] + c[2] if b in PS} for c in calls]
+
+        def place(order, lags, first):
+            at, busy = {}, {}
+            for i in order:
+                q, n = calls[i][0], calls[i][3]
+                s = max([first[i]] + [at[j] + d for j, d in lags[i].items()])
+                taken = sorted([e for e in busy.get(q, []) if e[1] > s] + [(a - HOP, b + HOP) for k in banks[i] for (a, b, p) in busy.get(k, []) if p != q and b + HOP > s])
+                for (a, b) in taken:
+                    if a >= s + n:
+                        break
+                    s = max(s, b)
+                at[i] = s
+                busy.setdefault(q, []).append((s, s + n))
+                for k in banks[i]:
+                    busy.setdefault(k, []).append((s, s + n, q))
+            return at
+
+        every, best = list(range(len(calls))), None
+        order = every
+        for _ in range(PASSES):
+            at = place(order, before, [0] * len(calls))
+            end = max(at[i] + calls[i][4] for i in every)
+            if best is None or end < best[0]:
+                best = (end, sorted(every, key=lambda i: (at[i], i)))
+            back = place(sorted(every, key=lambda i: (-at[i] - calls[i][3], -i)), after, [c[4] - c[3] for c in calls])
+            order = sorted(every, key=lambda i: (-back[i] - calls[i][3], i))
+        return best[1]
 
     def C(name, a=0, b=None, st=1):
         buf, at, n = PLACE[name]
         b = n if b is None else b
-        if name == "qr":
-            return (T[buf][:, a:b:st], [("qr", a, a + 1)], []) if st == 16 else (T[buf][:, a:b], [("qr", 0, 16)], [])
         return (T[buf][:, at + a:at + b:st] if st != 1 else T[buf][:, at + a:at + b], [(name, a, b)], [])
 
     def U(name, s, n=1):
         return C(name, 16 * s, 16 * s + 16 * n)
 
-    def PB(r):
-        return C("pb", 128 * r, 128 * r + 128)
+    def B(name, s, n=1):
+        return C(name, 256 * s, 256 * s + 256 * n)
+
+    def M(name, r):
+        return C(name, 128 * r, 128 * r + 128)
+
+    def W(name, r):
+        return C(name, 15 - r, 143 - r)
 
     def IND(w, o):
         return (w[0].indirect(o[0]), w[1], o[1])
+
+    def QR(c0, c1, e0=0, e1=16):
+        if c0 >= QV:
+            x = T["qr3"][:, 16 * (c0 - QV):16 * (c1 - QV), e0:e1]
+        else:
+            x = T["qr"][:, 256 * c0:256 * c1] if e1 - e0 == 16 else T["qr"][:, 256 * c0 + e0:256 * c1:16]
+        return (x, [("qr%d" % k, e0, e1) for k, (_, a, b) in enumerate(REPEAT) if a < c1 and c0 < b], [])
 
     def rg(*xs):
         return [r for x in xs if isinstance(x, tuple) for r in x[1] + x[2]]
@@ -139,171 +212,179 @@ def rank_program(g, core, T, topo):
     def ap(x):
         return x[0] if isinstance(x, tuple) else x
 
+    def cols(x):
+        n = 1
+        for k in x[0].shape[1:]:
+            n *= k
+        return n
+
+    def short(x):
+        buf = PLACE.get(x[1][0][0], (None,))[0]
+        return buf is None or SCRATCH[buf][2] in ("bfloat16", "uint16")
+
+    def work(out, *ins):
+        if out[2]:
+            return 60 + cols(ins[-1]) * SCATTER
+        if ins[0][2]:
+            return 60 + cols(out) * GATHER
+        if short(out) and all(short(x) for x in ins):
+            return cols(out) * len(ins) / 2
+        return cols(out) * (1 if any(x[1][0][0] in PS for x in ins) else len(ins))
+
     def tt(out, a, b, o):
-        op("V", rg(a, b) + out[2], out[1], lambda: g.vector.tensor_tensor(out[0], a[0], b[0], o))
+        op("V", rg(a, b) + out[2], out[1], work(out, a, b), lambda: g.vector.tensor_tensor(out[0], a[0], b[0], o))
 
     def ts(out, a, s1, o1, s2=None, o2=None):
         if o2 is None:
-            op("V", rg(a, s1), out[1], lambda: g.vector.tensor_scalar(out[0], a[0], ap(s1), None, o1))
+            op("V", rg(a, s1), out[1], work(out, a), lambda: g.vector.tensor_scalar(out[0], a[0], ap(s1), None, o1))
         else:
-            op("V", rg(a, s1, s2), out[1], lambda: g.vector.tensor_scalar(out[0], a[0], ap(s1), ap(s2), o1, o2))
+            op("V", rg(a, s1, s2), out[1], work(out, a), lambda: g.vector.tensor_scalar(out[0], a[0], ap(s1), ap(s2), o1, o2))
 
     def cp(out, a):
-        op("V", rg(a) + out[2], out[1], lambda: g.vector.tensor_copy(out[0], a[0]))
+        op("V", rg(a) + out[2], out[1], work(out, a), lambda: g.vector.tensor_copy(out[0], a[0]))
 
     def fill(out, k):
-        op("V", [], out[1], lambda: g.vector.memset(out[0], k))
+        op("V", [], out[1], work(out, out), lambda: g.vector.memset(out[0], k))
 
     def scan(out, d0, d1, o0, o1):
-        op("V", rg(d0, d1), out[1], lambda: g.vector.tensor_tensor_scan(out[0], d0[0], d1[0], 0.0, o0, o1))
+        op("V", rg(d0, d1), out[1], cols(out), lambda: g.vector.tensor_tensor_scan(out[0], d0[0], d1[0], 0.0, o0, o1))
 
-    def act(out, a, func=AF.Copy, bias=None, scale=None, acc=None):
+    def act(out, a, func=AF.Copy, bias=None, scale=None):
         kw = {}
         if bias is not None:
             kw["bias"] = ap(bias)
         if scale is not None:
             kw["scale"] = ap(scale)
-        if acc is not None:
-            kw["accum_out"] = acc[0]
-        op("S", rg(a, bias, scale), out[1] + (acc[1] if acc is not None else []), lambda: g.scalar.activation(out[0], a[0], func, **kw))
+        op("S", rg(a, bias, scale), out[1], 80 + GATHER * cols(out) if a[2] else cols(out), lambda: g.scalar.activation(out[0], a[0], func, **kw))
 
     def iota(x, pattern, start, by):
-        op("G", [], x[1], lambda: g.iota(x[0], pattern, start, by, allow_small_or_imprecise_dtypes=True))
+        op("G", [], x[1], 150 + 2 * cols(x), lambda: g.iota(x[0], pattern, start, by, allow_small_or_imprecise_dtypes=True))
+
+    def gcopy(out, a):
+        op("G", rg(a), out[1], 200 + 2 * cols(out), lambda: g.affine_select(out[0], a[0], [[0, cols(out)]], OP.is_ge, 0.0, 0, 0))
 
     def mms(lst):
         def go():
             for (o, l, r, a, b) in lst:
                 ins = g.tensor.matmul(o[0], l[0], r[0], a, b)
             return ins
-        op("P", [x for m in lst for x in m[1][1] + m[2][1]], [x for m in lst for x in m[0][1]], go)
+        n = sum(max(64, cols(r)) * (PE if short(r) else 4 * PE) for (_, _, r, _, _) in lst)
+        op("P", [x for m in lst for x in m[1][1] + m[2][1]], [x for m in lst for x in m[0][1]], n, go)
 
-    dma("dq", T["qf0"][:], T.qs[:], [], [("qf0", 0, 256)])
-    dma("dt", T["twi"][:], T.towns[:], [], [("twi", 0, 1024)])
-    dma("dx", T["xw"][:, 0:3904], T.x[:], [], [("xw", 0, 3904)])
-    dma("dh", T["thi"][:], T.th[:], [], [("thi", 0, 1)])
-    dma("dm", T["mo8"][:], T.mo[:], [], [("mo8", 0, 1024)])
+    def total(out, terms, first=True, last=True):
+        mms([(out, l, r, first and i == 0, last and i == len(terms) - 1) for i, (l, r) in enumerate(terms)])
+
+    dma("dq", T["qf0"][:, 0:256], T.qs[:], [], [("qf0", 0, 256)], 2500)
+    dma("dt", T["twi"][:], T.towns[:], [], [("twi", 0, 1024)], 5500)
+    dma("dh", T["thi"][:], T.th[:], [], [("thi", 0, 1)], 5500)
+    dma("dm", T["mo8"][:], T.mo[:], [], [("mo8", 0, 1024)], 5600)
+    dma("dx", T["xw"][:, 0:H], T.x[:], [], [("xw", 0, H)], 11000)
 
     iota(C("ip"), [[0, 1]], 0, 1)
+    iota(C("mf"), [[1, 144]], 0, 0)
     iota(C("il"), [[16, 16]], 0, 1)
-    iota(C("mf"), [[1, 256]], 0, 0)
     iota(C("mr"), [[0, 16], [1, 16]], 0, 0)
     iota(C("mg"), [[16, 16], [0, 16]], 0, 0)
-    iota(C("ep"), [[0, 16], [1, 16]], 1, 0)
-    iota(C("lanep"), [[1, 256]], 0, 0)
+    iota(C("pw", NUM, PDUMP), [[1, PDUMP - NUM]], H, 0)
+    for name, a, b, k in (("xw", H, DUMP, 0.0), ("pw", 1024, NUM, 0.0), ("dd3", 1024, 1040, 0.0), ("ftab", 0, 16, 0.0), ("ftab", 1, 2, 1.0 / 512), ("zm", 0, 128, 0.0),
+                          ("one", 0, 16, 1.0), ("fc", 0, 16, 1.0), ("cum", 0, 24, 0.0)):
+        fill(C(name, a, b), k)
     ts(C("pr"), C("ip"), 15, OP.bitwise_and)
+    ts(C("pp"), C("ip"), 1, OP.bitwise_and)
     cp(C("colp"), C("ip"))
     cp(C("colr"), C("pr"))
+    cp(C("par"), C("pp"))
     tt(C("colg"), C("colp"), C("colr"), OP.subtract)
     ts(C("colr1"), C("colr"), 1.0, OP.add)
     ts(C("colg15"), C("colg"), 15.0, OP.add)
-    ts(C("bwf"), C("mf", 0, 144), C("colg15"), OP.is_equal, C("colr1"), OP.mult)
-    ts(C("lu"), C("il"), C("colg"), OP.subtract)
-    ts(C("b4"), C("lu"), 4.0, OP.mult)
-    ts(C("bo"), C("mg", 0, 128), C("colg"), OP.is_equal)
-    ts(C("mask"), C("mr"), C("colr"), OP.is_equal)
-    ts(C("bw"), C("mf", 0, 144), C("colg15"), OP.is_equal, 32.0, OP.mult)
+    ts(C("bwf"), C("mf"), C("colg15"), OP.is_equal, C("colr1"), OP.mult)
     ts(C("idm"), C("mf", 0, 128), C("colp"), OP.is_equal)
+    ts(C("lu"), C("il"), C("colg"), OP.subtract)
+    ts(C("bw"), C("mf"), C("colg15"), OP.is_equal, 32.0, OP.mult)
+    ts(C("b4"), C("lu"), 4.0, OP.mult)
 
-    def spread(qn, where):
-        for e in range(16):
-            o = C("qr", e, 4096, 16)
-            if e in POOL:
-                if where == "G":
-                    op("G", [(qn, 0, 256)], o[1], lambda: g.affine_select(o[0], C(qn)[0], [[0, 256]], OP.is_ge, 0.0, 0, 0))
-            elif e in VEC:
-                if where == "V":
-                    cp(o, C(qn))
-            elif where == "S":
-                act(o, C(qn))
+    def repeat(qn, who, c0, c1):
+        copies = [(QR(c0, c1, e, e + 1), C(qn, 16 * c0, 16 * c1)) for e in range(16 if c0 < QV else 2)]
+        for (o, a) in copies + [(QR(c0, c1, e, 2 * e), QR(c0, c1, 0, e)) for e in (2, 4, 8) if c0 >= QV]:
+            {"G": gcopy, "V": cp, "S": act}[who](o, a)
 
-    def starts(t, qn):
-        lst = [(C("SM", 0, 16), C("bwf", 15 - r, 143 - r), C(qn, r, 256, 16), r == 0, t == 0 and r == 15) for r in range(16)]
-        if t:
-            lst.append((C("SM", 0, 16), C("rr"), C("got"), False, True))
-        mms(lst)
-
-    def start_towns():
-        cp(C("u0i"), C("SM", 0, 16))
+    def starts(qn, more):
+        total(C("K1", 256, 272), [(W("bwf", r), C(qn, r, 256, 16)) for r in range(16)], True, not more)
+        if more:
+            total(C("K1", 256, 272), more, False, True)
+        cp(C("u0i"), C("K1", 256, 272))
         ts(C("mmi"), C("u0i"), 3, OP.bitwise_and)
         tt(U("uu", 0), C("mmi"), C("b4"), OP.add)
         cp(C("uo0"), U("uu", 0))
 
-    def entries(s, P):
-        cp(C("li%d" % s), IND(C(P, 0, 1024), C("uo%d" % s)))
+    def entries(s):
+        cp(C("li%d" % s), IND(C("pw", 0, 1024), C("uo%d" % s)))
 
-    starts(0, "qf0")
-    for e in range(16):
-        act(C("qr", e, 4096, 16), C("qf0"))
+    starts("qf0", [])
+    for (_, c0, c1) in REPEAT:
+        repeat("qf0", "S", c0, c1)
     act(C("nid"), C("idm"), AF.Copy, None, -1.0)
+    ts(C("ep"), C("mr"), 1.0, OP.add)
+    ts(C("mask"), C("mr"), C("colr"), OP.is_equal)
+    ts(C("bo"), C("mg", 0, 128), C("colg"), OP.is_equal)
+    ts(C("colp16"), C("colp"), 16.0, OP.mult)
     cp(C("pw", 0, 1024), C("twi"))
-    start_towns()
-    entries(0, "pw")
-    fill(C("xw", 3904, 4096), 0.0)
-    fill(C("pw", 1024, 1032), 0.0)
     cp(C("pw", 1024, 1025), C("thi"))
+    ts(C("th32"), C("thi"), 32.0, OP.mult)
+    entries(0)
 
-    def constants():
-        for r in range(16):
-            if r % 2:
-                act(PB(r), C("bo"), AF.Identity, None, C("mask", r, r + 1))
-            else:
-                ts(PB(r), C("bo"), C("mask", r, r + 1), OP.mult)
-        ts(C("th32"), C("thi"), 32.0, OP.mult)
-        ts(C("mn0"), C("mr"), 0.0, OP.is_equal, 2.0 * BIG, OP.mult)
-        ts(C("mn0"), C("mn0"), -BIG, OP.add)
-        ts(C("sd0"), C("mr"), 0.0, OP.not_equal)
-        ts(C("mx0"), C("mr"), 0.0, OP.is_equal, -BIG, OP.mult)
-        ts(C("mx0"), C("mx0"), 2.0, OP.add)
-        fill(C("dd", 16384 + VL, 16640), 0.0)
+    op("V", [("mo8", 0, 1024)], [("mo8f", 0, 1024)], 1024, lambda: g.vector.tensor_copy(T["mo8f"][:, :], T["mo8"][:, :]))
+    bm, am, _ = PLACE["mg"]
+    bc, ac, _ = PLACE["colp16"]
+    op("V", [("mg", 0, 128), ("colp16", 0, 1)], [("sel8", 0, 128)], 128, lambda: g.vector.tensor_scalar(T["sel8"][:, :], T[bm][0:8, am:am + 128], T[bc][0:8, ac:ac + 1], None, OP.is_equal))
+    for h, b in ((0, "WB"), (1, "KN")):
+        op("P", [("sel8", 0, 128), ("mo8f", 0, 1024)], [(b, 0, 512)], 2048 * PE, lambda h=h, b=b: g.tensor.matmul(T[b][:, :], T["sel8"][:, :], T["mo8f"][:, 512 * h:512 * h + 512], True, True))
+        act(C("mw", 512 * h, 512 * h + 512), C(b))
 
-    def late_constants():
-        ts(C("pp"), C("ip"), 1, OP.bitwise_and)
-        cp(C("par"), C("pp"))
-        ts(C("cole"), C("colr"), -1.0, OP.mult, 31.0, OP.add)
-        ts(C("colb"), C("colr"), 64.0, OP.mult, -1984.0, OP.add)
-        ts(C("colsw"), C("par"), -2.0, OP.mult, 1.0, OP.add)
-        ts(C("cold"), C("par"), -8.0, OP.mult, 4.0, OP.add)
-        tt(C("colsw"), C("colsw"), C("colp"), OP.add)
-        ts(C("tri"), C("mr", 0, 128), C("colr"), OP.is_gt)
-        tt(C("tri"), C("tri"), C("bo"), OP.mult)
-        ts(C("sw"), C("mf", 0, 128), C("colsw"), OP.is_equal)
-        tt(C("swi"), C("sw"), C("idm"), OP.subtract)
-        ts(C("dlt"), C("mr", 0, 16), 0.0, OP.mult, C("cold"), OP.add)
-        act(C("rr"), C("mask", 0, 128))
-        ts(C("bo32"), C("mg", 0, 128), C("colg"), OP.is_equal)
-        act(C("idm32"), C("idm"))
-        act(C("lub"), C("lu"))
-        for s in range(R):
-            act(U("gcs", s), C("lu"), AF.Copy, 64.0 * s - 192.0, 0.0)
-        act(C("bo256"), C("bo32"), AF.Copy, None, 256.0)
-        fill(C("one"), 1.0)
-        fill(C("fc", 0, 16), 1.0)
-        fill(C("cum"), 0.0)
-        fill(C("zz"), 0.0)
-        for s in range(3):
-            act(U("dp", s), C("lu"), AF.Copy, 1032.0)
-        act(C("dx"), C("lu"), AF.Copy, 4096.0)
-        act(C("dn"), C("lu"), AF.Copy, 16384.0)
-        for s in range(4):
-            act(U("bp", s), C("lu"), AF.Copy, 4096.0 * s - 16385.0, 15.0)
+    ts(C("mn0"), C("mr"), 0.0, OP.is_equal, 2.0 * BIG, OP.mult)
+    ts(C("sd0"), C("mr"), 0.0, OP.not_equal)
+    ts(C("mx0"), C("mr"), 0.0, OP.is_equal, -BIG, OP.mult)
+    act(C("mn0"), C("mn0"), AF.Copy, -BIG)
+    act(C("mx0"), C("mx0"), AF.Copy, 2.0)
+    ts(C("colb"), C("colr"), 64.0, OP.mult, -1984.0, OP.add)
+    ts(C("colsw"), C("par"), -2.0, OP.mult, 1.0, OP.add)
+    ts(C("cola"), C("colr"), 0.0, OP.is_equal, 1048576.0, OP.mult)
+    ts(C("colc"), C("colr"), 1.0, OP.is_equal, 65536.0, OP.mult)
+    ts(C("coln"), C("colr"), 2.0, OP.is_lt)
+    ts(C("cold"), C("colr"), 15.0, OP.mult, 1.0, OP.add)
+    tt(C("colsw"), C("colsw"), C("colp"), OP.add)
+    tt(C("coln"), C("coln"), C("cold"), OP.mult)
+    ts(C("tri"), C("mr", 0, 128), C("colr"), OP.is_gt)
+    ts(C("nib"), C("mr"), C("cola"), OP.mult)
+    ts(C("nib2"), C("mg"), C("colc"), OP.mult)
+    tt(C("tri"), C("tri"), C("bo"), OP.mult)
+    ts(C("sw"), C("mf", 0, 128), C("colsw"), OP.is_equal)
+    tt(C("nib"), C("nib"), C("nib2"), OP.add)
+    act(C("i4k"), C("idm"), AF.Copy, None, 4096.0)
+    act(C("n128"), C("idm"), AF.Copy, None, -128.0)
+    act(C("trim"), C("idm"), AF.Copy, None, -256.0)
+    tt(C("swi"), C("sw"), C("idm"), OP.subtract)
+    ts(C("fillk"), C("nib", 0, 64), 33554432.0, OP.add)
+    ts(C("bwn"), C("mf"), C("colg15"), OP.is_equal, C("coln"), OP.mult)
+    tt(C("trim"), C("trim"), C("tri"), OP.add)
+    act(C("rr"), C("mask", 0, 128))
+    act(C("bo32"), C("bo"))
+    act(C("idm32"), C("idm"))
+    act(C("lub"), C("lu"))
+    for s in range(3):
+        act(U("dp", s), C("lu"), AF.Copy, float(PDUMP))
+    act(C("dx"), C("lu"), AF.Copy, float(DUMP))
+    act(C("bp"), C("lu", 0, 4), AF.Copy, -1.0, 16.0)
+    for r in range(16):
+        ts(M("pb", r), C("bo"), C("mask", r, r + 1), OP.mult)
+        act(M("dg", r), C("idm"), AF.Identity, None, C("mask", r, r + 1))
 
-    def load_mothers():
-        cp((T["mo8f"][:, :], [("mo8f", 0, 1024)], []), (T["mo8"][:, :], [("mo8", 0, 1024)], []))
-        ts(C("colp16"), C("colp"), 16.0, OP.mult)
-        bm, am, _ = PLACE["mg"]
-        bc, ac, _ = PLACE["colp16"]
-        op("V", [("mg", 0, 128), ("colp16", 0, 1)], [("sel8", 0, 128)], lambda: g.vector.tensor_scalar(T["sel8"][:, :], T[bm][0:8, am:am + 128], T[bc][0:8, ac:ac + 1], None, OP.is_equal))
-        for h, b in ((0, "WB0"), (1, "WB1")):
-            mms([(C(b), (T["sel8"][:, :], [("sel8", 0, 128)], []), (T["mo8f"][:, 512 * h:512 * h + 512], [("mo8f", 0, 1024)], []), True, True)])
-
-    def keep_mothers():
-        for h, b in ((0, "WB0"), (1, "WB1")):
-            act(C("mw", 512 * h, 512 * h + 512), C(b))
-
-    def send(t):
+    def send(t, kind):
         dst, frm = T.cores[(rank - 1 - t) % N], T.cores[(rank + 1 + t) % N]
         rid, pid, _ = topo.addr(dst)
-        for kind, src, dest, n in (("p", "pw", "pb%d" % t, 1032), ("x", "xw", "xb%d" % t, 4096)):
+        src, dest, n = ("pw", "pb%d" % t, 1032) if kind == "p" else ("xw", "xb%d" % t, H + 64 * t)
+
+        def go():
             wait_toks("G", deps("G", [(src, 0, n)], []))
             asem, lsem = "a%s%d" % (kind, t), "l%s%d" % (kind, t)
             g.remote_dma(T[dest][:, 0:n], T[src][:, 0:n], T.sem[asem], T.sem[lsem], pid, rid, topo.mask(core, dst))
@@ -313,289 +394,239 @@ def rank_program(g, core, T, topo):
             note("dma", [(src, 0, n)], [], (lsem, count[lsem], vc))
             count[asem] = len(topo.engines(frm, core))
             note("dma", [], [(dest, 0, n)], (asem, count[asem], {asem: count[asem]}))
+        calls.append(("G", [(src, 0, n)], [(dest, 0, n)], 1100, 16000 if kind == "x" else 8000, go))
+
+    def own(k, src):
+        tt(B("bm", k), src, C("mask"), OP.mult)
+        scan(B("bs", k), C("sd0"), B("bm", k), OP.mult, OP.add)
+        return C("bs", 256 * k + 15, 256 * k + 256, 16)
 
     def mother(s):
-        tt(C("bm"), IND(C("mw"), C("uo%d" % s)), C("mask"), OP.mult)
-        scan(C("bs"), C("sd0"), C("bm"), OP.mult, OP.add)
-        cp(C("uo%d" % (s + 1)), C("bs", 15, 256, 16))
+        u = own(s, IND(C("mw"), C("uo%d" % s)))
+        cp(C("uo%d" % (s + 1)), u)
         if s < 2:
-            act(U("uu", s + 1), C("bs", 15, 256, 16))
+            act(U("uu", s + 1), u)
 
-    def dcols(s, k):
-        a, n = LANES[k]
-        return C("dd", 4096 * s + 16 * a, 4096 * s + 16 * (a + n))
+    def dcols(s, c0, c1):
+        return C("dd", 4096 * s + 256 * c0, 4096 * s + 256 * c1)
 
-    def half(k, h):
-        c = LANES[k][1] // 16
-        lo, hi = (0, (c + 1) // 2) if h == 0 else ((c + 1) // 2, c)
-        o = LANES[2][1] // 16 if k == 3 else 0
-        return (T["ring2"][:, o + lo:o + hi, :, :], [("ring2", 256 * (o + lo), 256 * (o + hi))], []), 256 * lo, 256 * hi
+    def ring(s, c0, c1, r=None):
+        n = "ring%d" % s
+        return (T[n][:, c0:c1, :, :] if r is None else T[n][:, c0:c1, r, :], [(n, c0, c1)], [])
 
-    def vpart(s, a, n, X):
-        tt(C("dd", 4096 * s + 16 * a, 4096 * s + 16 * (a + n)), IND(C(X, 0, 4096), C("li%d" % s, a, a + n)), C("qr", 16 * a, 16 * (a + n)), OP.subtract)
+    def dist(s, c0, c1):
+        total(C("K%d" % (s % 2), 16 * c0, 16 * c1), [(C("idm"), C("ep", 0, 16 * (c1 - c0)))] + [(W("bw", r), ring(s, c0, c1, r)) for r in range(16)])
 
-    def vget(s, k, X):
-        vpart(s, LANES[k][0], LANES[k][1], X)
+    turn = [0]
 
-    def sget(s, k, X):
-        a, n = LANES[k]
-        act(dcols(s, k), IND(C(X, 0, 4096), C("li%d" % s, a, a + n)))
+    def tries(s, between):
+        for k, (c0, c1) in enumerate(VEC[s]):
+            tt(dcols(s, c0, c1), IND(C("xw", 0, 4096), C("li%d" % s, 16 * c0, 16 * c1)), QR(c0, c1), OP.subtract)
+            a0, a1 = SCA[s][k]
+            act(dcols(s, a0, a1), IND(C("xw", 0, 4096), C("li%d" % s, 16 * a0, 16 * a1)))
+            if k == 0:
+                between()
+        (c0, c1), (d0, d1) = VEC[s]
+        act(ring(s, c0, c1), dcols(s, c0, c1), AF.Abs)
+        dist(s, c0, c1)
+        for a0, a1 in SCA[s]:
+            for c in range(a0, a1, 2):
+                e = min(c + 2, a1)
+                bank = C("SUB%d" % (turn[0] % 2), 0, 256 * (e - c))
+                turn[0] += 1
+                total(bank, [(C("nid"), QR(c, e)), (C("idm"), dcols(s, c, e))])
+                act(ring(s, c, e), bank, AF.Abs)
+        dist(s, SCA[s][0][0], 16)
+        act(ring(s, d0, d1), dcols(s, d0, d1), AF.Abs)
+        dist(s, d0, d1)
 
-    def ssub(s, k):
-        for h in range(2):
-            _, lo, hi = half(k, h)
-            a = 16 * LANES[k][0]
-            o = C("SUB%d" % h, 0, hi - lo)
-            mms([(o, C("nid"), C("qr", a + lo, a + hi), True, False), (o, C("idm"), C("dd", 4096 * s + a + lo, 4096 * s + a + hi), False, True)])
-
-    def vabs(s, k, c0=0, c1=None):
-        c1 = LANES[k][1] // 16 if c1 is None else c1
-        n, a = "ring%d" % k, 4096 * s + 16 * LANES[k][0]
-        act((T[n][:, c0:c1, :, :], [(n, 256 * c0, 256 * c1)], []), C("dd", a + 256 * c0, a + 256 * c1), AF.Abs)
-
-    def sabs(s, k):
-        for h in range(2):
-            r, lo, hi = half(k, h)
-            act(r, C("SUB%d" % h, 0, hi - lo), AF.Abs)
-
-    def dist(s, k, c0=0, c1=None):
-        c1 = LANES[k][1] // 16 if c1 is None else c1
-        a, n = LANES[k][0] + 16 * c0, 16 * (c1 - c0)
-        o = C("K%d" % (s % 2), a, a + n)
-        rn = "ring%d" % k
-        mms([(o, PB(0), C("ep", 0, n), True, False)] + [(o, C("bw", 15 - r, 143 - r), (T[rn][:, c0:c1, r, :], [(rn, 256 * c0, 256 * c1)], []), False, r == 15) for r in range(16)])
-
-    def sdist(s):
-        dist(s, 2, 0, (256 - VL) // 16)
-
-    def sA(s, X):
-        if s:
-            sget(s, 2, X)
-            ssub(s, 2)
-        vabs(s, 0)
-        dist(s, 0)
-        sget(s, 3, X)
-        sabs(s, 2)
-        ssub(s, 3)
-
-    def sB(s):
-        vabs(s, 1)
-        dist(s, 1)
-        sabs(s, 3)
-        sdist(s)
-
-    def minscan(s):
-        scan(C("km", LEAST[s], LEAST[s] + 256), C("mn0"), C("K%d" % (s % 2), 0, 256), OP.max, OP.min)
+    def minscan(s, n=256):
+        scan(C("km", LEAST[s], LEAST[s] + n), C("mn0", 0, n), C("K%d" % (s % 2), 0, n), OP.max, OP.min)
 
     def maxscan(s):
         scan(C("km", MOST[s], MOST[s] + 256), C("mx0"), C("K%d" % (s % 2), 0, 256), OP.add, OP.max)
 
-    def bcast(bank, at, srcs, whole):
-        return [(C(bank, at + r, at + 256, 16), PB(r), src, whole and i == 0, whole and i == len(srcs) - 1) for r in range(16) for i, src in enumerate(srcs)]
+    def best(s, n=256):
+        return C("km", LEAST[s] + 15, LEAST[s] + n, 16)
+
+    def bcast(bank, at, src):
+        mms([(C(bank, at + r, at + 256, 16), M("pb", r), src, True, True) for r in range(16)])
+
+    def keep_others(s):
+        tt(B("lim", s), IND(C("pw", 0, 1024), C("uo%d" % s)), B("yy", s), OP.min)
 
     for t in range(R):
         last = t == R - 1
-        split = 16 if last else SPLIT
         q, qn = "qf%d" % (t % 2), "qf%d" % ((t + 1) % 2)
         X3, P3 = "xb%d" % t, "pb%d" % t
-        if t:
-            entries(0, "pw")
-        vget(0, 0, "xw")
-        sget(0, 2, "xw")
-        ssub(0, 2)
-        if t == 0:
-            constants()
-            load_mothers()
-        vget(0, 1, "xw")
-        if t == 0:
-            send(0)
-        sA(0, "xw")
-        if t == 0:
-            keep_mothers()
-            late_constants()
-        mother(0)
-        entries(1, "pw")
-        vget(1, 0, "xw")
-        sB(0)
-        mother(1)
-        entries(2, "pw")
-        vget(1, 1, "xw")
+        place = H + 64 * t
+        send(t, "p")
+        send(t, "x")
+        tries(0, lambda: (mother(0), entries(1)))
         act(C("b1"), IND(C("mw"), C("uo0")))
-        cp(C("mmb"), C("mmi"))
+        tries(1, lambda: (mother(1), entries(2)))
         mother(2)
+        cp(C("pk", 0, 64), C("fillk"))
+        iota(C("cf", 0, 256), [[0, 256]], 0, 0)
         minscan(0)
         maxscan(0)
-        sA(1, "xw")
-        ts(U("fc", 1), C("km", 15, 256, 16), C("th32"), OP.is_ge)
-        cp(C("f0h"), U("fc", 1))
-        act(C("li32", 0, 256), IND(C("pw", 0, 1024), C("uo0")))
-        sB(1)
-        mms([(C("SM", 16, 32), C("sw"), C("f0h"), True, True), (C("SM", 32, 48), C("swi"), C("mmb"), True, False), (C("SM", 32, 48), C("idm"), C("dlt"), False, True)])
-        vget(2, 0, "xw")
-        vget(2, 1, "xw")
-        act(C("li32", 256, 512), IND(C("pw", 0, 1024), C("uo1")))
-        minscan(1)
-        maxscan(1)
-        sA(2, "xw")
+        ts(U("fc", 1), best(0), C("th32"), OP.is_ge)
+        total(C("SM", 16, 32), [(C("sw"), U("fc", 1))])
+        total(C("SM", 32, 48), [(C("swi"), U("uu", 0))])
+        total(C("ZA", 0, 256), [(C("i4k"), C(q, 0, 256)), (C("idm"), C("nib"))])
+        act(C("qp"), C("ZA", 0, 256))
+        act(C("ud2"), U("uu", 2), AF.Copy, NUM + 256.0 + 64 * t, -1.0)
         tt(C("ex"), U("fc", 1), C("SM", 16, 32), OP.mult)
-        tt(C("exd"), C("ex"), C("SM", 32, 48), OP.mult)
-        tt(C("xo"), C("exd"), U("uu", 0), OP.add)
+        tt(C("ex"), C("ex"), C("SM", 32, 48), OP.mult)
+        tt(C("xo"), C("ex"), U("uu", 0), OP.add)
         cp(C("xo16"), C("xo"))
+        tt(C("ud"), C("uu"), C("dp"), OP.subtract)
+        tries(2, lambda: None)
         cp(IND(C("mw"), C("xo16")), C("b1"))
         if last:
-            dma("om", T.ym[:], T["mw"][0:128:16, :], [("mw", 0, 1024)], [])
-        act(C("li32", 512, 768), IND(C("pw", 0, 1024), C("uo2")))
-        cp(U("wi", 0, 2), C("km", 1039, 1536, 16))
-        ts(U("wj", 0, 2), U("wi", 0, 2), 31, OP.bitwise_and)
-        cp(U("wb16", 0, 2), U("wj", 0, 2))
-        mms(bcast("WB0", 0, [U("wb16", 0)], True) + bcast("WB0", 256, [U("wb16", 1)], True))
-        sB(2)
-        entries(3, P3)
-        vget(3, 0, X3)
-        tt(C("ud"), C("uu"), C("dp"), OP.subtract)
-        ts(C("wm", 0, 512), C("WB0"), C("cole"), OP.is_equal)
-        act(C("WB0"), C("WB0"), AF.Square, C("colb"), 64.0)
-        tt(C("lim", 0, 512), C("li32", 0, 512), C("WB0"), OP.min)
-        act(C("tb32"), C(P3, 1024, 1025), AF.Copy, None, 32.0)
-        sget(3, 2, X3)
-        ssub(3, 2)
-        minscan(2)
-        maxscan(2)
-        ts(C("nft"), C("km", 271, 768, 16), C("th32"), OP.is_ge)
+            dma("om", T.ym[:], T["mw"][0:128:16, :], [("mw", 0, 1024)], [], 2500)
+        minscan(1)
+        maxscan(1)
         cp(C("ki"), C("km", 15, 1024, 16))
-        tt(U("fc", 2), U("fc", 1), U("nft", 0), OP.mult)
         ts(C("em"), C("ki"), 31, OP.bitwise_and)
-        tt(U("fc", 3), U("fc", 2), U("nft", 1), OP.mult)
-        tt(C("hit"), U("fc", 0, 3), U("fc", 1, 3), OP.subtract)
-        scan(C("cum", 1, 17), C("one"), U("fc", 3), OP.mult, OP.add)
-        tt(C("te"), C("hit"), U("em", 0, 3), OP.mult)
-        tt(C("tu"), C("hit"), C("uu"), OP.mult)
+        cp(U("wb16", 0, 2), U("em", 2, 2))
+        ts(U("nft", 0), best(1), C("th32"), OP.is_ge)
+        tt(U("fc", 2), U("fc", 1), U("nft", 0), OP.mult)
+        bcast("WB", 0, U("wb16", 0))
+        bcast("WB", 256, U("wb16", 1))
+        act(B("yy", 0, 2), C("WB"), AF.Square, C("colb"), 64.0)
+        act(C("tb32"), C(P3, 1024, 1025), AF.Copy, None, 32.0)
+        tt(C("hit"), U("fc", 0, 2), U("fc", 1, 2), OP.subtract)
+        tt(U("te", 0, 2), C("hit"), U("em", 0, 2), OP.mult)
         tt(U("te", 0), U("te", 0), U("te", 1), OP.add)
-        tt(C("us"), U("tu", 0), U("tu", 1), OP.add)
-        tt(U("te", 0), U("te", 0), U("te", 2), OP.add)
+        tt(U("tu", 2), U("fc", 2), U("uu", 2), OP.mult)
+        tt(U("tu", 0, 2), C("hit"), U("uu", 0, 2), OP.mult)
+        tt(U("tu", 2), U("tu", 2), U("tu", 0), OP.add)
+        tt(U("tu", 2), U("tu", 2), U("tu", 1), OP.add)
+        tt(C("pack"), IND(C(P3, 0, 1024), C("uo3")), C("qp"), OP.add)
+        keep_others(0)
+        keep_others(1)
+        for h in range(2):
+            total(C("SUB%d" % h), [(C("zm"), QR(0, 2))], True, False)
+
+        minscan(2)
+        ts(U("nft", 1), best(2), C("th32"), OP.is_ge)
+        tt(U("fc", 3), U("fc", 2), U("nft", 1), OP.mult)
+        scan(C("cum", 1, 17), C("one"), U("fc", 3), OP.mult, OP.add)
+        tt(C("fl"), U("fc", 3), C("lub"), OP.mult)
+        total(C("SM", 48, 64), [(C("idm"), C("lub")), (C("trim"), U("fc", 3)), (C("bo"), C("cum", 0, 16)), (C("nid"), C("fl"))])
+        ts(C("sl16"), C("SM", 48, 64), 256.0, OP.add)
+        cp(IND(C("pk"), C("sl16")), C("pack"))
+        ts(C("a3"), C("pk", 0, 64), 4095, OP.bitwise_and)
+        cp(C("li3"), C("a3"))
+        ts(C("q3"), C("pk", 0, 64), 12, OP.arith_shift_right, 8447, OP.bitwise_and)
+        cp(C("sq"), C("q3"))
+        maxscan(2)
+        cp(C("k2"), C("km", 1039, 1536, 16))
+        ts(C("e2"), C("k2"), 31, OP.bitwise_and)
+        tt(U("te", 2), U("fc", 2), U("e2", 0), OP.mult)
+        tt(U("te", 3), U("te", 0), U("te", 2), OP.add)
+        cp(U("wb16", 2), U("e2", 1))
+        bcast("WB", 0, U("te", 3))
+        bcast("K0", 0, U("wb16", 2))
+        act(B("yy", 2), C("K0", 0, 256), AF.Square, C("colb"), 64.0)
+        tt(C("us"), C("SM", 48, 64), C("ud2"), OP.add)
+        tt(C("us"), C("us"), U("fc", 3), OP.mult)
         tt(C("us"), C("us"), U("tu", 2), OP.add)
-        mms(bcast("SM", 256, [U("te", 0)], True))
         cp(C("us16"), C("us"))
-        cp(C("f2h"), U("fc", 3))
-        mms([(C("SM", 48, 64), C("bo"), C("cum", 0, 16), True, False), (C("SM", 48, 64), C("tri"), C("f2h"), False, True)])
-        mms([(C("SM", 80, 96), l, x, i == 0, i == 3) for i, (l, x) in enumerate([(C("bo"), C("cum", 0, 16)), (C("tri"), C("f2h")), (C("nid"), C("lub")), (C("idm"), U("gcs", t))])])
-        sget(3, 3, X3)
-        act(C("f2b"), U("fc", 3), AF.Copy, None, FAR)
-        act(C("hm"), U("fc", 3), AF.Copy, 1.0, -1.0)
-        mms([(C("KN", 0, 256), PB(0), C("lanep"), True, False)] + bcast("KN", 0, [C("f2b")], False))
-        sabs(3, 2)
-        ssub(3, 3)
-        ts(C("m1"), C("SM", 256, 512), C("colr1"), OP.is_equal)
-        tt(C("pm"), IND(C("pw", 0, 1024), C("us16")), C("m1"), OP.mult)
-        mms([(C("KN", 0, 256), C("bo256"), C("pm"), False, True)])
-        cp(U("wb16", 2), U("em", 3))
-        vabs(3, 0)
-        dist(3, 0)
-        sabs(3, 3)
-        a3, n3 = LANES[1]
-        vpart(3, a3, PART, X3)
-        mms(bcast("WB1", 0, [U("wb16", 2)], True))
-        sdist(3)
-        vabs(3, 1, 0, PART // 16)
-        dist(3, 1, 0, PART // 16)
-        tt(C("be"), U("em", 0, 3), U("bp", 0, 3), OP.add)
-        ts(C("fin"), C("SM", 48, 64), 64.0, OP.is_lt)
-        tt(C("hb"), C("hit"), C("be"), OP.mult)
-        tt(C("fin"), C("fin"), U("fc", 3), OP.mult)
+        ts(C("m1"), C("WB", 0, 256), C("colr1"), OP.is_equal)
+        for h in range(2):
+            mms([(C("SUB%d" % h, e, 512, 16), C("nid"), C("sq", 32 * h, 32 * h + 32), False, False) for e in range(16)])
+        for h in range(2):
+            act(C("dd3", 512 * h, 512 * h + 512), IND(C(X3), C("li3", 32 * h, 32 * h + 32)))
+            total(C("SUB%d" % h), [(C("idm"), C("dd3", 512 * h, 512 * h + 512))], False, True)
+            act(ring(3, 2 * h, 2 * h + 2), C("SUB%d" % h), AF.Abs)
+        dist(3, 0, 4)
+
+        ZS = (C("K0", 0, 256), C("K0", 256, 512), C("WB", 0, 256))
+
+        def answer(s):
+            total(ZS[s], [(C("nid"), B("yy", s)), (C("bo32"), C("pm"))])
+            act(B("rl", s), ZS[s], AF.Relu)
+
+        tt(C("pm"), IND(C("pw", 0, PDUMP), C("us16")), C("m1"), OP.mult)
+        total(C("KN", 0, 256), [(C("bo32"), C("pm"))])
+        ts(C("n3"), C("pk", 0, 64), 20, OP.arith_shift_right)
+        cp(C("nb"), C("n3"))
+        total(C("SM", 64, 68), [(W("bwn", r), C("nb", r, 64, 16)) for r in range(16)])
+        cp(C("ls16"), C("SM", 64, 68))
         tt(C("fud"), U("fc", 1, 3), C("ud"), OP.mult)
-        tt(C("bm"), C("KN", 0, 256), C("mask"), OP.mult)
-        act(C("kb"), C("KN", 0, 256))
-        act(C("WB1", 256, 512), C("WB1", 0, 256), AF.Square, C("colb"), 64.0)
-        mms([(C("KN", 256, 512), C("bo32"), C("pm"), True, False)])
-        scan(C("bs"), C("sd0"), C("bm"), OP.mult, OP.add)
-        ts(C("na"), C("bs", 15, 256, 16), -1.0, OP.mult, 0.5, OP.add)
-        tt(C("nb"), C("na"), C("lu"), OP.add)
-        act(C("nd"), C("nb"), AF.Copy, 1.0 / 512, -1.0 / 256)
-        vpart(3, a3 + PART, n3 - PART, X3)
+        tt(C("fud"), C("fud"), C("dp"), OP.add)
+        keep_others(2)
+        answer(2)
+        num = own(3, C("KN", 0, 256))
+        cp(C("kb16"), C("KN", 0, 256))
+        cp(C("an16"), num)
+        act(C("av"), IND(C("xw", 0, DUMP), C("an16")))
+        total(C("ZA", 0, 256), [(C("idm"), C(q, 0, 256)), (C("idm"), C("av"))])
+        if not last:
+            act(C("sg"), C("ZA", 0, 256), AF.Sign, -255.5)
+            total(C("SUB0", 0, 256), [(C("idm"), C(q, 0, 256)), (C("idm"), C("av")), (C("n128"), C("sg"))])
+            act(C(qn, 0, 256), C("SUB0", 0, 256), AF.Copy, -128.0)
 
-        def lowest(c0, c1):
-            for c in range(c0, c1):
-                for k, o in (("na", "aa"), ("nb", "ab")):
-                    act(C("junk", 0, 16 * c + 16), C("kb", 0, 16 * c + 16), AF.Sign, C(k, c, c + 1), None, C(o, c, c + 1))
-
-        lowest(0, SPLIT0)
-        vabs(3, 1, PART // 16)
-        dist(3, 1, PART // 16)
-        ts(C("wm", 512, 768), C("WB1", 0, 256), C("cole"), OP.is_equal)
-        tt(C("lim", 512, 768), C("li32", 512, 768), C("WB1", 256, 512), OP.min)
-        mms([(C("SM", 64, 80), C("idm32"), x, i == 0, i == 3) for i, x in enumerate([U("hb", 0), U("hb", 1), U("hb", 2), C("dn")])])
-        act(C("dd", 16384, 16384 + VL), C(q, 0, VL), AF.Copy, None, -1.0)
-        act(C("q2", 0, VL), C(q, 0, VL), AF.Copy, None, 2.0)
-        act(C("q2", VL, 256), C(q, VL, 256))
-        mms([(C("WB0", 0, 256), C("idm"), C(q), True, True)])
-        tt(C("nd"), C("nd"), C("dx"), OP.subtract)
-        tt(C("nd"), C("nd"), C("hm"), OP.mult)
-        lowest(SPLIT0, split)
-        minscan(3)
-        ts(C("c3"), C("km", 1551, 1792, 16), C("tb32"), OP.is_lt)
-        cp(C("k3"), C("km", 1551, 1792, 16))
-        tt(C("came"), C("c3"), C("fin"), OP.mult)
+        minscan(3, 64)
+        ts(C("c16"), best(3, 64), C("tb32"), OP.is_lt)
+        cp(C("fl64"), IND(C("ftab"), C("c16")))
+        cp(IND(C("cf"), C("ls16")), C("fl64"))
+        total(C("SM", 96, 112), [(C("nid"), U("fc", 3))] + [(W("bw", r), C("cf", r, 256, 16)) for r in range(16)])
+        cp(C("k3"), best(3, 64))
         ts(C("e3"), C("k3"), 31, OP.bitwise_and)
-        tt(C("got"), C("came"), C("hm"), OP.add)
-        tt(C("t3"), C("e3"), U("bp", 3), OP.add)
-        tt(C("cs"), C("came"), C("SM", 48, 64), OP.mult)
-        tt(C("i3"), C("t3"), C("came"), OP.mult)
-        act(C("cc"), C("came"), AF.Copy, None, 3904.0 + 64 * t)
+        ts(C("f3"), best(3, 64), C("tb32"), OP.is_ge, 2048.0, OP.mult)
+        tt(C("f3"), C("f3"), C("bp"), OP.add)
+        tt(C("t3"), C("e3"), C("f3"), OP.add)
+        ts(C("i316"), C("t3"), 1024.0, OP.min)
+        cp(C("xw", place, place + 64), IND(C("dd3"), C("i316")))
+        if not last:
+            act(C("got"), C("SM", 96, 112), AF.Copy, 1.0)
+            tt(C("vs"), C("xw", place, place + 64), C("sq"), OP.add)
+            ts(C("vt"), C("vs"), 255, OP.bitwise_and)
+            cp(IND(C(qn), C("ls16")), C("vt"))
         for s in range(3):
-            act(U("g48", s), C("got"))
-        mms(bcast("KN", 256, [C("cs"), C("cc")], False) + [(C("KN", 256, 512), PB(0), C("zz"), False, True)])
-        tt(C("i3"), C("i3"), C("SM", 64, 80), OP.add)
-        cp(C("i316"), C("i3"))
-        tt(C("cg"), C("came"), C("SM", 80, 96), OP.mult)
-        tt(C("vi"), IND(C("dd"), C("i316")), C("q2"), OP.add)
-        tt(C("og"), C("cg"), C("dx"), OP.add)
+            tt(U("so", s), C("SM", 96, 112), U("ud", s), OP.mult)
+        tt(C("so"), C("so"), C("fud"), OP.add)
+        cp(C("so16"), C("so"))
         if not last:
-            ts(C("vq"), C("vi"), 255, OP.bitwise_and)
-        cp(C("og16"), C("og"))
-        if not last:
-            cp(C(qn), C("vq"))
-            starts(t + 1, qn)
-            spread(qn, "G")
-            spread(qn, "S")
-        lowest(split, 16)
-        tt(C("gv"), C("vi"), C("WB0", 0, 256), OP.subtract)
-        ts(C("hv"), C("vi"), 1, OP.arith_shift_right)
-        cp(IND(C("xw"), C("og16")), C("gv"))
+            starts(qn, [(C("rr"), C("got"))])
+            for part in REPEAT:
+                repeat(qn, *part)
+        answer(1)
+        answer(0)
 
-        def lists():
-            tt(C("so"), C("fud"), C("g48"), OP.mult)
-            for s in (2, 1, 0):
-                tt(C("mn", 256 * s, 256 * s + 256), C("KN", 256, 512), C("wm", 256 * s, 256 * s + 256), OP.mult)
-                if s == 2:
-                    tt(C("so"), C("so"), C("dp"), OP.add)
-                if s == 1:
-                    cp(C("so16"), C("so"))
-
-        def lists_in():
-            for s in (2, 1, 0):
-                a, b = 256 * s, 256 * s + 256
-                tt(IND(C("pw"), U("so16", s)), C("lim", a, b), C("mn", a, b), OP.add)
+        total(C("KN", 256, 512), [(C("zm"), C("ep"))], True, False)
+        for c in range(16):
+            ts((T["eq"][:, c, 0:256 - 16 * c], [("eq", c, c + 1)], []), C("kb16", 16 * c, 256), C("bs", 783 + 16 * c, 784 + 16 * c), OP.is_equal)
+        for c0, c1 in ((0, 6), (6, 15)):
+            mms([(C("KN", 272 + 16 * c, 512), C("bo"), (T["eq"][:, c, 16:256 - 16 * c], [("eq", c, c + 1)], []), False, False) for c in range(c0, c1)])
+        total(C("KN", 256, 512), [(C("tri"), (T["eq"][:, :, 0:16], [("eq", 0, 16)], []))], False, True)
+        act(C("cntb"), C("KN", 256, 512), AF.Copy, None, 8192.0)
+        total(C("SUB1", 0, 16), [(C("i4k"), U("fc", 3)), (C("idm32"), num)] + [(M("dg", r), C("cntb", r, 256, 16)) for r in range(16)])
+        ts(C("hv"), C("ZA", 0, 256), 0.5, OP.mult, -0.25, OP.add)
+        tt(C("oh"), C("SUB1", 0, 16), C("dx"), OP.min)
+        cp(C("oh16"), C("oh"))
 
         def records():
-            tt(C("okd"), C("ab"), C("aa"), OP.is_equal)
-            tt(C("oh"), C("okd"), C("nd"), OP.mult)
-            tt(C("oh"), C("oh"), C("dx"), OP.add)
-            cp(C("oh16"), C("oh"))
             cp(IND(C("xw"), C("oh16")), C("hv"))
 
-        lists()
         if last:
             records()
-            dma("oy", T.yx[:], T["xw"][:, 0:4096], [("xw", 0, 4096)], [])
-            lists_in()
-            dma("op", T.yp[:], T["pw"][:, 0:1024], [("pw", 0, 1024)], [])
+            dma("oy", T.yx[:], T["xw"][:, 0:4096], [("xw", 0, 4096)], [], 7500)
+        for s in (2, 1, 0):
+            tt(IND(C("pw"), U("so16", s)), B("lim", s), B("rl", s), OP.add)
+        if last:
+            dma("op", T.yp[:], T["pw"][:, 0:1024], [("pw", 0, 1024)], [], 5000)
         else:
-            lists_in()
-            start_towns()
-            spread(qn, "V")
+            entries(0)
             records()
-            send(t + 1)
 
+    if not ORDER:
+        ORDER.extend(plan())
+    for i in ORDER:
+        calls[i][5]()
     for s in count:
         if known["G"].get(s, 0) < count[s]:
             g.wait_ge(T.sem[s], count[s])

@@ -1,16 +1,17 @@
 from concourse.mybir import AluOpType as OP, ActivationFunctionType as AF
 
 R, N = 3, 4
-BIG = 1000000.0
-H, ZERO, DUMP = 3904, 4096, 4288
+BIG, WHOLE = 16777216.0, 12582912.0
+H, ZERO, DUMP = 3904, 4096, 4304
 NUM, PDUMP = 1040, 1424
 REPEAT = [("S", 0, 4), ("S", 4, 11), ("G", 11, 16)]
 QV = 11
 VEC = [[(0, 4), (4, 11)], [(0, 4), (4, 11)], [(0, 7), (7, 11)]]
 SCA = [[(11, 13), (13, 16)]] * 3
 LEAST, MOST = [0, 256, 1024, 1536], [512, 768, 1280]
-FLOOR, HOP, GATHER, SCATTER, PE = 64, 180, 1.5, 3.5, 0.5
-PASSES = 4
+FLOOR, HOP, GATHER, SCATTER, PE = 64, 200, 1.5, 3.5, 0.5
+BYTES, LAND = 190, 2200
+PASSES, SHAKE = 300, 1500
 ORDER = []
 
 SCRATCH = {}
@@ -27,14 +28,15 @@ def _declare():
             k, n = w.split(":")
             sb[k] = (int(n), d)
 
-    add(b, "xw:4544 dd:12288 dd3:1040 qf0:608 qf1:608 cf:608 yy:768 fc:64 te:64 cum:24 fl:16 wb16:48 got:16 hit:32 m1:256 cntb:256 av:256 sg:256")
-    add(b, "sq:64 nb:64 fl64:64 ftab:16 bo:128 bw:144 bwf:144 bwn:144 pb:2048 dg:2048 rr:128 tri:128 trim:128 sw:128 idm:128 nid:128 i4k:128")
-    add(b, "n128:128 zm:128 lub:16 ep:256 nib:256 nib2:256")
-    add(f, "pw:1680 mw:1024 th32:1 tb32:1 km:1600 bm:1024 bs:1024 b1:256 lim:768 rl:768 uu:48 nft:32 tu:64 us:16 ud2:16 qp:256 pack:256 pm:256")
-    add(f, "ud:48 fud:48 so:48 ex:16 xo:16 oh:16 f3:4 t3:4")
-    add(f, "colr:1 colp:1 colg:1 colg15:1 colr1:1 colb:1 par:1 colsw:1 colp16:1 coln:1 cola:1 colc:1 cold:1 mr:256 mf:144 mg:256 mask:256 bo32:128 idm32:128 swi:128")
-    add(f, "mn0:256 mx0:256 sd0:256 one:16 lu:16 dp:48 dx:16 bp:4")
-    add(i, "twi:1024 pk:768 thi:1 u0i:16 mmi:16 ki:64 em:64 k2:32 e2:32 k3:4 e3:4 hv:256 a3:64 q3:64 n3:64 vs:64 vt:64 fillk:64 ip:1 il:16 pr:1 pp:1 b4:16")
+    add(b, "xw:4560 dd:12288 dd3:1040 qf0:608 qf1:608 cf:608 yy:768 fc:64 te:64 cum:24 fl:16 wb16:64 got:16 hit:32 m0:256 m1:256 cntb:256 av:256 sg:256 hv:256")
+    add(b, "sq:64 nb:64 fl64:64 ftab:16 bo:128 bw:144 bwf:144 bwn:144 bw2k:144 pb:2048 dg:2048 rr:128 tri:128 trim:128 tri4:128 sw:128 swb:128 idm:128 nid:128 i4k:128")
+    add(b, "n4k:128 n128:128 zm:128 lub:16 ep:256 nib:256 nib2:256 half:256")
+    add("float16", "bm:1024")
+    add(f, "pw:1680 mw:1024 th32:1 tb2k:1 km:1600 b1:256 lim:768 rl:768 uu:48 nft:32 tu:64 us:16 qp:256 pack:256 pm:256 hw:256")
+    add(f, "so:48 us0:16 xo:16 oh:16 num:16 pos:64")
+    add(f, "colr:1 colp:1 colg:1 colg15:1 colr1:1 colm:1 colb:1 par:1 colsg:1 colsw:1 colp16:1 colr16:1 coln:1 cola:1 colc:1 cold:1")
+    add(f, "mr:256 mf:144 mg:256 mask:256 bo32:128 idm32:128 sws:128 mn0:256 mx0:256 one:16 lu:16 dp:48 dx:16")
+    add(i, "twi:1024 pk:768 thi:1 u0i:16 mmi:16 ki:64 em:64 k2:32 e2:32 k3:4 e3:4 a3:64 q3:64 n3:64 vs:64 vt:64 fillk:64 ip:1 il:16 pr:1 pp:1 b4:16")
     add(u, "us16:16 so16:48 sl16:16 xo16:16 i316:4 c16:4 ls16:4 oh16:16 an16:16 kb16:256 li0:256 li1:256 li2:256 li3:64 uo0:16 uo1:16 uo2:16 uo3:16")
     for t in range(R):
         add(b, "xb%d:%d" % (t, H + 64 * t))
@@ -64,7 +66,7 @@ def _declare():
 
 
 _declare()
-SEMAPHORES = ["sv", "sa", "st", "sg", "dq", "dx", "dt", "dh", "dm", "oy", "op", "om"] + ["%s%d" % (k, t) for k in ("ax", "ap", "lx", "lp") for t in range(R)]
+SEMAPHORES = ["sv", "sa", "st", "sg", "dq", "dx", "dt", "dh", "dm", "oy", "oz", "op", "om"] + ["%s%d" % (k, t) for k in ("ax", "ap", "lx", "lp") for t in range(R)]
 
 
 def rank_program(g, core, T, topo):
@@ -99,7 +101,7 @@ def rank_program(g, core, T, topo):
                     if b in PS and not same:
                         out.append(tok)
                     elif l < hi and lo < h and (w or wr):
-                        if same and (q == "P" or not w):
+                        if same and q == "P":
                             continue
                         out.append(tok)
         return out
@@ -129,7 +131,7 @@ def rank_program(g, core, T, topo):
         def go():
             wait_toks("Y", deps("Y", reads, writes))
             finish("Y", sem, 16, g.sync.dma_start(out, in_), reads, writes, "dma")
-        calls.append(("Y", reads, writes, FLOOR, n, go))
+        calls.append(("Y", reads, writes, n // BYTES + FLOOR, n // BYTES + LAND, go))
 
     def plan():
         before, seen = [], {}
@@ -139,8 +141,8 @@ def rank_program(g, core, T, topo):
                 for (b, lo, hi) in regs:
                     for (l, h, w, j) in seen.get(b, []):
                         p = calls[j][0]
-                        if (b in PS and p == q == "P") or (l < hi and lo < h and (w or wr)):
-                            pre[j] = max(pre.get(j, 0), calls[j][4] + (0 if p == q and (q == "P" or not w) else HOP))
+                        if l < hi and lo < h and (w or wr):
+                            pre[j] = max(pre.get(j, 0), calls[j][4] + (0 if p == q == "P" else HOP))
             for wr, regs in ((False, reads), (True, writes)):
                 for (b, lo, hi) in regs:
                     seen[b] = [e for e in seen.get(b, []) if not (wr and lo <= e[0] and e[1] <= hi)] + [(lo, hi, wr, i)]
@@ -168,16 +170,19 @@ def rank_program(g, core, T, topo):
                     busy.setdefault(k, []).append((s, s + n, q))
             return at
 
-        every, best = list(range(len(calls))), None
-        order = every
+        every, zero, tail = list(range(len(calls))), [0] * len(calls), [c[4] - c[3] for c in calls]
+        best, end, dice = dict(enumerate(every)), None, 1
         for _ in range(PASSES):
-            at = place(order, before, [0] * len(calls))
-            end = max(at[i] + calls[i][4] for i in every)
-            if best is None or end < best[0]:
-                best = (end, sorted(every, key=lambda i: (at[i], i)))
-            back = place(sorted(every, key=lambda i: (-at[i] - calls[i][3], -i)), after, [c[4] - c[3] for c in calls])
-            order = sorted(every, key=lambda i: (-back[i] - calls[i][3], i))
-        return best[1]
+            key, lo = {}, (end or 0) * (dice % 97) / 97
+            for i in every:
+                dice = dice * 16807 % 2147483647
+                key[i] = max([best[i] + (dice % SHAKE if lo < best[i] < lo + 10 * SHAKE and end else 0)] + [key[j] + 0.001 for j in before[i]])
+            at = place(sorted(every, key=key.get), before, zero)
+            back = place(sorted(every, key=lambda i: (-at[i] - calls[i][3], -i)), after, tail)
+            at = place(sorted(every, key=lambda i: (-back[i] - calls[i][3], i)), before, zero)
+            if end is None or max(at[i] + calls[i][4] for i in every) <= end:
+                best, end = at, max(at[i] + calls[i][4] for i in every)
+        return sorted(every, key=lambda i: (best[i], i))
 
     def C(name, a=0, b=None, st=1):
         buf, at, n = PLACE[name]
@@ -220,7 +225,7 @@ def rank_program(g, core, T, topo):
 
     def short(x):
         buf = PLACE.get(x[1][0][0], (None,))[0]
-        return buf is None or SCRATCH[buf][2] in ("bfloat16", "uint16")
+        return buf is None or SCRATCH[buf][2] in ("bfloat16", "uint16", "float16")
 
     def work(out, *ins):
         if out[2]:
@@ -269,16 +274,18 @@ def rank_program(g, core, T, topo):
                 ins = g.tensor.matmul(o[0], l[0], r[0], a, b)
             return ins
         n = sum(max(64, cols(r)) * (PE if short(r) else 4 * PE) for (_, _, r, _, _) in lst)
-        op("P", [x for m in lst for x in m[1][1] + m[2][1]], [x for m in lst for x in m[0][1]], n, go)
+        group = [("group" + lst[0][0][1][0][0], 0, 1)]
+        whole = lst[0][3] and lst[-1][4]
+        op("P", [x for m in lst for x in m[1][1] + m[2][1]] + group * whole, [x for m in lst for x in m[0][1]] + group * (not whole), n, go)
 
     def total(out, terms, first=True, last=True):
         mms([(out, l, r, first and i == 0, last and i == len(terms) - 1) for i, (l, r) in enumerate(terms)])
 
-    dma("dq", T["qf0"][:, 0:256], T.qs[:], [], [("qf0", 0, 256)], 2500)
-    dma("dt", T["twi"][:], T.towns[:], [], [("twi", 0, 1024)], 5500)
-    dma("dh", T["thi"][:], T.th[:], [], [("thi", 0, 1)], 5500)
-    dma("dm", T["mo8"][:], T.mo[:], [], [("mo8", 0, 1024)], 5600)
-    dma("dx", T["xw"][:, 0:H], T.x[:], [], [("xw", 0, H)], 11000)
+    dma("dq", T["qf0"][:, 0:256], T.qs[:], [], [("qf0", 0, 256)], 128 * 512)
+    dma("dt", T["twi"][:], T.towns[:], [], [("twi", 0, 1024)], 128 * 4096)
+    dma("dh", T["thi"][:], T.th[:], [], [("thi", 0, 1)], 128 * 4)
+    dma("dm", T["mo8"][:], T.mo[:], [], [("mo8", 0, 1024)], 8 * 4096)
+    dma("dx", T["xw"][:, 0:H], T.x[:], [], [("xw", 0, H)], 256 * H)
 
     iota(C("ip"), [[0, 1]], 0, 1)
     iota(C("mf"), [[1, 144]], 0, 0)
@@ -287,7 +294,7 @@ def rank_program(g, core, T, topo):
     iota(C("mg"), [[16, 16], [0, 16]], 0, 0)
     iota(C("pw", NUM, PDUMP), [[1, PDUMP - NUM]], H, 0)
     for name, a, b, k in (("xw", H, DUMP, 0.0), ("pw", 1024, NUM, 0.0), ("dd3", 1024, 1040, 0.0), ("ftab", 0, 16, 0.0), ("ftab", 1, 2, 1.0 / 512), ("zm", 0, 128, 0.0),
-                          ("one", 0, 16, 1.0), ("fc", 0, 16, 1.0), ("cum", 0, 24, 0.0)):
+                          ("one", 0, 16, 1.0), ("half", 0, 256, -0.5), ("fc", 0, 16, 1.0), ("cum", 0, 24, 0.0)):
         fill(C(name, a, b), k)
     ts(C("pr"), C("ip"), 15, OP.bitwise_and)
     ts(C("pp"), C("ip"), 1, OP.bitwise_and)
@@ -342,17 +349,18 @@ def rank_program(g, core, T, topo):
         act(C("mw", 512 * h, 512 * h + 512), C(b))
 
     ts(C("mn0"), C("mr"), 0.0, OP.is_equal, 2.0 * BIG, OP.mult)
-    ts(C("sd0"), C("mr"), 0.0, OP.not_equal)
-    ts(C("mx0"), C("mr"), 0.0, OP.is_equal, -BIG, OP.mult)
+    ts(C("mx0"), C("mr"), 0.0, OP.is_equal, -BIG / 16, OP.mult)
     act(C("mn0"), C("mn0"), AF.Copy, -BIG)
     act(C("mx0"), C("mx0"), AF.Copy, 2.0)
     ts(C("colb"), C("colr"), 64.0, OP.mult, -1984.0, OP.add)
-    ts(C("colsw"), C("par"), -2.0, OP.mult, 1.0, OP.add)
+    ts(C("colm"), C("colr"), -1.0, OP.mult, -1.0, OP.add)
+    ts(C("colr16"), C("colr"), 16.0, OP.mult)
+    ts(C("colsg"), C("par"), -2.0, OP.mult, 1.0, OP.add)
     ts(C("cola"), C("colr"), 0.0, OP.is_equal, 1048576.0, OP.mult)
     ts(C("colc"), C("colr"), 1.0, OP.is_equal, 65536.0, OP.mult)
     ts(C("coln"), C("colr"), 2.0, OP.is_lt)
     ts(C("cold"), C("colr"), 15.0, OP.mult, 1.0, OP.add)
-    tt(C("colsw"), C("colsw"), C("colp"), OP.add)
+    tt(C("colsw"), C("colsg"), C("colp"), OP.add)
     tt(C("coln"), C("coln"), C("cold"), OP.mult)
     ts(C("tri"), C("mr", 0, 128), C("colr"), OP.is_gt)
     ts(C("nib"), C("mr"), C("cola"), OP.mult)
@@ -363,7 +371,14 @@ def rank_program(g, core, T, topo):
     act(C("i4k"), C("idm"), AF.Copy, None, 4096.0)
     act(C("n128"), C("idm"), AF.Copy, None, -128.0)
     act(C("trim"), C("idm"), AF.Copy, None, -256.0)
-    tt(C("swi"), C("sw"), C("idm"), OP.subtract)
+    act(C("n4k"), C("idm"), AF.Copy, None, -4096.0)
+    ts(C("bw2k"), C("mf"), C("colg15"), OP.is_equal, 2048.0, OP.mult)
+    ts(C("sws"), C("sw"), C("colsg"), OP.mult, -1.0, OP.mult)
+    tt(C("swb"), C("sw"), C("idm"), OP.add)
+    act(C("swb"), C("swb"), AF.Copy, None, 4096.0)
+    tt(C("tri4"), C("tri"), C("i4k"), OP.add)
+    iota(C("pos"), [[256, 4], [1, 16]], 0, 0)
+    ts(C("pos"), C("pos"), C("colr16"), OP.add)
     ts(C("fillk"), C("nib", 0, 64), 33554432.0, OP.add)
     ts(C("bwn"), C("mf"), C("colg15"), OP.is_equal, C("coln"), OP.mult)
     tt(C("trim"), C("trim"), C("tri"), OP.add)
@@ -372,9 +387,8 @@ def rank_program(g, core, T, topo):
     act(C("idm32"), C("idm"))
     act(C("lub"), C("lu"))
     for s in range(3):
-        act(U("dp", s), C("lu"), AF.Copy, float(PDUMP))
-    act(C("dx"), C("lu"), AF.Copy, float(DUMP))
-    act(C("bp"), C("lu", 0, 4), AF.Copy, -1.0, 16.0)
+        act(U("dp", s), C("lu"), AF.Copy, PDUMP - 8192.0)
+    act(C("dx"), C("lu"), AF.Copy, DUMP - 2048.0)
     for r in range(16):
         ts(M("pb", r), C("bo"), C("mask", r, r + 1), OP.mult)
         act(M("dg", r), C("idm"), AF.Identity, None, C("mask", r, r + 1))
@@ -394,12 +408,14 @@ def rank_program(g, core, T, topo):
             note("dma", [(src, 0, n)], [], (lsem, count[lsem], vc))
             count[asem] = len(topo.engines(frm, core))
             note("dma", [], [(dest, 0, n)], (asem, count[asem], {asem: count[asem]}))
-        calls.append(("G", [(src, 0, n)], [(dest, 0, n)], 1100, 16000 if kind == "x" else 8000, go))
+        first, then = ([("sent", t, t + 1)], []) if kind == "p" else ([], [("sent", t, t + 1)])
+        calls.append(("G", [(src, 0, n)] + first, [(dest, 0, n)] + then, 1100, 16000 if kind == "x" else 8000, go))
 
     def own(k, src):
-        tt(B("bm", k), src, C("mask"), OP.mult)
-        scan(B("bs", k), C("sd0"), B("bm", k), OP.mult, OP.add)
-        return C("bs", 256 * k + 15, 256 * k + 256, 16)
+        cp(B("bm", k), src)
+        u = C("SM", 208 + 16 * k, 224 + 16 * k)
+        total(u, [(M("dg", r), C("bm", 256 * k + r, 256 * k + 256, 16)) for r in range(16)])
+        return u
 
     def mother(s):
         u = own(s, IND(C("mw"), C("uo%d" % s)))
@@ -415,7 +431,8 @@ def rank_program(g, core, T, topo):
         return (T[n][:, c0:c1, :, :] if r is None else T[n][:, c0:c1, r, :], [(n, c0, c1)], [])
 
     def dist(s, c0, c1):
-        total(C("K%d" % (s % 2), 16 * c0, 16 * c1), [(C("idm"), C("ep", 0, 16 * (c1 - c0)))] + [(W("bw", r), ring(s, c0, c1, r)) for r in range(16)])
+        low = (C("idm"), C("ep", 0, 16 * (c1 - c0))) if s < 3 else (C("idm32"), C("pos"))
+        total(C("K%d" % (s % 2), 16 * c0, 16 * c1), [low] + [(W("bw" if s < 3 else "bw2k", r), ring(s, c0, c1, r)) for r in range(16)])
 
     turn = [0]
 
@@ -449,8 +466,8 @@ def rank_program(g, core, T, topo):
     def best(s, n=256):
         return C("km", LEAST[s] + 15, LEAST[s] + n, 16)
 
-    def bcast(bank, at, src):
-        mms([(C(bank, at + r, at + 256, 16), M("pb", r), src, True, True) for r in range(16)])
+    def bcast(src):
+        mms([(C("WB", r, 512, 16), M("pb", r), src, True, True) for r in range(16)])
 
     def keep_others(s):
         tt(B("lim", s), IND(C("pw", 0, 1024), C("uo%d" % s)), B("yy", s), OP.min)
@@ -463,7 +480,6 @@ def rank_program(g, core, T, topo):
         send(t, "p")
         send(t, "x")
         tries(0, lambda: (mother(0), entries(1)))
-        act(C("b1"), IND(C("mw"), C("uo0")))
         tries(1, lambda: (mother(1), entries(2)))
         mother(2)
         cp(C("pk", 0, 64), C("fillk"))
@@ -471,20 +487,16 @@ def rank_program(g, core, T, topo):
         minscan(0)
         maxscan(0)
         ts(U("fc", 1), best(0), C("th32"), OP.is_ge)
-        total(C("SM", 16, 32), [(C("sw"), U("fc", 1))])
-        total(C("SM", 32, 48), [(C("swi"), U("uu", 0))])
+        total(C("SM", 16, 32), [(C("swb"), U("fc", 1)), (C("sws"), U("uu", 0))])
         total(C("ZA", 0, 256), [(C("i4k"), C(q, 0, 256)), (C("idm"), C("nib"))])
         act(C("qp"), C("ZA", 0, 256))
-        act(C("ud2"), U("uu", 2), AF.Copy, NUM + 256.0 + 64 * t, -1.0)
-        tt(C("ex"), U("fc", 1), C("SM", 16, 32), OP.mult)
-        tt(C("ex"), C("ex"), C("SM", 32, 48), OP.mult)
-        tt(C("xo"), C("ex"), U("uu", 0), OP.add)
-        cp(C("xo16"), C("xo"))
-        tt(C("ud"), C("uu"), C("dp"), OP.subtract)
+        act(C("us0"), U("uu", 0), AF.Identity, 8192.0, C("colsg"))
+        tt(C("xo"), C("SM", 16, 32), C("us0"), OP.max)
+        ts(C("xo16"), C("xo"), -8192.0, OP.add, C("colsg"), OP.mult)
         tries(2, lambda: None)
-        cp(IND(C("mw"), C("xo16")), C("b1"))
+        cp(IND(C("mw"), C("xo16")), B("bm", 0))
         if last:
-            dma("om", T.ym[:], T["mw"][0:128:16, :], [("mw", 0, 1024)], [], 2500)
+            dma("om", T.ym[:], T["mw"][0:128:16, :], [("mw", 0, 1024)], [], 8 * 4096)
         minscan(1)
         maxscan(1)
         cp(C("ki"), C("km", 15, 1024, 16))
@@ -492,22 +504,21 @@ def rank_program(g, core, T, topo):
         cp(U("wb16", 0, 2), U("em", 2, 2))
         ts(U("nft", 0), best(1), C("th32"), OP.is_ge)
         tt(U("fc", 2), U("fc", 1), U("nft", 0), OP.mult)
-        bcast("WB", 0, U("wb16", 0))
-        bcast("WB", 256, U("wb16", 1))
+        bcast(U("wb16", 0, 2))
         act(B("yy", 0, 2), C("WB"), AF.Square, C("colb"), 64.0)
-        act(C("tb32"), C(P3, 1024, 1025), AF.Copy, None, 32.0)
+        act(C("tb2k"), C(P3, 1024, 1025), AF.Copy, -1024.0, 2048.0)
         tt(C("hit"), U("fc", 0, 2), U("fc", 1, 2), OP.subtract)
         tt(U("te", 0, 2), C("hit"), U("em", 0, 2), OP.mult)
         tt(U("te", 0), U("te", 0), U("te", 1), OP.add)
-        tt(U("tu", 2), U("fc", 2), U("uu", 2), OP.mult)
-        tt(U("tu", 0, 2), C("hit"), U("uu", 0, 2), OP.mult)
-        tt(U("tu", 2), U("tu", 2), U("tu", 0), OP.add)
-        tt(U("tu", 2), U("tu", 2), U("tu", 1), OP.add)
+        total(C("SM", 112, 160), [(C("idm32"), C("uu")), (C("n4k"), U("fc", 0, 3))], True, False)
+        total(C("SM", 112, 144), [(C("i4k"), U("fc", 1, 2))], False, True)
+        act(U("tu", 0), C("SM", 112, 128))
+        tt(U("tu", 1), C("SM", 128, 144), U("tu", 0), OP.min)
+        tt(U("tu", 2), C("SM", 144, 160), U("tu", 1), OP.min)
+        act(U("tu", 3), U("tu", 2), AF.Copy, 8192.0 - NUM - 64 * t)
         tt(C("pack"), IND(C(P3, 0, 1024), C("uo3")), C("qp"), OP.add)
         keep_others(0)
         keep_others(1)
-        for h in range(2):
-            total(C("SUB%d" % h), [(C("zm"), QR(0, 2))], True, False)
 
         minscan(2)
         ts(U("nft", 1), best(2), C("th32"), OP.is_ge)
@@ -515,6 +526,7 @@ def rank_program(g, core, T, topo):
         scan(C("cum", 1, 17), C("one"), U("fc", 3), OP.mult, OP.add)
         tt(C("fl"), U("fc", 3), C("lub"), OP.mult)
         total(C("SM", 48, 64), [(C("idm"), C("lub")), (C("trim"), U("fc", 3)), (C("bo"), C("cum", 0, 16)), (C("nid"), C("fl"))])
+        total(C("SM", 32, 48), [(C("tri4"), U("fc", 3)), (C("bo"), C("cum", 0, 16))])
         ts(C("sl16"), C("SM", 48, 64), 256.0, OP.add)
         cp(IND(C("pk"), C("sl16")), C("pack"))
         ts(C("a3"), C("pk", 0, 64), 4095, OP.bitwise_and)
@@ -525,71 +537,64 @@ def rank_program(g, core, T, topo):
         cp(C("k2"), C("km", 1039, 1536, 16))
         ts(C("e2"), C("k2"), 31, OP.bitwise_and)
         tt(U("te", 2), U("fc", 2), U("e2", 0), OP.mult)
-        tt(U("te", 3), U("te", 0), U("te", 2), OP.add)
-        cp(U("wb16", 2), U("e2", 1))
-        bcast("WB", 0, U("te", 3))
-        bcast("K0", 0, U("wb16", 2))
-        act(B("yy", 2), C("K0", 0, 256), AF.Square, C("colb"), 64.0)
-        tt(C("us"), C("SM", 48, 64), C("ud2"), OP.add)
-        tt(C("us"), C("us"), U("fc", 3), OP.mult)
-        tt(C("us"), C("us"), U("tu", 2), OP.add)
-        cp(C("us16"), C("us"))
-        ts(C("m1"), C("WB", 0, 256), C("colr1"), OP.is_equal)
-        for h in range(2):
-            mms([(C("SUB%d" % h, e, 512, 16), C("nid"), C("sq", 32 * h, 32 * h + 32), False, False) for e in range(16)])
+        tt(U("wb16", 2), U("te", 0), U("te", 2), OP.add)
+        cp(U("wb16", 3), U("e2", 1))
+        bcast(U("wb16", 2, 2))
+        act(B("yy", 2), C("WB", 256, 512), AF.Square, C("colb"), 64.0)
+        tt(C("us"), C("SM", 32, 48), U("tu", 3), OP.max)
+        ts(C("us16"), C("us"), NUM + 64.0 * t - 4096, OP.add)
+        act(C("m0"), C("WB", 0, 256), AF.Square, C("colm"))
+        act(C("m1"), C("m0"), AF.Relu, 1.0, -1.0)
         for h in range(2):
             act(C("dd3", 512 * h, 512 * h + 512), IND(C(X3), C("li3", 32 * h, 32 * h + 32)))
-            total(C("SUB%d" % h), [(C("idm"), C("dd3", 512 * h, 512 * h + 512))], False, True)
+            mms([(C("SUB%d" % h), C("idm"), C("dd3", 512 * h, 512 * h + 512), True, False)]
+                + [(C("SUB%d" % h, e, 512, 16), C("nid"), C("sq", 32 * h, 32 * h + 32), False, e == 15) for e in range(16)])
             act(ring(3, 2 * h, 2 * h + 2), C("SUB%d" % h), AF.Abs)
         dist(3, 0, 4)
 
         ZS = (C("K0", 0, 256), C("K0", 256, 512), C("WB", 0, 256))
 
         def answer(s):
-            total(ZS[s], [(C("nid"), B("yy", s)), (C("bo32"), C("pm"))])
-            act(B("rl", s), ZS[s], AF.Relu)
+            total(ZS[s], [(C("nid"), B("yy", s)), (C("idm"), B("bm", 3))])
+            act(B("rl", s), ZS[s], AF.Relu, 2048.0)
 
         tt(C("pm"), IND(C("pw", 0, PDUMP), C("us16")), C("m1"), OP.mult)
-        total(C("KN", 0, 256), [(C("bo32"), C("pm"))])
+        total(C("KN", 0, 256), [(C("i4k"), C("half")), (C("bo32"), C("pm"))])
         ts(C("n3"), C("pk", 0, 64), 20, OP.arith_shift_right)
         cp(C("nb"), C("n3"))
         total(C("SM", 64, 68), [(W("bwn", r), C("nb", r, 64, 16)) for r in range(16)])
         cp(C("ls16"), C("SM", 64, 68))
-        tt(C("fud"), U("fc", 1, 3), C("ud"), OP.mult)
-        tt(C("fud"), C("fud"), C("dp"), OP.add)
         keep_others(2)
+        u = own(3, C("KN", 0, 256))
         answer(2)
-        num = own(3, C("KN", 0, 256))
-        cp(C("kb16"), C("KN", 0, 256))
-        cp(C("an16"), num)
+        ts(C("an16"), u, 2048.0, OP.add)
+        act(C("num"), u)
         act(C("av"), IND(C("xw", 0, DUMP), C("an16")))
-        total(C("ZA", 0, 256), [(C("idm"), C(q, 0, 256)), (C("idm"), C("av"))])
+        total(C("ZA", 0, 256), [(C("idm"), C(q, 0, 256)), (C("idm"), C("half")), (C("idm"), C("av"))])
         if not last:
-            act(C("sg"), C("ZA", 0, 256), AF.Sign, -255.5)
+            act(C("sg"), C("ZA", 0, 256), AF.Sign, -255.0)
             total(C("SUB0", 0, 256), [(C("idm"), C(q, 0, 256)), (C("idm"), C("av")), (C("n128"), C("sg"))])
             act(C(qn, 0, 256), C("SUB0", 0, 256), AF.Copy, -128.0)
 
         minscan(3, 64)
-        ts(C("c16"), best(3, 64), C("tb32"), OP.is_lt)
+        ts(C("c16"), best(3, 64), C("tb2k"), OP.is_lt)
         cp(C("fl64"), IND(C("ftab"), C("c16")))
         cp(IND(C("cf"), C("ls16")), C("fl64"))
         total(C("SM", 96, 112), [(C("nid"), U("fc", 3))] + [(W("bw", r), C("cf", r, 256, 16)) for r in range(16)])
-        cp(C("k3"), best(3, 64))
-        ts(C("e3"), C("k3"), 31, OP.bitwise_and)
-        ts(C("f3"), best(3, 64), C("tb32"), OP.is_ge, 2048.0, OP.mult)
-        tt(C("f3"), C("f3"), C("bp"), OP.add)
-        tt(C("t3"), C("e3"), C("f3"), OP.add)
-        ts(C("i316"), C("t3"), 1024.0, OP.min)
-        cp(C("xw", place, place + 64), IND(C("dd3"), C("i316")))
+        ts(C("k3"), best(3, 64), C("tb2k"), OP.min)
+        ts(C("e3"), C("k3"), 2047, OP.bitwise_and)
+        cp(C("i316"), C("e3"))
         if not last:
-            act(C("got"), C("SM", 96, 112), AF.Copy, 1.0)
+            cp(C("xw", place, place + 64), IND(C("dd3"), C("i316")))
+        act(C("got"), C("SM", 96, 112), AF.Copy, 1.0)
+        if not last:
             tt(C("vs"), C("xw", place, place + 64), C("sq"), OP.add)
             ts(C("vt"), C("vs"), 255, OP.bitwise_and)
             cp(IND(C(qn), C("ls16")), C("vt"))
-        for s in range(3):
-            tt(U("so", s), C("SM", 96, 112), U("ud", s), OP.mult)
-        tt(C("so"), C("so"), C("fud"), OP.add)
-        cp(C("so16"), C("so"))
+        total(C("SM", 160, 208), [(C("idm32"), C("uu")), (C("n4k"), U("fc", 1, 3))], True, False)
+        mms([(C("SM", 160 + 16 * s, 176 + 16 * s), C("n4k"), C("got"), False, s == 2) for s in range(3)])
+        tt(C("so"), C("SM", 160, 208), C("dp"), OP.min)
+        ts(C("so16"), C("so"), 8192.0, OP.add)
         if not last:
             starts(qn, [(C("rr"), C("got"))])
             for part in REPEAT:
@@ -599,26 +604,29 @@ def rank_program(g, core, T, topo):
 
         total(C("KN", 256, 512), [(C("zm"), C("ep"))], True, False)
         for c in range(16):
-            ts((T["eq"][:, c, 0:256 - 16 * c], [("eq", c, c + 1)], []), C("kb16", 16 * c, 256), C("bs", 783 + 16 * c, 784 + 16 * c), OP.is_equal)
+            ts((T["eq"][:, c, 0:256 - 16 * c], [("eq", c, c + 1)], []), C("bm", 768 + 16 * c, 1024), C("num", c, c + 1), OP.is_equal)
         for c0, c1 in ((0, 6), (6, 15)):
             mms([(C("KN", 272 + 16 * c, 512), C("bo"), (T["eq"][:, c, 16:256 - 16 * c], [("eq", c, c + 1)], []), False, False) for c in range(c0, c1)])
         total(C("KN", 256, 512), [(C("tri"), (T["eq"][:, :, 0:16], [("eq", 0, 16)], []))], False, True)
         act(C("cntb"), C("KN", 256, 512), AF.Copy, None, 8192.0)
-        total(C("SUB1", 0, 16), [(C("i4k"), U("fc", 3)), (C("idm32"), num)] + [(M("dg", r), C("cntb", r, 256, 16)) for r in range(16)])
-        ts(C("hv"), C("ZA", 0, 256), 0.5, OP.mult, -0.25, OP.add)
+        total(C("SUB1", 0, 16), [(C("i4k"), U("fc", 3)), (C("idm32"), C("num"))] + [(M("dg", r), C("cntb", r, 256, 16)) for r in range(16)])
+        act(C("hw"), C("ZA", 0, 256), AF.Copy, WHOLE, 0.5)
+        act(C("hv"), C("hw"), AF.Copy, -WHOLE)
         tt(C("oh"), C("SUB1", 0, 16), C("dx"), OP.min)
-        cp(C("oh16"), C("oh"))
+        ts(C("oh16"), C("oh"), 2048.0, OP.add)
 
         def records():
             cp(IND(C("xw"), C("oh16")), C("hv"))
 
         if last:
             records()
-            dma("oy", T.yx[:], T["xw"][:, 0:4096], [("xw", 0, 4096)], [], 7500)
+            dma("oy", T.yx[:, 0:place], T["xw"][:, 0:place], [("xw", 0, place)], [], 256 * place)
+            cp(C("xw", place, place + 64), IND(C("dd3"), C("i316")))
+            dma("oz", T.yx[:, place:4096], T["xw"][:, place:4096], [("xw", place, 4096)], [], 256 * 64)
         for s in (2, 1, 0):
             tt(IND(C("pw"), U("so16", s)), B("lim", s), B("rl", s), OP.add)
         if last:
-            dma("op", T.yp[:], T["pw"][:, 0:1024], [("pw", 0, 1024)], [], 5000)
+            dma("op", T.yp[:], T["pw"][:, 0:1024], [("pw", 0, 1024)], [], 128 * 4096)
         else:
             entries(0)
             records()

@@ -1,17 +1,19 @@
-from concourse.mybir import AluOpType as OP, ActivationFunctionType as AF
+from concourse.mybir import AxisListType, AluOpType as OP, ActivationFunctionType as AF
 
 R, N = 3, 4
-BIG, WHOLE = 16777216.0, 12582912.0
-H, ZERO, DUMP = 3904, 4096, 4304
+BIG = 16777216.0
+H, DUMP = 3904, 4304
 NUM, PDUMP = 1040, 1424
 REPEAT = [("S", 0, 4), ("S", 4, 11), ("G", 11, 16)]
 QV = 11
-VEC = [[(0, 4), (4, 11)], [(0, 4), (4, 11)], [(0, 7), (7, 11)]]
-SCA = [[(11, 13), (13, 16)]] * 3
-LEAST, MOST = [0, 256, 1024, 1536], [512, 768, 1280]
-FLOOR, HOP, GATHER, SCATTER, PE = 64, 200, 1.5, 3.5, 0.5
-BYTES, LAND = 190, 2200
-PASSES, SHAKE = 300, 1500
+VEC = [(0, 4, 8, 11), (0, 4, 8, 11), (0, 4, 8, 11)]
+SCA = [(11, 13, 16), (11, 13, 16), (11, 13, 16)]
+LISTS = [(0, 4, 10, 16), (0, 16), (0, 16)]
+SCANS = [(0, 256), (0, 256), (0, 128, 176, 256)]
+LEAST, MOST = [0, 256, 1024], [512, 768, 1280]
+FLOOR, HOP, GATHER, SCATTER, PE = 64, 325, 1.4, 3.0, 0.5
+BYTES, LAND = 290, 1100
+PASSES, STRETCH, SHAKE = 2000, 15000, (300, 800, 1500, 3000)
 ORDER = []
 
 SCRATCH = {}
@@ -28,16 +30,16 @@ def _declare():
             k, n = w.split(":")
             sb[k] = (int(n), d)
 
-    add(b, "xw:4560 dd:12288 dd3:1040 qf0:608 qf1:608 cf:608 yy:768 fc:64 te:64 cum:24 fl:16 wb16:64 got:16 hit:32 m0:256 m1:256 cntb:256 av:256 sg:256 hv:256")
-    add(b, "sq:64 nb:64 fl64:64 ftab:16 bo:128 bw:144 bwf:144 bwn:144 bw2k:144 pb:2048 dg:2048 rr:128 tri:128 trim:128 tri4:128 sw:128 swb:128 idm:128 nid:128 i4k:128")
-    add(b, "n4k:128 n128:128 zm:128 lub:16 ep:256 nib:256 nib2:256 half:256")
-    add("float16", "bm:1024")
-    add(f, "pw:1680 mw:1024 th32:1 tb2k:1 km:1600 b1:256 lim:768 rl:768 uu:48 nft:32 tu:64 us:16 qp:256 pack:256 pm:256 hw:256")
-    add(f, "so:48 us0:16 xo:16 oh:16 num:16 pos:64")
-    add(f, "colr:1 colp:1 colg:1 colg15:1 colr1:1 colm:1 colb:1 par:1 colsg:1 colsw:1 colp16:1 colr16:1 coln:1 cola:1 colc:1 cold:1")
-    add(f, "mr:256 mf:144 mg:256 mask:256 bo32:128 idm32:128 sws:128 mn0:256 mx0:256 one:16 lu:16 dp:48 dx:16")
-    add(i, "twi:1024 pk:768 thi:1 u0i:16 mmi:16 ki:64 em:64 k2:32 e2:32 k3:4 e3:4 a3:64 q3:64 n3:64 vs:64 vt:64 fillk:64 ip:1 il:16 pr:1 pp:1 b4:16")
-    add(u, "us16:16 so16:48 sl16:16 xo16:16 i316:4 c16:4 ls16:4 oh16:16 an16:16 kb16:256 li0:256 li1:256 li2:256 li3:64 uo0:16 uo1:16 uo2:16 uo3:16")
+    add(b, "xw:4560 dd:12288 dd3:1040 ab3:1024 qf0:608 qf1:608 cf:608 yy:1120 ys:64 fl:16 fc:64 te:48 cum:24 wb16:64 got:16 hit:32 m1:256 cntb:256 av:256 sg:256")
+    add(b, "sq:64 nb:64 fl64:64 fail:4 ftab:16 bo:128 bw:144 bwf:144 bwn:144 bw2k:144 pb:2048 dg:2048 rr:128 tri:128 trim:128 tri4:128 sw:128 swb:128")
+    add(b, "idm:128 nid:128 i4k:128 n4k:128 n128:128 zm:128 lub:16 ep:256 half:256 nib:256 nib2:256")
+    add("float16", "bm:1024 zs:64")
+    add(f, "pw:1680 mw:1024 th32:1 thb:1 tb2k:1 km:1536 lim:512 rl:512 zf:608 tid:1024 pf:768 fillk:64 qp:256 pack:256 uu:48 thr:32 tu:64 us:16 pm:256")
+    add(f, "so:32 us0:16 xo:16 oh:16 num:16 pos:64 lims:64 rls:64 ouf:4 b3:4 og:4 dps:4")
+    add(f, "colr:1 colp:1 colg:1 colg15:1 colr1:1 colb:1 par:1 colsg:1 colsw:1 colp16:1 colr16:1 coln:1 cola:1 colc:1 cold:1")
+    add(f, "mr:256 mf:144 mg:256 mask:256 bo32:128 idm32:128 sws:128 mn0:256 mx0:256 one:16 lu:16 dp:32 dx:16")
+    add(i, "twi:1024 pk:64 a3:64 q3:64 n3:64 thi:1 u0i:16 mmi:16 ki:64 em:64 k2:32 e2:32 k3:4 e3:4 vs:64 vt:64 hv:256 ip:1 il:16 pr:1 pp:1 b4:16")
+    add(u, "us16:16 so16:32 xo16:16 i316:4 c16:4 ls16:4 ou16:4 sl16:16 og16:4 oh16:16 an16:16 li0:256 li1:256 li2:256 li3:64 uo0:16 uo1:16 uo2:16 uo3:16")
     for t in range(R):
         add(b, "xb%d:%d" % (t, H + 64 * t))
         add(f, "pb%d:1032" % t)
@@ -53,7 +55,6 @@ def _declare():
         SCRATCH["all_" + d] = ("sbuf", [128, size[d]], d)
     for k in range(3):
         SCRATCH["ring%d" % k] = ("sbuf", [128, 16, 16, 16], b)
-    SCRATCH["ring3"] = ("sbuf", [128, 4, 16, 16], b)
     SCRATCH["qr"] = ("sbuf", [128, 256 * QV], b)
     SCRATCH["qr3"] = ("sbuf", [128, 256 - 16 * QV, 16], b)
     SCRATCH["eq"] = ("sbuf", [128, 16, 256], b)
@@ -155,28 +156,37 @@ def rank_program(g, core, T, topo):
         banks = [{b for (b, _, _) in c[1] + c[2] if b in PS} for c in calls]
 
         def place(order, lags, first):
-            at, busy = {}, {}
+            at, queue, bank = {}, {q: [] for q in ENG}, {b: [] for b in PS}
             for i in order:
-                q, n = calls[i][0], calls[i][3]
-                s = max([first[i]] + [at[j] + d for j, d in lags[i].items()])
-                taken = sorted([e for e in busy.get(q, []) if e[1] > s] + [(a - HOP, b + HOP) for k in banks[i] for (a, b, p) in busy.get(k, []) if p != q and b + HOP > s])
-                for (a, b) in taken:
-                    if a >= s + n:
-                        break
-                    s = max(s, b)
+                q, n, s = calls[i][0], calls[i][3], first[i]
+                for j, d in lags[i].items():
+                    if at[j] + d > s:
+                        s = at[j] + d
+                busy, seen = queue[q], None
+                while s != seen:
+                    k = len(busy)
+                    while k and busy[k - 1][1] > s:
+                        k -= 1
+                    while k < len(busy) and busy[k][0] < s + n:
+                        s, k = busy[k][1], k + 1
+                    seen = s
+                    for x in banks[i]:
+                        for (a, b, p) in bank[x]:
+                            if p != q and a - HOP < s + n and b + HOP > s:
+                                s = b + HOP
                 at[i] = s
-                busy.setdefault(q, []).append((s, s + n))
-                for k in banks[i]:
-                    busy.setdefault(k, []).append((s, s + n, q))
+                busy.insert(k, (s, s + n))
+                for x in banks[i]:
+                    bank[x].append((s, s + n, q))
             return at
 
         every, zero, tail = list(range(len(calls))), [0] * len(calls), [c[4] - c[3] for c in calls]
         best, end, dice = dict(enumerate(every)), None, 1
         for _ in range(PASSES):
-            key, lo = {}, (end or 0) * (dice % 97) / 97
+            key, lo, by = {}, (end or 0) * (dice % 97) / 97, SHAKE[dice % len(SHAKE)]
             for i in every:
                 dice = dice * 16807 % 2147483647
-                key[i] = max([best[i] + (dice % SHAKE if lo < best[i] < lo + 10 * SHAKE and end else 0)] + [key[j] + 0.001 for j in before[i]])
+                key[i] = max([best[i] + (dice % by if end and lo < best[i] < lo + STRETCH else 0)] + [key[j] + 0.001 for j in before[i]])
             at = place(sorted(every, key=key.get), before, zero)
             back = place(sorted(every, key=lambda i: (-at[i] - calls[i][3], -i)), after, tail)
             at = place(sorted(every, key=lambda i: (-back[i] - calls[i][3], i)), before, zero)
@@ -210,6 +220,9 @@ def rank_program(g, core, T, topo):
         else:
             x = T["qr"][:, 256 * c0:256 * c1] if e1 - e0 == 16 else T["qr"][:, 256 * c0 + e0:256 * c1:16]
         return (x, [("qr%d" % k, e0, e1) for k, (_, a, b) in enumerate(REPEAT) if a < c1 and c0 < b], [])
+
+    def pairs(bounds):
+        return list(zip(bounds, bounds[1:]))
 
     def rg(*xs):
         return [r for x in xs if isinstance(x, tuple) for r in x[1] + x[2]]
@@ -254,12 +267,11 @@ def rank_program(g, core, T, topo):
     def scan(out, d0, d1, o0, o1):
         op("V", rg(d0, d1), out[1], cols(out), lambda: g.vector.tensor_tensor_scan(out[0], d0[0], d1[0], 0.0, o0, o1))
 
+    def least(out, a):
+        op("V", rg(a), out[1], cols(a), lambda: g.vector.tensor_reduce(out[0], a[0], AxisListType.X, OP.min))
+
     def act(out, a, func=AF.Copy, bias=None, scale=None):
-        kw = {}
-        if bias is not None:
-            kw["bias"] = ap(bias)
-        if scale is not None:
-            kw["scale"] = ap(scale)
+        kw = {k: ap(x) for k, x in (("bias", bias), ("scale", scale)) if x is not None}
         op("S", rg(a, bias, scale), out[1], 80 + GATHER * cols(out) if a[2] else cols(out), lambda: g.scalar.activation(out[0], a[0], func, **kw))
 
     def iota(x, pattern, start, by):
@@ -293,8 +305,8 @@ def rank_program(g, core, T, topo):
     iota(C("mr"), [[0, 16], [1, 16]], 0, 0)
     iota(C("mg"), [[16, 16], [0, 16]], 0, 0)
     iota(C("pw", NUM, PDUMP), [[1, PDUMP - NUM]], H, 0)
-    for name, a, b, k in (("xw", H, DUMP, 0.0), ("pw", 1024, NUM, 0.0), ("dd3", 1024, 1040, 0.0), ("ftab", 0, 16, 0.0), ("ftab", 1, 2, 1.0 / 512), ("zm", 0, 128, 0.0),
-                          ("one", 0, 16, 1.0), ("half", 0, 256, -0.5), ("fc", 0, 16, 1.0), ("cum", 0, 24, 0.0)):
+    for name, a, b, k in (("xw", H, DUMP, 0.0), ("pw", 1024, NUM, 0.0), ("dd3", 1024, 1040, 0.0), ("ftab", 0, 16, 0.0), ("ftab", 1, 2, 0.25), ("zm", 0, 128, 0.0),
+                          ("one", 0, 16, 1.0), ("half", 0, 256, -0.5), ("fc", 0, 16, 1.0), ("cum", 0, 24, 0.0), ("yy", 768, 1120, 0.0), ("zf", 256, 608, 0.0)):
         fill(C(name, a, b), k)
     ts(C("pr"), C("ip"), 15, OP.bitwise_and)
     ts(C("pp"), C("ip"), 1, OP.bitwise_and)
@@ -325,7 +337,8 @@ def rank_program(g, core, T, topo):
         cp(C("uo0"), U("uu", 0))
 
     def entries(s):
-        cp(C("li%d" % s), IND(C("pw", 0, 1024), C("uo%d" % s)))
+        for a, b in pairs(LISTS[s]):
+            cp(C("li%d" % s, 16 * a, 16 * b), IND(C("pw", 0, 1024), C("uo%d" % s, a, b)))
 
     starts("qf0", [])
     for (_, c0, c1) in REPEAT:
@@ -353,41 +366,43 @@ def rank_program(g, core, T, topo):
     act(C("mn0"), C("mn0"), AF.Copy, -BIG)
     act(C("mx0"), C("mx0"), AF.Copy, 2.0)
     ts(C("colb"), C("colr"), 64.0, OP.mult, -1984.0, OP.add)
-    ts(C("colm"), C("colr"), -1.0, OP.mult, -1.0, OP.add)
     ts(C("colr16"), C("colr"), 16.0, OP.mult)
     ts(C("colsg"), C("par"), -2.0, OP.mult, 1.0, OP.add)
-    ts(C("cola"), C("colr"), 0.0, OP.is_equal, 1048576.0, OP.mult)
-    ts(C("colc"), C("colr"), 1.0, OP.is_equal, 65536.0, OP.mult)
-    ts(C("coln"), C("colr"), 2.0, OP.is_lt)
-    ts(C("cold"), C("colr"), 15.0, OP.mult, 1.0, OP.add)
     tt(C("colsw"), C("colsg"), C("colp"), OP.add)
-    tt(C("coln"), C("coln"), C("cold"), OP.mult)
     ts(C("tri"), C("mr", 0, 128), C("colr"), OP.is_gt)
-    ts(C("nib"), C("mr"), C("cola"), OP.mult)
-    ts(C("nib2"), C("mg"), C("colc"), OP.mult)
     tt(C("tri"), C("tri"), C("bo"), OP.mult)
     ts(C("sw"), C("mf", 0, 128), C("colsw"), OP.is_equal)
-    tt(C("nib"), C("nib"), C("nib2"), OP.add)
     act(C("i4k"), C("idm"), AF.Copy, None, 4096.0)
     act(C("n128"), C("idm"), AF.Copy, None, -128.0)
-    act(C("trim"), C("idm"), AF.Copy, None, -256.0)
     act(C("n4k"), C("idm"), AF.Copy, None, -4096.0)
+    act(C("trim"), C("idm"), AF.Copy, None, -256.0)
     ts(C("bw2k"), C("mf"), C("colg15"), OP.is_equal, 2048.0, OP.mult)
     ts(C("sws"), C("sw"), C("colsg"), OP.mult, -1.0, OP.mult)
     tt(C("swb"), C("sw"), C("idm"), OP.add)
     act(C("swb"), C("swb"), AF.Copy, None, 4096.0)
     tt(C("tri4"), C("tri"), C("i4k"), OP.add)
-    iota(C("pos"), [[256, 4], [1, 16]], 0, 0)
-    ts(C("pos"), C("pos"), C("colr16"), OP.add)
-    ts(C("fillk"), C("nib", 0, 64), 33554432.0, OP.add)
-    ts(C("bwn"), C("mf"), C("colg15"), OP.is_equal, C("coln"), OP.mult)
     tt(C("trim"), C("trim"), C("tri"), OP.add)
+    iota(C("pos"), [[1, 16], [256, 4]], 0, 0)
+    ts(C("pos"), C("pos"), C("colr16"), OP.add)
     act(C("rr"), C("mask", 0, 128))
     act(C("bo32"), C("bo"))
     act(C("idm32"), C("idm"))
     act(C("lub"), C("lu"))
-    for s in range(3):
-        act(U("dp", s), C("lu"), AF.Copy, PDUMP - 8192.0)
+    ts(C("cola"), C("colr"), 0.0, OP.is_equal, 1048576.0, OP.mult)
+    ts(C("colc"), C("colr"), 1.0, OP.is_equal, 65536.0, OP.mult)
+    ts(C("coln"), C("colr"), 2.0, OP.is_lt)
+    ts(C("cold"), C("colr"), 15.0, OP.mult, 1.0, OP.add)
+    tt(C("coln"), C("coln"), C("cold"), OP.mult)
+    ts(C("nib"), C("mr"), C("cola"), OP.mult)
+    ts(C("nib2"), C("mg"), C("colc"), OP.mult)
+    tt(C("nib"), C("nib"), C("nib2"), OP.add)
+    act(C("fillk"), C("nib", 0, 64), AF.Copy, 33554432.0)
+    ts(C("bwn"), C("mf"), C("colg15"), OP.is_equal, C("coln"), OP.mult)
+    iota(C("tid"), [[1, 1024]], 0, 0)
+    act(C("thb"), C("th32"), AF.Copy, BIG / 16)
+    for s in range(2):
+        act(U("dp", s), C("lu"), AF.Copy, PDUMP - 4096.0)
+    act(C("dps"), C("lu", 0, 4), AF.Copy, float(PDUMP))
     act(C("dx"), C("lu"), AF.Copy, DUMP - 2048.0)
     for r in range(16):
         ts(M("pb", r), C("bo"), C("mask", r, r + 1), OP.mult)
@@ -431,46 +446,47 @@ def rank_program(g, core, T, topo):
         return (T[n][:, c0:c1, :, :] if r is None else T[n][:, c0:c1, r, :], [(n, c0, c1)], [])
 
     def dist(s, c0, c1):
-        low = (C("idm"), C("ep", 0, 16 * (c1 - c0))) if s < 3 else (C("idm32"), C("pos"))
-        total(C("K%d" % (s % 2), 16 * c0, 16 * c1), [low] + [(W("bw" if s < 3 else "bw2k", r), ring(s, c0, c1, r)) for r in range(16)])
+        total(C("K%d" % (s % 2), 16 * c0, 16 * c1), [(C("idm"), C("ep", 0, 16 * (c1 - c0)))] + [(W("bw", r), ring(s, c0, c1, r)) for r in range(16)])
 
     turn = [0]
 
     def tries(s, between):
-        for k, (c0, c1) in enumerate(VEC[s]):
-            tt(dcols(s, c0, c1), IND(C("xw", 0, 4096), C("li%d" % s, 16 * c0, 16 * c1)), QR(c0, c1), OP.subtract)
-            a0, a1 = SCA[s][k]
+        for (a0, a1) in pairs(SCA[s]):
             act(dcols(s, a0, a1), IND(C("xw", 0, 4096), C("li%d" % s, 16 * a0, 16 * a1)))
+        for k, (c0, c1) in enumerate(pairs(VEC[s])):
+            tt(dcols(s, c0, c1), IND(C("xw", 0, 4096), C("li%d" % s, 16 * c0, 16 * c1)), QR(c0, c1), OP.subtract)
             if k == 0:
                 between()
-        (c0, c1), (d0, d1) = VEC[s]
-        act(ring(s, c0, c1), dcols(s, c0, c1), AF.Abs)
-        dist(s, c0, c1)
-        for a0, a1 in SCA[s]:
-            for c in range(a0, a1, 2):
-                e = min(c + 2, a1)
-                bank = C("SUB%d" % (turn[0] % 2), 0, 256 * (e - c))
-                turn[0] += 1
-                total(bank, [(C("nid"), QR(c, e)), (C("idm"), dcols(s, c, e))])
-                act(ring(s, c, e), bank, AF.Abs)
-        dist(s, SCA[s][0][0], 16)
-        act(ring(s, d0, d1), dcols(s, d0, d1), AF.Abs)
-        dist(s, d0, d1)
+                for a0, a1 in pairs(SCA[s]):
+                    for c in range(a0, a1, 2):
+                        e = min(c + 2, a1)
+                        bank = C("SUB%d" % (turn[0] % 2), 0, 256 * (e - c))
+                        turn[0] += 1
+                        total(bank, [(C("nid"), QR(c, e)), (C("idm"), dcols(s, c, e))])
+                        act(ring(s, c, e), bank, AF.Abs)
+                dist(s, SCA[s][0], 16)
+            act(ring(s, c0, c1), dcols(s, c0, c1), AF.Abs)
+            dist(s, c0, c1)
 
-    def minscan(s, n=256):
-        scan(C("km", LEAST[s], LEAST[s] + n), C("mn0", 0, n), C("K%d" % (s % 2), 0, n), OP.max, OP.min)
+    def minscan(s):
+        for a, b in pairs(SCANS[s]):
+            scan(C("km", LEAST[s] + a, LEAST[s] + b), C("mn0", a, b), C("K%d" % (s % 2), a, b), OP.max, OP.min)
 
     def maxscan(s):
-        scan(C("km", MOST[s], MOST[s] + 256), C("mx0"), C("K%d" % (s % 2), 0, 256), OP.add, OP.max)
+        for a, b in pairs(SCANS[s]):
+            scan(C("km", MOST[s] + a, MOST[s] + b), C("mx0", a, b), C("K%d" % (s % 2), a, b), OP.add, OP.max)
 
-    def best(s, n=256):
-        return C("km", LEAST[s] + 15, LEAST[s] + n, 16)
+    def best(s):
+        return C("km", LEAST[s] + 15, LEAST[s] + 256, 16)
 
     def bcast(src):
         mms([(C("WB", r, 512, 16), M("pb", r), src, True, True) for r in range(16)])
 
-    def keep_others(s):
-        tt(B("lim", s), IND(C("pw", 0, 1024), C("uo%d" % s)), B("yy", s), OP.min)
+    def failed(s):
+        act(U("thr", s - 1), U("fc", s), AF.Identity, C("thb"), -BIG / 16)
+        tt(U("fc", s + 1), best(s), U("thr", s - 1), OP.is_ge)
+
+    LS = C("ls16")
 
     for t in range(R):
         last = t == R - 1
@@ -482,14 +498,14 @@ def rank_program(g, core, T, topo):
         tries(0, lambda: (mother(0), entries(1)))
         tries(1, lambda: (mother(1), entries(2)))
         mother(2)
-        cp(C("pk", 0, 64), C("fillk"))
+        act(C("pf", 0, 64), C("fillk"))
         iota(C("cf", 0, 256), [[0, 256]], 0, 0)
+        total(C("ZA", 0, 256), [(C("i4k"), C(q, 0, 256)), (C("idm"), C("nib"))])
+        act(C("qp"), C("ZA", 0, 256))
         minscan(0)
         maxscan(0)
         ts(U("fc", 1), best(0), C("th32"), OP.is_ge)
         total(C("SM", 16, 32), [(C("swb"), U("fc", 1)), (C("sws"), U("uu", 0))])
-        total(C("ZA", 0, 256), [(C("i4k"), C(q, 0, 256)), (C("idm"), C("nib"))])
-        act(C("qp"), C("ZA", 0, 256))
         act(C("us0"), U("uu", 0), AF.Identity, 8192.0, C("colsg"))
         tt(C("xo"), C("SM", 16, 32), C("us0"), OP.max)
         ts(C("xo16"), C("xo"), -8192.0, OP.add, C("colsg"), OP.mult)
@@ -502,8 +518,7 @@ def rank_program(g, core, T, topo):
         cp(C("ki"), C("km", 15, 1024, 16))
         ts(C("em"), C("ki"), 31, OP.bitwise_and)
         cp(U("wb16", 0, 2), U("em", 2, 2))
-        ts(U("nft", 0), best(1), C("th32"), OP.is_ge)
-        tt(U("fc", 2), U("fc", 1), U("nft", 0), OP.mult)
+        failed(1)
         bcast(U("wb16", 0, 2))
         act(B("yy", 0, 2), C("WB"), AF.Square, C("colb"), 64.0)
         act(C("tb2k"), C(P3, 1024, 1025), AF.Copy, -1024.0, 2048.0)
@@ -516,23 +531,27 @@ def rank_program(g, core, T, topo):
         tt(U("tu", 1), C("SM", 128, 144), U("tu", 0), OP.min)
         tt(U("tu", 2), C("SM", 144, 160), U("tu", 1), OP.min)
         act(U("tu", 3), U("tu", 2), AF.Copy, 8192.0 - NUM - 64 * t)
-        tt(C("pack"), IND(C(P3, 0, 1024), C("uo3")), C("qp"), OP.add)
-        keep_others(0)
-        keep_others(1)
+        act(C("pack"), IND(C(P3, 0, 1024), C("uo3")))
+        for s in range(2):
+            tt(B("lim", s), IND(C("pw", 0, 1024), C("uo%d" % s)), B("yy", s), OP.min)
 
         minscan(2)
-        ts(U("nft", 1), best(2), C("th32"), OP.is_ge)
-        tt(U("fc", 3), U("fc", 2), U("nft", 1), OP.mult)
+        failed(2)
         scan(C("cum", 1, 17), C("one"), U("fc", 3), OP.mult, OP.add)
         tt(C("fl"), U("fc", 3), C("lub"), OP.mult)
         total(C("SM", 48, 64), [(C("idm"), C("lub")), (C("trim"), U("fc", 3)), (C("bo"), C("cum", 0, 16)), (C("nid"), C("fl"))])
-        total(C("SM", 32, 48), [(C("tri4"), U("fc", 3)), (C("bo"), C("cum", 0, 16))])
         ts(C("sl16"), C("SM", 48, 64), 256.0, OP.add)
-        cp(IND(C("pk"), C("sl16")), C("pack"))
-        ts(C("a3"), C("pk", 0, 64), 4095, OP.bitwise_and)
+        tt(IND(C("pf"), C("sl16")), C("pack"), C("qp"), OP.add)
+        cp(C("pk"), C("pf", 0, 64))
+        ts(C("a3"), C("pk"), 4095, OP.bitwise_and)
         cp(C("li3"), C("a3"))
-        ts(C("q3"), C("pk", 0, 64), 12, OP.arith_shift_right, 8447, OP.bitwise_and)
+        ts(C("q3"), C("pk"), 12, OP.arith_shift_right, 8447, OP.bitwise_and)
         cp(C("sq"), C("q3"))
+        ts(C("n3"), C("pk"), 20, OP.arith_shift_right)
+        cp(C("nb"), C("n3"))
+        total(C("SM", 64, 68), [(W("bwn", r), C("nb", r, 64, 16)) for r in range(16)])
+        cp(LS, C("SM", 64, 68))
+        total(C("SM", 32, 48), [(C("tri4"), U("fc", 3)), (C("bo"), C("cum", 0, 16))])
         maxscan(2)
         cp(C("k2"), C("km", 1039, 1536, 16))
         ts(C("e2"), C("k2"), 31, OP.bitwise_and)
@@ -543,64 +562,64 @@ def rank_program(g, core, T, topo):
         act(B("yy", 2), C("WB", 256, 512), AF.Square, C("colb"), 64.0)
         tt(C("us"), C("SM", 32, 48), U("tu", 3), OP.max)
         ts(C("us16"), C("us"), NUM + 64.0 * t - 4096, OP.add)
-        act(C("m0"), C("WB", 0, 256), AF.Square, C("colm"))
-        act(C("m1"), C("m0"), AF.Relu, 1.0, -1.0)
+        ts(C("m1"), C("WB", 0, 256), C("colr1"), OP.is_equal)
         for h in range(2):
-            act(C("dd3", 512 * h, 512 * h + 512), IND(C(X3), C("li3", 32 * h, 32 * h + 32)))
-            mms([(C("SUB%d" % h), C("idm"), C("dd3", 512 * h, 512 * h + 512), True, False)]
-                + [(C("SUB%d" % h, e, 512, 16), C("nid"), C("sq", 32 * h, 32 * h + 32), False, e == 15) for e in range(16)])
-            act(ring(3, 2 * h, 2 * h + 2), C("SUB%d" % h), AF.Abs)
-        dist(3, 0, 4)
-
-        ZS = (C("K0", 0, 256), C("K0", 256, 512), C("WB", 0, 256))
-
-        def answer(s):
-            total(ZS[s], [(C("nid"), B("yy", s)), (C("idm"), B("bm", 3))])
-            act(B("rl", s), ZS[s], AF.Relu, 2048.0)
+            (act, cp)[h](C("dd3", 512 * h, 512 * h + 512), IND(C(X3), C("li3", 32 * h, 32 * h + 32)))
+        for h in range(2):
+            mms([(C("SUB%d" % h, 64 * e, 64 * e + 64), l, x, k == 0, k == 1) for e in range(8) for k, (l, x) in enumerate(((C("nid"), C("sq")), (C("idm"), C("dd3", 8 * h + e, 1024, 16))))])
+            act(C("ab3", 512 * h, 512 * h + 512), C("SUB%d" % h), AF.Abs)
+        total(C("K1", 0, 64), [(C("idm32"), C("pos"))] + [(W("bw2k", r), C("ab3", r, 1024, 16)) for r in range(16)])
 
         tt(C("pm"), IND(C("pw", 0, PDUMP), C("us16")), C("m1"), OP.mult)
         total(C("KN", 0, 256), [(C("i4k"), C("half")), (C("bo32"), C("pm"))])
-        ts(C("n3"), C("pk", 0, 64), 20, OP.arith_shift_right)
-        cp(C("nb"), C("n3"))
-        total(C("SM", 64, 68), [(W("bwn", r), C("nb", r, 64, 16)) for r in range(16)])
-        cp(C("ls16"), C("SM", 64, 68))
-        keep_others(2)
+        act(C("zf", 0, 256), IND(C("tid"), C("uo2")))
+        cp(C("zs"), IND(C("zf"), LS))
+        total(C("SM", 68, 72), [(M("dg", r), C("zs", r, 64, 16)) for r in range(16)])
+        act(C("ouf"), C("SM", 68, 72))
         u = own(3, C("KN", 0, 256))
-        answer(2)
+        for s in (1, 0):
+            total(B("K0", s), [(C("nid"), B("yy", s)), (C("idm"), B("bm", 3))])
+            act(B("rl", s), B("K0", s), AF.Relu, 2048.0)
+        cp(C("ou16"), C("SM", 68, 72))
+        act(C("ys"), IND(C("yy", 512, 1120), LS))
+        tt(C("lims"), IND(C("pw", 0, 1024), C("ou16")), C("ys"), OP.min)
+        total(C("WB", 0, 64), [(C("nid"), C("ys")), (C("idm32"), C("pw", NUM + 64 * t, NUM + 64 * t + 64))])
+        act(C("rls"), C("WB", 0, 64), AF.Relu)
         ts(C("an16"), u, 2048.0, OP.add)
         act(C("num"), u)
         act(C("av"), IND(C("xw", 0, DUMP), C("an16")))
-        total(C("ZA", 0, 256), [(C("idm"), C(q, 0, 256)), (C("idm"), C("half")), (C("idm"), C("av"))])
+        total(C("ZA", 0, 256), [(C("idm"), C(q, 0, 256)), (C("idm"), C("av"))])
         if not last:
-            act(C("sg"), C("ZA", 0, 256), AF.Sign, -255.0)
+            act(C("sg"), C("ZA", 0, 256), AF.Sign, -255.5)
             total(C("SUB0", 0, 256), [(C("idm"), C(q, 0, 256)), (C("idm"), C("av")), (C("n128"), C("sg"))])
             act(C(qn, 0, 256), C("SUB0", 0, 256), AF.Copy, -128.0)
 
-        minscan(3, 64)
-        ts(C("c16"), best(3, 64), C("tb2k"), OP.is_lt)
-        cp(C("fl64"), IND(C("ftab"), C("c16")))
-        cp(IND(C("cf"), C("ls16")), C("fl64"))
-        total(C("SM", 96, 112), [(C("nid"), U("fc", 3))] + [(W("bw", r), C("cf", r, 256, 16)) for r in range(16)])
-        ts(C("k3"), best(3, 64), C("tb2k"), OP.min)
+        for c in range(4):
+            least(C("b3", c, c + 1), C("K1", c, 64, 4))
+        ts(C("k3"), C("b3"), C("tb2k"), OP.min)
         ts(C("e3"), C("k3"), 2047, OP.bitwise_and)
         cp(C("i316"), C("e3"))
+        ts(C("fail"), C("b3"), C("tb2k"), OP.is_ge)
+        ts(C("c16"), C("b3"), C("tb2k"), OP.is_lt)
+        cp(C("fl64"), IND(C("ftab"), C("c16")))
+        cp(IND(C("cf"), LS), C("fl64"))
+        total(C("K1", 272, 288), [(C("n128"), U("fc", 3))] + [(W("bw", r), C("cf", r, 256, 16)) for r in range(16)])
+        act(C("got"), C("K1", 272, 288), AF.Copy, None, 1.0 / 128)
+        mms([(C("SM", 160, 192), C("idm32"), U("uu", 0, 2), True, False), (C("SM", 160, 192), C("n4k"), U("fc", 1, 2), False, False)]
+            + [(C("SM", 160 + 16 * s, 176 + 16 * s), C("n4k"), C("got"), False, s == 1) for s in range(2)])
+        tt(C("so"), C("SM", 160, 192), C("dp"), OP.min)
+        ts(C("so16"), C("so"), 4096.0, OP.add)
         if not last:
             cp(C("xw", place, place + 64), IND(C("dd3"), C("i316")))
-        act(C("got"), C("SM", 96, 112), AF.Copy, 1.0)
-        if not last:
             tt(C("vs"), C("xw", place, place + 64), C("sq"), OP.add)
             ts(C("vt"), C("vs"), 255, OP.bitwise_and)
-            cp(IND(C(qn), C("ls16")), C("vt"))
-        total(C("SM", 160, 208), [(C("idm32"), C("uu")), (C("n4k"), U("fc", 1, 3))], True, False)
-        mms([(C("SM", 160 + 16 * s, 176 + 16 * s), C("n4k"), C("got"), False, s == 2) for s in range(3)])
-        tt(C("so"), C("SM", 160, 208), C("dp"), OP.min)
-        ts(C("so16"), C("so"), 8192.0, OP.add)
-        if not last:
-            starts(qn, [(C("rr"), C("got"))])
+            cp(IND(C(qn), LS), C("vt"))
+            starts(qn, [(C("rr"), U("fc", 0)), (C("rr"), C("got"))])
             for part in REPEAT:
                 repeat(qn, *part)
-        answer(1)
-        answer(0)
+        total(C("SM", 192, 196), [(C("idm32"), C("ouf")), (C("i4k"), C("fail"))])
+        tt(C("og"), C("SM", 192, 196), C("dps"), OP.min)
+        cp(C("og16"), C("og"))
 
         total(C("KN", 256, 512), [(C("zm"), C("ep"))], True, False)
         for c in range(16):
@@ -610,8 +629,7 @@ def rank_program(g, core, T, topo):
         total(C("KN", 256, 512), [(C("tri"), (T["eq"][:, :, 0:16], [("eq", 0, 16)], []))], False, True)
         act(C("cntb"), C("KN", 256, 512), AF.Copy, None, 8192.0)
         total(C("SUB1", 0, 16), [(C("i4k"), U("fc", 3)), (C("idm32"), C("num"))] + [(M("dg", r), C("cntb", r, 256, 16)) for r in range(16)])
-        act(C("hw"), C("ZA", 0, 256), AF.Copy, WHOLE, 0.5)
-        act(C("hv"), C("hw"), AF.Copy, -WHOLE)
+        ts(C("hv"), C("ZA", 0, 256), 0.5, OP.mult, -0.25, OP.add)
         tt(C("oh"), C("SUB1", 0, 16), C("dx"), OP.min)
         ts(C("oh16"), C("oh"), 2048.0, OP.add)
 
@@ -623,7 +641,8 @@ def rank_program(g, core, T, topo):
             dma("oy", T.yx[:, 0:place], T["xw"][:, 0:place], [("xw", 0, place)], [], 256 * place)
             cp(C("xw", place, place + 64), IND(C("dd3"), C("i316")))
             dma("oz", T.yx[:, place:4096], T["xw"][:, place:4096], [("xw", place, 4096)], [], 256 * 64)
-        for s in (2, 1, 0):
+        tt(IND(C("pw"), C("og16")), C("lims"), C("rls"), OP.add)
+        for s in (1, 0):
             tt(IND(C("pw"), U("so16", s)), B("lim", s), B("rl", s), OP.add)
         if last:
             dma("op", T.yp[:], T["pw"][:, 0:1024], [("pw", 0, 1024)], [], 128 * 4096)

from concourse.mybir import AxisListType, AluOpType as OP, ActivationFunctionType as AF

R, N = 3, 4
BIG = 16777216.0
H, DUMP = 3904, 4304
NUM, PDUMP = 1040, 1424
REPEAT = [("S", 0, 4), ("S", 4, 11), ("G", 11, 16)]
QV = 11
VEC = [(0, 4, 8, 11), (0, 4, 8, 11), (0, 4, 8, 11)]
SCA = [(11, 13, 16), (11, 13, 16), (11, 13, 16)]
LISTS = [(0, 4, 10, 16), (0, 16), (0, 16)]
SCANS = [(0, 256), (0, 256), (0, 128, 176, 256)]
LEAST, MOST = [0, 256, 1024], [512, 768, 1280]
FLOOR, HOP, GATHER, SCATTER, PE = 64, 325, 1.4, 3.0, 0.5
BYTES, LAND = 290, 1100
PASSES, STRETCH, SHAKE = 2000, 15000, (300, 800, 1500, 3000)
ORDER = []

SCRATCH = {}
PLACE = {}
PS = ["K0", "K1", "SM", "WB", "KN", "ZA", "SUB0", "SUB1"]


def _declare():
    f, b, i, u = "float32", "bfloat16", "int32", "uint16"
    sb = {}

    def add(d, text):
        for w in text.split():
            k, n = w.split(":")
            sb[k] = (int(n), d)

    add(b, "xw:4560 dd:12288 dd3:1040 ab3:1024 qf0:608 qf1:608 cf:608 yy:1120 ys:64 fl:16 fc:64 te:48 cum:24 wb16:64 got:16 hit:32 m1:256 cntb:256 av:256 sg:256")
    add(b, "sq:64 nb:64 fl64:64 fail:4 ftab:16 bo:128 bw:144 bwf:144 bwn:144 bw2k:144 pb:2048 dg:2048 rr:128 tri:128 trim:128 tri4:128 sw:128 swb:128")
    add(b, "idm:128 nid:128 i4k:128 n4k:128 n128:128 zm:128 lub:16 ep:256 half:256 nib:256 nib2:256")
    add("float16", "bm:1024 zs:64")
    add(f, "pw:1680 mw:1024 th32:1 thb:1 tb2k:1 km:1536 lim:512 rl:512 zf:608 tid:1024 pf:768 fillk:64 qp:256 pack:256 uu:48 thr:32 tu:64 us:16 pm:256")
    add(f, "so:32 us0:16 xo:16 oh:16 num:16 pos:64 lims:64 rls:64 ouf:4 b3:4 og:4 dps:4")
    add(f, "colr:1 colp:1 colg:1 colg15:1 colr1:1 colb:1 par:1 colsg:1 colsw:1 colp16:1 colr16:1 coln:1 cola:1 colc:1 cold:1")
    add(f, "mr:256 mf:144 mg:256 mask:256 bo32:128 idm32:128 sws:128 mn0:256 mx0:256 one:16 lu:16 dp:32 dx:16")
    add(i, "twi:1024 pk:64 a3:64 q3:64 n3:64 thi:1 u0i:16 mmi:16 ki:64 em:64 k2:32 e2:32 k3:4 e3:4 vs:64 vt:64 hv:256 ip:1 il:16 pr:1 pp:1 b4:16")
    add(u, "us16:16 so16:32 xo16:16 i316:4 c16:4 ls16:4 ou16:4 sl16:16 og16:4 oh16:16 an16:16 li0:256 li1:256 li2:256 li3:64 uo0:16 uo1:16 uo2:16 uo3:16")
    for t in range(R):
        add(b, "xb%d:%d" % (t, H + 64 * t))
        add(f, "pb%d:1032" % t)
    size = {}
    for k, (n, d) in sb.items():
        if n > 256 or k == "thi":
            SCRATCH[k] = ("sbuf", [128, n], d)
            PLACE[k] = (k, 0, n)
        else:
            PLACE[k] = ("all_" + d, size.get(d, 0), n)
            size[d] = size.get(d, 0) + (n + 15) // 16 * 16
    for d in size:
        SCRATCH["all_" + d] = ("sbuf", [128, size[d]], d)
    for k in range(3):
        SCRATCH["ring%d" % k] = ("sbuf", [128, 16, 16, 16], b)
    SCRATCH["qr"] = ("sbuf", [128, 256 * QV], b)
    SCRATCH["qr3"] = ("sbuf", [128, 256 - 16 * QV, 16], b)
    SCRATCH["eq"] = ("sbuf", [128, 16, 256], b)
    SCRATCH["mo8"] = ("sbuf", [8, 1024], i)
    SCRATCH["mo8f"] = ("sbuf", [8, 1024], f)
    SCRATCH["sel8"] = ("sbuf", [8, 128], f)
    for k in PS:
        SCRATCH[k] = ("psum", [128, 512], f)
        PLACE[k] = (k, 0, 512)


_declare()
SEMAPHORES = ["sv", "sa", "st", "sg", "dq", "dx", "dt", "dh", "dm", "oy", "oz", "op", "om"] + ["%s%d" % (k, t) for k in ("ax", "ap", "lx", "lp") for t in range(R)]


def rank_program(g, core, T, topo):
    rank = T.rank_of(core)
    if rank is None:
        return
    ENG = {"V": g.vector, "S": g.scalar, "P": g.tensor, "G": g, "Y": g.sync}
    SEM = {"V": "sv", "S": "sa", "P": "st", "G": "sg"}
    count, known, hist = {}, {q: {} for q in ENG}, {}

    def wait_toks(q, toks):
        need = {}
        for (s, v, vc) in toks:
            if known[q].get(s, 0) < v and need.get(s, (0, None))[0] < v:
                need[s] = (v, vc)
        for s in list(need):
            if any(o != s and need[o][1].get(s, 0) >= need[s][0] for o in need):
                del need[s]
        for s in need:
            ENG[q].wait_ge(T.sem[s], need[s][0])
        for (s, v, vc) in toks:
            for k in vc:
                if known[q].get(k, 0) < vc[k]:
                    known[q][k] = vc[k]

    def deps(q, reads, writes):
        out = []
        for wr, regs in ((False, reads), (True, writes)):
            for (b, lo, hi) in regs:
                for (l, h, w, eq, tok) in hist.get(b, []):
                    same = eq == q
                    if b in PS and not same:
                        out.append(tok)
                    elif l < hi and lo < h and (w or wr):
                        if same and q == "P":
                            continue
                        out.append(tok)
        return out

    def note(eq, reads, writes, tok):
        for (b, lo, hi) in writes:
            hist[b] = [e for e in hist.get(b, []) if not (lo <= e[0] and e[1] <= hi)] + [(lo, hi, True, eq, tok)]
        for (b, lo, hi) in reads:
            hist[b] = [e for e in hist.get(b, []) if not (not e[2] and e[3] == eq and eq in SEM and lo <= e[0] and e[1] <= hi)] + [(lo, hi, False, eq, tok)]

    def finish(q, sem, n, ins, reads, writes, eq):
        count[sem] = count.get(sem, 0) + n
        ins.then_inc(T.sem[sem], n)
        vc = dict(known[q])
        vc[sem] = count[sem]
        note(eq, reads, writes, (sem, count[sem], vc))

    calls = []

    def op(q, reads, writes, n, fn):
        def go():
            wait_toks(q, deps(q, reads, writes))
            finish(q, SEM[q], 1, fn(), reads, writes, q)
        calls.append((q, reads, writes, max(n, FLOOR), max(n, FLOOR), go))

    def dma(sem, out, in_, reads, writes, n):
        def go():
            wait_toks("Y", deps("Y", reads, writes))
            finish("Y", sem, 16, g.sync.dma_start(out, in_), reads, writes, "dma")
        calls.append(("Y", reads, writes, n // BYTES + FLOOR, n // BYTES + LAND, go))

    def plan():
        before, seen = [], {}
        for i, (q, reads, writes, _, _, _) in enumerate(calls):
            pre = {i - 1: FLOOR} if i and q == calls[i - 1][0] == "Y" else {}
            for wr, regs in ((False, reads), (True, writes)):
                for (b, lo, hi) in regs:
                    for (l, h, w, j) in seen.get(b, []):
                        p = calls[j][0]
                        if l < hi and lo < h and (w or wr):
                            pre[j] = max(pre.get(j, 0), calls[j][4] + (0 if p == q == "P" else HOP))
            for wr, regs in ((False, reads), (True, writes)):
                for (b, lo, hi) in regs:
                    seen[b] = [e for e in seen.get(b, []) if not (wr and lo <= e[0] and e[1] <= hi)] + [(lo, hi, wr, i)]
            pre.pop(i, None)
            before.append(pre)
        after = [{} for _ in calls]
        for i, pre in enumerate(before):
            for j in pre:
                after[j][i] = pre[j] + calls[i][3] - calls[j][3]
        banks = [{b for (b, _, _) in c[1] + c[2] if b in PS} for c in calls]

        def place(order, lags, first):
            at, queue, bank = {}, {q: [] for q in ENG}, {b: [] for b in PS}
            for i in order:
                q, n, s = calls[i][0], calls[i][3], first[i]
                for j, d in lags[i].items():
                    if at[j] + d > s:
                        s = at[j] + d
                busy, seen = queue[q], None
                while s != seen:
                    k = len(busy)
                    while k and busy[k - 1][1] > s:
                        k -= 1
                    while k < len(busy) and busy[k][0] < s + n:
                        s, k = busy[k][1], k + 1
                    seen = s
                    for x in banks[i]:
                        for (a, b, p) in bank[x]:
                            if p != q and a - HOP < s + n and b + HOP > s:
                                s = b + HOP
                at[i] = s
                busy.insert(k, (s, s + n))
                for x in banks[i]:
                    bank[x].append((s, s + n, q))
            return at

        every, zero, tail = list(range(len(calls))), [0] * len(calls), [c[4] - c[3] for c in calls]
        best, end, dice = dict(enumerate(every)), None, 1
        for _ in range(PASSES):
            key, lo, by = {}, (end or 0) * (dice % 97) / 97, SHAKE[dice % len(SHAKE)]
            for i in every:
                dice = dice * 16807 % 2147483647
                key[i] = max([best[i] + (dice % by if end and lo < best[i] < lo + STRETCH else 0)] + [key[j] + 0.001 for j in before[i]])
            at = place(sorted(every, key=key.get), before, zero)
            back = place(sorted(every, key=lambda i: (-at[i] - calls[i][3], -i)), after, tail)
            at = place(sorted(every, key=lambda i: (-back[i] - calls[i][3], i)), before, zero)
            if end is None or max(at[i] + calls[i][4] for i in every) <= end:
                best, end = at, max(at[i] + calls[i][4] for i in every)
        return sorted(every, key=lambda i: (best[i], i))

    def C(name, a=0, b=None, st=1):
        buf, at, n = PLACE[name]
        b = n if b is None else b
        return (T[buf][:, at + a:at + b:st] if st != 1 else T[buf][:, at + a:at + b], [(name, a, b)], [])

    def U(name, s, n=1):
        return C(name, 16 * s, 16 * s + 16 * n)

    def B(name, s, n=1):
        return C(name, 256 * s, 256 * s + 256 * n)

    def M(name, r):
        return C(name, 128 * r, 128 * r + 128)

    def W(name, r):
        return C(name, 15 - r, 143 - r)

    def IND(w, o):
        return (w[0].indirect(o[0]), w[1], o[1])

    def QR(c0, c1, e0=0, e1=16):
        if c0 >= QV:
            x = T["qr3"][:, 16 * (c0 - QV):16 * (c1 - QV), e0:e1]
        else:
            x = T["qr"][:, 256 * c0:256 * c1] if e1 - e0 == 16 else T["qr"][:, 256 * c0 + e0:256 * c1:16]
        return (x, [("qr%d" % k, e0, e1) for k, (_, a, b) in enumerate(REPEAT) if a < c1 and c0 < b], [])

    def pairs(bounds):
        return list(zip(bounds, bounds[1:]))

    def rg(*xs):
        return [r for x in xs if isinstance(x, tuple) for r in x[1] + x[2]]

    def ap(x):
        return x[0] if isinstance(x, tuple) else x

    def cols(x):
        n = 1
        for k in x[0].shape[1:]:
            n *= k
        return n

    def short(x):
        buf = PLACE.get(x[1][0][0], (None,))[0]
        return buf is None or SCRATCH[buf][2] in ("bfloat16", "uint16", "float16")

    def work(out, *ins):
        if out[2]:
            return 60 + cols(ins[-1]) * SCATTER
        if ins[0][2]:
            return 60 + cols(out) * GATHER
        if short(out) and all(short(x) for x in ins):
            return cols(out) * len(ins) / 2
        return cols(out) * (1 if any(x[1][0][0] in PS for x in ins) else len(ins))

    def tt(out, a, b, o):
        op("V", rg(a, b) + out[2], out[1], work(out, a, b), lambda: g.vector.tensor_tensor(out[0], a[0], b[0], o))

    def ts(out, a, s1, o1, s2=None, o2=None):
        if o2 is None:
            op("V", rg(a, s1), out[1], work(out, a), lambda: g.vector.tensor_scalar(out[0], a[0], ap(s1), None, o1))
        else:
            op("V", rg(a, s1, s2), out[1], work(out, a), lambda: g.vector.tensor_scalar(out[0], a[0], ap(s1), ap(s2), o1, o2))

    def cp(out, a):
        op("V", rg(a) + out[2], out[1], work(out, a), lambda: g.vector.tensor_copy(out[0], a[0]))

    def fill(out, k):
        op("V", [], out[1], work(out, out), lambda: g.vector.memset(out[0], k))

    def scan(out, d0, d1, o0, o1):
        op("V", rg(d0, d1), out[1], cols(out), lambda: g.vector.tensor_tensor_scan(out[0], d0[0], d1[0], 0.0, o0, o1))

    def least(out, a):
        op("V", rg(a), out[1], cols(a), lambda: g.vector.tensor_reduce(out[0], a[0], AxisListType.X, OP.min))

    def act(out, a, func=AF.Copy, bias=None, scale=None):
        kw = {k: ap(x) for k, x in (("bias", bias), ("scale", scale)) if x is not None}
        op("S", rg(a, bias, scale), out[1], 80 + GATHER * cols(out) if a[2] else cols(out), lambda: g.scalar.activation(out[0], a[0], func, **kw))

    def iota(x, pattern, start, by):
        op("G", [], x[1], 150 + 2 * cols(x), lambda: g.iota(x[0], pattern, start, by, allow_small_or_imprecise_dtypes=True))

    def gcopy(out, a):
        op("G", rg(a), out[1], 200 + 2 * cols(out), lambda: g.affine_select(out[0], a[0], [[0, cols(out)]], OP.is_ge, 0.0, 0, 0))

    def mms(lst):
        def go():
            for (o, l, r, a, b) in lst:
                ins = g.tensor.matmul(o[0], l[0], r[0], a, b)
            return ins
        n = sum(max(64, cols(r)) * (PE if short(r) else 4 * PE) for (_, _, r, _, _) in lst)
        group = [("group" + lst[0][0][1][0][0], 0, 1)]
        whole = lst[0][3] and lst[-1][4]
        op("P", [x for m in lst for x in m[1][1] + m[2][1]] + group * whole, [x for m in lst for x in m[0][1]] + group * (not whole), n, go)

    def total(out, terms, first=True, last=True):
        mms([(out, l, r, first and i == 0, last and i == len(terms) - 1) for i, (l, r) in enumerate(terms)])

    dma("dq", T["qf0"][:, 0:256], T.qs[:], [], [("qf0", 0, 256)], 128 * 512)
    dma("dt", T["twi"][:], T.towns[:], [], [("twi", 0, 1024)], 128 * 4096)
    dma("dh", T["thi"][:], T.th[:], [], [("thi", 0, 1)], 128 * 4)
    dma("dm", T["mo8"][:], T.mo[:], [], [("mo8", 0, 1024)], 8 * 4096)
    dma("dx", T["xw"][:, 0:H], T.x[:], [], [("xw", 0, H)], 256 * H)

    iota(C("ip"), [[0, 1]], 0, 1)
    iota(C("mf"), [[1, 144]], 0, 0)
    iota(C("il"), [[16, 16]], 0, 1)
    iota(C("mr"), [[0, 16], [1, 16]], 0, 0)
    iota(C("mg"), [[16, 16], [0, 16]], 0, 0)
    iota(C("pw", NUM, PDUMP), [[1, PDUMP - NUM]], H, 0)
    for name, a, b, k in (("xw", H, DUMP, 0.0), ("pw", 1024, NUM, 0.0), ("dd3", 1024, 1040, 0.0), ("ftab", 0, 16, 0.0), ("ftab", 1, 2, 0.25), ("zm", 0, 128, 0.0),
                          ("one", 0, 16, 1.0), ("half", 0, 256, -0.5), ("fc", 0, 16, 1.0), ("cum", 0, 24, 0.0), ("yy", 768, 1120, 0.0), ("zf", 256, 608, 0.0)):
        fill(C(name, a, b), k)
    ts(C("pr"), C("ip"), 15, OP.bitwise_and)
    ts(C("pp"), C("ip"), 1, OP.bitwise_and)
    cp(C("colp"), C("ip"))
    cp(C("colr"), C("pr"))
    cp(C("par"), C("pp"))
    tt(C("colg"), C("colp"), C("colr"), OP.subtract)
    ts(C("colr1"), C("colr"), 1.0, OP.add)
    ts(C("colg15"), C("colg"), 15.0, OP.add)
    ts(C("bwf"), C("mf"), C("colg15"), OP.is_equal, C("colr1"), OP.mult)
    ts(C("idm"), C("mf", 0, 128), C("colp"), OP.is_equal)
    ts(C("lu"), C("il"), C("colg"), OP.subtract)
    ts(C("bw"), C("mf"), C("colg15"), OP.is_equal, 32.0, OP.mult)
    ts(C("b4"), C("lu"), 4.0, OP.mult)

    def repeat(qn, who, c0, c1):
        copies = [(QR(c0, c1, e, e + 1), C(qn, 16 * c0, 16 * c1)) for e in range(16 if c0 < QV else 2)]
        for (o, a) in copies + [(QR(c0, c1, e, 2 * e), QR(c0, c1, 0, e)) for e in (2, 4, 8) if c0 >= QV]:
            {"G": gcopy, "V": cp, "S": act}[who](o, a)

    def starts(qn, more):
        total(C("K1", 256, 272), [(W("bwf", r), C(qn, r, 256, 16)) for r in range(16)], True, not more)
        if more:
            total(C("K1", 256, 272), more, False, True)
        cp(C("u0i"), C("K1", 256, 272))
        ts(C("mmi"), C("u0i"), 3, OP.bitwise_and)
        tt(U("uu", 0), C("mmi"), C("b4"), OP.add)
        cp(C("uo0"), U("uu", 0))

    def entries(s):
        for a, b in pairs(LISTS[s]):
            cp(C("li%d" % s, 16 * a, 16 * b), IND(C("pw", 0, 1024), C("uo%d" % s, a, b)))

    starts("qf0", [])
    for (_, c0, c1) in REPEAT:
        repeat("qf0", "S", c0, c1)
    act(C("nid"), C("idm"), AF.Copy, None, -1.0)
    ts(C("ep"), C("mr"), 1.0, OP.add)
    ts(C("mask"), C("mr"), C("colr"), OP.is_equal)
    ts(C("bo"), C("mg", 0, 128), C("colg"), OP.is_equal)
    ts(C("colp16"), C("colp"), 16.0, OP.mult)
    cp(C("pw", 0, 1024), C("twi"))
    cp(C("pw", 1024, 1025), C("thi"))
    ts(C("th32"), C("thi"), 32.0, OP.mult)
    entries(0)

    op("V", [("mo8", 0, 1024)], [("mo8f", 0, 1024)], 1024, lambda: g.vector.tensor_copy(T["mo8f"][:, :], T["mo8"][:, :]))
    bm, am, _ = PLACE["mg"]
    bc, ac, _ = PLACE["colp16"]
    op("V", [("mg", 0, 128), ("colp16", 0, 1)], [("sel8", 0, 128)], 128, lambda: g.vector.tensor_scalar(T["sel8"][:, :], T[bm][0:8, am:am + 128], T[bc][0:8, ac:ac + 1], None, OP.is_equal))
    for h, b in ((0, "WB"), (1, "KN")):
        op("P", [("sel8", 0, 128), ("mo8f", 0, 1024)], [(b, 0, 512)], 2048 * PE, lambda h=h, b=b: g.tensor.matmul(T[b][:, :], T["sel8"][:, :], T["mo8f"][:, 512 * h:512 * h + 512], True, True))
        act(C("mw", 512 * h, 512 * h + 512), C(b))

    ts(C("mn0"), C("mr"), 0.0, OP.is_equal, 2.0 * BIG, OP.mult)
    ts(C("mx0"), C("mr"), 0.0, OP.is_equal, -BIG / 16, OP.mult)
    act(C("mn0"), C("mn0"), AF.Copy, -BIG)
    act(C("mx0"), C("mx0"), AF.Copy, 2.0)
    ts(C("colb"), C("colr"), 64.0, OP.mult, -1984.0, OP.add)
    ts(C("colr16"), C("colr"), 16.0, OP.mult)
    ts(C("colsg"), C("par"), -2.0, OP.mult, 1.0, OP.add)
    tt(C("colsw"), C("colsg"), C("colp"), OP.add)
    ts(C("tri"), C("mr", 0, 128), C("colr"), OP.is_gt)
    tt(C("tri"), C("tri"), C("bo"), OP.mult)
    ts(C("sw"), C("mf", 0, 128), C("colsw"), OP.is_equal)
    act(C("i4k"), C("idm"), AF.Copy, None, 4096.0)
    act(C("n128"), C("idm"), AF.Copy, None, -128.0)
    act(C("n4k"), C("idm"), AF.Copy, None, -4096.0)
    act(C("trim"), C("idm"), AF.Copy, None, -256.0)
    ts(C("bw2k"), C("mf"), C("colg15"), OP.is_equal, 2048.0, OP.mult)
    ts(C("sws"), C("sw"), C("colsg"), OP.mult, -1.0, OP.mult)
    tt(C("swb"), C("sw"), C("idm"), OP.add)
    act(C("swb"), C("swb"), AF.Copy, None, 4096.0)
    tt(C("tri4"), C("tri"), C("i4k"), OP.add)
    tt(C("trim"), C("trim"), C("tri"), OP.add)
    iota(C("pos"), [[1, 16], [256, 4]], 0, 0)
    ts(C("pos"), C("pos"), C("colr16"), OP.add)
    act(C("rr"), C("mask", 0, 128))
    act(C("bo32"), C("bo"))
    act(C("idm32"), C("idm"))
    act(C("lub"), C("lu"))
    ts(C("cola"), C("colr"), 0.0, OP.is_equal, 1048576.0, OP.mult)
    ts(C("colc"), C("colr"), 1.0, OP.is_equal, 65536.0, OP.mult)
    ts(C("coln"), C("colr"), 2.0, OP.is_lt)
    ts(C("cold"), C("colr"), 15.0, OP.mult, 1.0, OP.add)
    tt(C("coln"), C("coln"), C("cold"), OP.mult)
    ts(C("nib"), C("mr"), C("cola"), OP.mult)
    ts(C("nib2"), C("mg"), C("colc"), OP.mult)
    tt(C("nib"), C("nib"), C("nib2"), OP.add)
    act(C("fillk"), C("nib", 0, 64), AF.Copy, 33554432.0)
    ts(C("bwn"), C("mf"), C("colg15"), OP.is_equal, C("coln"), OP.mult)
    iota(C("tid"), [[1, 1024]], 0, 0)
    act(C("thb"), C("th32"), AF.Copy, BIG / 16)
    for s in range(2):
        act(U("dp", s), C("lu"), AF.Copy, PDUMP - 4096.0)
    act(C("dps"), C("lu", 0, 4), AF.Copy, float(PDUMP))
    act(C("dx"), C("lu"), AF.Copy, DUMP - 2048.0)
    for r in range(16):
        ts(M("pb", r), C("bo"), C("mask", r, r + 1), OP.mult)
        act(M("dg", r), C("idm"), AF.Identity, None, C("mask", r, r + 1))

    def send(t, kind):
        dst, frm = T.cores[(rank - 1 - t) % N], T.cores[(rank + 1 + t) % N]
        rid, pid, _ = topo.addr(dst)
        src, dest, n = ("pw", "pb%d" % t, 1032) if kind == "p" else ("xw", "xb%d" % t, H + 64 * t)

        def go():
            wait_toks("G", deps("G", [(src, 0, n)], []))
            asem, lsem = "a%s%d" % (kind, t), "l%s%d" % (kind, t)
            g.remote_dma(T[dest][:, 0:n], T[src][:, 0:n], T.sem[asem], T.sem[lsem], pid, rid, topo.mask(core, dst))
            count[lsem] = len(topo.engines(core, dst))
            vc = dict(known["G"])
            vc[lsem] = count[lsem]
            note("dma", [(src, 0, n)], [], (lsem, count[lsem], vc))
            count[asem] = len(topo.engines(frm, core))
            note("dma", [], [(dest, 0, n)], (asem, count[asem], {asem: count[asem]}))
        first, then = ([("sent", t, t + 1)], []) if kind == "p" else ([], [("sent", t, t + 1)])
        calls.append(("G", [(src, 0, n)] + first, [(dest, 0, n)] + then, 1100, 16000 if kind == "x" else 8000, go))

    def own(k, src):
        cp(B("bm", k), src)
        u = C("SM", 208 + 16 * k, 224 + 16 * k)
        total(u, [(M("dg", r), C("bm", 256 * k + r, 256 * k + 256, 16)) for r in range(16)])
        return u

    def mother(s):
        u = own(s, IND(C("mw"), C("uo%d" % s)))
        cp(C("uo%d" % (s + 1)), u)
        if s < 2:
            act(U("uu", s + 1), u)

    def dcols(s, c0, c1):
        return C("dd", 4096 * s + 256 * c0, 4096 * s + 256 * c1)

    def ring(s, c0, c1, r=None):
        n = "ring%d" % s
        return (T[n][:, c0:c1, :, :] if r is None else T[n][:, c0:c1, r, :], [(n, c0, c1)], [])

    def dist(s, c0, c1):
        total(C("K%d" % (s % 2), 16 * c0, 16 * c1), [(C("idm"), C("ep", 0, 16 * (c1 - c0)))] + [(W("bw", r), ring(s, c0, c1, r)) for r in range(16)])

    turn = [0]

    def tries(s, between):
        for (a0, a1) in pairs(SCA[s]):
            act(dcols(s, a0, a1), IND(C("xw", 0, 4096), C("li%d" % s, 16 * a0, 16 * a1)))
        for k, (c0, c1) in enumerate(pairs(VEC[s])):
            tt(dcols(s, c0, c1), IND(C("xw", 0, 4096), C("li%d" % s, 16 * c0, 16 * c1)), QR(c0, c1), OP.subtract)
            if k == 0:
                between()
                for a0, a1 in pairs(SCA[s]):
                    for c in range(a0, a1, 2):
                        e = min(c + 2, a1)
                        bank = C("SUB%d" % (turn[0] % 2), 0, 256 * (e - c))
                        turn[0] += 1
                        total(bank, [(C("nid"), QR(c, e)), (C("idm"), dcols(s, c, e))])
                        act(ring(s, c, e), bank, AF.Abs)
                dist(s, SCA[s][0], 16)
            act(ring(s, c0, c1), dcols(s, c0, c1), AF.Abs)
            dist(s, c0, c1)

    def minscan(s):
        for a, b in pairs(SCANS[s]):
            scan(C("km", LEAST[s] + a, LEAST[s] + b), C("mn0", a, b), C("K%d" % (s % 2), a, b), OP.max, OP.min)

    def maxscan(s):
        for a, b in pairs(SCANS[s]):
            scan(C("km", MOST[s] + a, MOST[s] + b), C("mx0", a, b), C("K%d" % (s % 2), a, b), OP.add, OP.max)

    def best(s):
        return C("km", LEAST[s] + 15, LEAST[s] + 256, 16)

    def bcast(src):
        mms([(C("WB", r, 512, 16), M("pb", r), src, True, True) for r in range(16)])

    def failed(s):
        act(U("thr", s - 1), U("fc", s), AF.Identity, C("thb"), -BIG / 16)
        tt(U("fc", s + 1), best(s), U("thr", s - 1), OP.is_ge)

    LS = C("ls16")

    for t in range(R):
        last = t == R - 1
        q, qn = "qf%d" % (t % 2), "qf%d" % ((t + 1) % 2)
        X3, P3 = "xb%d" % t, "pb%d" % t
        place = H + 64 * t
        send(t, "p")
        send(t, "x")
        tries(0, lambda: (mother(0), entries(1)))
        tries(1, lambda: (mother(1), entries(2)))
        mother(2)
        act(C("pf", 0, 64), C("fillk"))
        iota(C("cf", 0, 256), [[0, 256]], 0, 0)
        total(C("ZA", 0, 256), [(C("i4k"), C(q, 0, 256)), (C("idm"), C("nib"))])
        act(C("qp"), C("ZA", 0, 256))
        minscan(0)
        maxscan(0)
        ts(U("fc", 1), best(0), C("th32"), OP.is_ge)
        total(C("SM", 16, 32), [(C("swb"), U("fc", 1)), (C("sws"), U("uu", 0))])
        act(C("us0"), U("uu", 0), AF.Identity, 8192.0, C("colsg"))
        tt(C("xo"), C("SM", 16, 32), C("us0"), OP.max)
        ts(C("xo16"), C("xo"), -8192.0, OP.add, C("colsg"), OP.mult)
        tries(2, lambda: None)
        cp(IND(C("mw"), C("xo16")), B("bm", 0))
        if last:
            dma("om", T.ym[:], T["mw"][0:128:16, :], [("mw", 0, 1024)], [], 8 * 4096)
        minscan(1)
        maxscan(1)
        cp(C("ki"), C("km", 15, 1024, 16))
        ts(C("em"), C("ki"), 31, OP.bitwise_and)
        cp(U("wb16", 0, 2), U("em", 2, 2))
        failed(1)
        bcast(U("wb16", 0, 2))
        act(B("yy", 0, 2), C("WB"), AF.Square, C("colb"), 64.0)
        act(C("tb2k"), C(P3, 1024, 1025), AF.Copy, -1024.0, 2048.0)
        tt(C("hit"), U("fc", 0, 2), U("fc", 1, 2), OP.subtract)
        tt(U("te", 0, 2), C("hit"), U("em", 0, 2), OP.mult)
        tt(U("te", 0), U("te", 0), U("te", 1), OP.add)
        total(C("SM", 112, 160), [(C("idm32"), C("uu")), (C("n4k"), U("fc", 0, 3))], True, False)
        total(C("SM", 112, 144), [(C("i4k"), U("fc", 1, 2))], False, True)
        act(U("tu", 0), C("SM", 112, 128))
        tt(U("tu", 1), C("SM", 128, 144), U("tu", 0), OP.min)
        tt(U("tu", 2), C("SM", 144, 160), U("tu", 1), OP.min)
        act(U("tu", 3), U("tu", 2), AF.Copy, 8192.0 - NUM - 64 * t)
        act(C("pack"), IND(C(P3, 0, 1024), C("uo3")))
        for s in range(2):
            tt(B("lim", s), IND(C("pw", 0, 1024), C("uo%d" % s)), B("yy", s), OP.min)

        minscan(2)
        failed(2)
        scan(C("cum", 1, 17), C("one"), U("fc", 3), OP.mult, OP.add)
        tt(C("fl"), U("fc", 3), C("lub"), OP.mult)
        total(C("SM", 48, 64), [(C("idm"), C("lub")), (C("trim"), U("fc", 3)), (C("bo"), C("cum", 0, 16)), (C("nid"), C("fl"))])
        ts(C("sl16"), C("SM", 48, 64), 256.0, OP.add)
        tt(IND(C("pf"), C("sl16")), C("pack"), C("qp"), OP.add)
        cp(C("pk"), C("pf", 0, 64))
        ts(C("a3"), C("pk"), 4095, OP.bitwise_and)
        cp(C("li3"), C("a3"))
        ts(C("q3"), C("pk"), 12, OP.arith_shift_right, 8447, OP.bitwise_and)
        cp(C("sq"), C("q3"))
        ts(C("n3"), C("pk"), 20, OP.arith_shift_right)
        cp(C("nb"), C("n3"))
        total(C("SM", 64, 68), [(W("bwn", r), C("nb", r, 64, 16)) for r in range(16)])
        cp(LS, C("SM", 64, 68))
        total(C("SM", 32, 48), [(C("tri4"), U("fc", 3)), (C("bo"), C("cum", 0, 16))])
        maxscan(2)
        cp(C("k2"), C("km", 1039, 1536, 16))
        ts(C("e2"), C("k2"), 31, OP.bitwise_and)
        tt(U("te", 2), U("fc", 2), U("e2", 0), OP.mult)
        tt(U("wb16", 2), U("te", 0), U("te", 2), OP.add)
        cp(U("wb16", 3), U("e2", 1))
        bcast(U("wb16", 2, 2))
        act(B("yy", 2), C("WB", 256, 512), AF.Square, C("colb"), 64.0)
        tt(C("us"), C("SM", 32, 48), U("tu", 3), OP.max)
        ts(C("us16"), C("us"), NUM + 64.0 * t - 4096, OP.add)
        ts(C("m1"), C("WB", 0, 256), C("colr1"), OP.is_equal)
        for h in range(2):
            (act, cp)[h](C("dd3", 512 * h, 512 * h + 512), IND(C(X3), C("li3", 32 * h, 32 * h + 32)))
        for h in range(2):
            mms([(C("SUB%d" % h, 64 * e, 64 * e + 64), l, x, k == 0, k == 1) for e in range(8) for k, (l, x) in enumerate(((C("nid"), C("sq")), (C("idm"), C("dd3", 8 * h + e, 1024, 16))))])
            act(C("ab3", 512 * h, 512 * h + 512), C("SUB%d" % h), AF.Abs)
        total(C("K1", 0, 64), [(C("idm32"), C("pos"))] + [(W("bw2k", r), C("ab3", r, 1024, 16)) for r in range(16)])

        tt(C("pm"), IND(C("pw", 0, PDUMP), C("us16")), C("m1"), OP.mult)
        total(C("KN", 0, 256), [(C("i4k"), C("half")), (C("bo32"), C("pm"))])
        act(C("zf", 0, 256), IND(C("tid"), C("uo2")))
        cp(C("zs"), IND(C("zf"), LS))
        total(C("SM", 68, 72), [(M("dg", r), C("zs", r, 64, 16)) for r in range(16)])
        act(C("ouf"), C("SM", 68, 72))
        u = own(3, C("KN", 0, 256))
        for s in (1, 0):
            total(B("K0", s), [(C("nid"), B("yy", s)), (C("idm"), B("bm", 3))])
            act(B("rl", s), B("K0", s), AF.Relu, 2048.0)
        cp(C("ou16"), C("SM", 68, 72))
        act(C("ys"), IND(C("yy", 512, 1120), LS))
        tt(C("lims"), IND(C("pw", 0, 1024), C("ou16")), C("ys"), OP.min)
        total(C("WB", 0, 64), [(C("nid"), C("ys")), (C("idm32"), C("pw", NUM + 64 * t, NUM + 64 * t + 64))])
        act(C("rls"), C("WB", 0, 64), AF.Relu)
        ts(C("an16"), u, 2048.0, OP.add)
        act(C("num"), u)
        act(C("av"), IND(C("xw", 0, DUMP), C("an16")))
        total(C("ZA", 0, 256), [(C("idm"), C(q, 0, 256)), (C("idm"), C("av"))])
        if not last:
            act(C("sg"), C("ZA", 0, 256), AF.Sign, -255.5)
            total(C("SUB0", 0, 256), [(C("idm"), C(q, 0, 256)), (C("idm"), C("av")), (C("n128"), C("sg"))])
            act(C(qn, 0, 256), C("SUB0", 0, 256), AF.Copy, -128.0)

        for c in range(4):
            least(C("b3", c, c + 1), C("K1", c, 64, 4))
        ts(C("k3"), C("b3"), C("tb2k"), OP.min)
        ts(C("e3"), C("k3"), 2047, OP.bitwise_and)
        cp(C("i316"), C("e3"))
        ts(C("fail"), C("b3"), C("tb2k"), OP.is_ge)
        ts(C("c16"), C("b3"), C("tb2k"), OP.is_lt)
        cp(C("fl64"), IND(C("ftab"), C("c16")))
        cp(IND(C("cf"), LS), C("fl64"))
        total(C("K1", 272, 288), [(C("n128"), U("fc", 3))] + [(W("bw", r), C("cf", r, 256, 16)) for r in range(16)])
        act(C("got"), C("K1", 272, 288), AF.Copy, None, 1.0 / 128)
        mms([(C("SM", 160, 192), C("idm32"), U("uu", 0, 2), True, False), (C("SM", 160, 192), C("n4k"), U("fc", 1, 2), False, False)]
            + [(C("SM", 160 + 16 * s, 176 + 16 * s), C("n4k"), C("got"), False, s == 1) for s in range(2)])
        tt(C("so"), C("SM", 160, 192), C("dp"), OP.min)
        ts(C("so16"), C("so"), 4096.0, OP.add)
        if not last:
            cp(C("xw", place, place + 64), IND(C("dd3"), C("i316")))
            tt(C("vs"), C("xw", place, place + 64), C("sq"), OP.add)
            ts(C("vt"), C("vs"), 255, OP.bitwise_and)
            cp(IND(C(qn), LS), C("vt"))
            starts(qn, [(C("rr"), U("fc", 0)), (C("rr"), C("got"))])
            for part in REPEAT:
                repeat(qn, *part)
        total(C("SM", 192, 196), [(C("idm32"), C("ouf")), (C("i4k"), C("fail"))])
        tt(C("og"), C("SM", 192, 196), C("dps"), OP.min)
        cp(C("og16"), C("og"))

        total(C("KN", 256, 512), [(C("zm"), C("ep"))], True, False)
        for c in range(16):
            ts((T["eq"][:, c, 0:256 - 16 * c], [("eq", c, c + 1)], []), C("bm", 768 + 16 * c, 1024), C("num", c, c + 1), OP.is_equal)
        for c0, c1 in ((0, 6), (6, 15)):
            mms([(C("KN", 272 + 16 * c, 512), C("bo"), (T["eq"][:, c, 16:256 - 16 * c], [("eq", c, c + 1)], []), False, False) for c in range(c0, c1)])
        total(C("KN", 256, 512), [(C("tri"), (T["eq"][:, :, 0:16], [("eq", 0, 16)], []))], False, True)
        act(C("cntb"), C("KN", 256, 512), AF.Copy, None, 8192.0)
        total(C("SUB1", 0, 16), [(C("i4k"), U("fc", 3)), (C("idm32"), C("num"))] + [(M("dg", r), C("cntb", r, 256, 16)) for r in range(16)])
        ts(C("hv"), C("ZA", 0, 256), 0.5, OP.mult, -0.25, OP.add)
        tt(C("oh"), C("SUB1", 0, 16), C("dx"), OP.min)
        ts(C("oh16"), C("oh"), 2048.0, OP.add)

        def records():
            cp(IND(C("xw"), C("oh16")), C("hv"))

        if last:
            records()
            dma("oy", T.yx[:, 0:place], T["xw"][:, 0:place], [("xw", 0, place)], [], 256 * place)
            cp(C("xw", place, place + 64), IND(C("dd3"), C("i316")))
            dma("oz", T.yx[:, place:4096], T["xw"][:, place:4096], [("xw", place, 4096)], [], 256 * 64)
        tt(IND(C("pw"), C("og16")), C("lims"), C("rls"), OP.add)
        for s in (1, 0):
            tt(IND(C("pw"), U("so16", s)), B("lim", s), B("rl", s), OP.add)
        if last:
            dma("op", T.yp[:], T["pw"][:, 0:1024], [("pw", 0, 1024)], [], 128 * 4096)
        else:
            entries(0)
            records()

    if not ORDER:
        ORDER.extend(plan())
    for i in ORDER:
        calls[i][5]()
    for s in count:
        if known["G"].get(s, 0) < count[s]:
            g.wait_ge(T.sem[s], count[s])
